import numpy as np, ml_dtypes
CORES = [25,29,65,69,153,157,193,197]
N = 8
BF = ml_dtypes.bfloat16
D, T, L, RO, CM, SH = 2048, 512, 3, 4, 255, 11
def at(c, p):
    return c.reshape(-1)[np.arange(N * 8).reshape((N, 8) + (1,) * (p.ndim - 2)) * D + p]
def grow(rng, c, p):
    e = at(c, p); u = rng.random(p.shape)
    e = np.where(u < 0.06, e + rng.integers(1, RO, p.shape), e)
    return np.where(u > 0.97, rng.integers(0, CM + 1, p.shape), e)
def parts(rng):
    c = rng.integers(0, CM - RO + 1, (N, 8, D)); p = rng.integers(0, D, (N, 8, 16, D)); hot = rng.integers(0, D, (N, 8, 32))
    for n in range(N):
        for g in range(8): p[n, g] = np.where(rng.random((16, D)) < 0.03, hot[n, g][rng.integers(0, 32, (16, D))], p[n, g])
    return c, p, rng.integers(0, 16, (N, 8, 16, D)), rng.integers(0, 16, (N, 8, 16, T))
def pack(k, x, c, z):
    return {"nkey": np.ascontiguousarray(k.reshape(N, 128, D)).astype(np.float32), "xreg": np.ascontiguousarray(x.reshape(N, 128, D)).astype(np.float32).astype(BF),
            "cnt": np.ascontiguousarray(c).astype(np.int32), "zin": np.ascontiguousarray(z.reshape(N, 128, T)).astype(np.float32).astype(BF)}
def setup_inputs(rng):
    c, p, x, z = parts(rng)
    return pack(np.where(rng.random(p.shape) < 0.04, -1, p + D * grow(rng, c, p)), x, c, z)
def setup_inputs_calm(rng):
    c, p, x, z = parts(rng)
    base = (np.arange(N)[:, None, None] + np.arange(8)[None, :, None]) & 3
    c = np.where(rng.random(c.shape) < 0.8, base, rng.integers(0, 4, c.shape))
    e = at(c, p); e = np.maximum(np.where(rng.random(p.shape) < 0.75, e, e + rng.integers(-3, 4, p.shape)), 0)
    return pack(np.where(rng.random(p.shape) < 0.02, -1, p + D * e), x, c, z)
def setup_inputs_corners(rng):
    c, p, x, z = parts(rng); k = np.where(rng.random(p.shape) < 0.04, -1, p + D * grow(rng, c, p)); col = np.arange(D); r16 = np.arange(16)[:, None]
    who = rng.permutation(N)
    for n in range(N):
        kinds = rng.permutation(8)
        for g in range(8):
            m = int(kinds[g]); w = c[n, g]
            if n == who[0]:
                if m < 4: k[n, g] = -1
                else:
                    q = p[n, g]; k[n, g] = np.where(rng.random((16, D)) < 0.1, -1, q + D * ((w[q] + rng.integers(1, CM + 1, (16, D))) & CM))
            elif n == who[1]:
                q = (col + (D >> 2) * ((r16 & 3) if m > 2 else 0 * r16)) & (D - 1); k[n, g] = q + D * w[q]
            elif m == 0: k[n, g] = col + D * (w[col] + (r16 >= 12))
            elif m == 1:
                q = (5 * col + int(rng.integers(0, D))) & (D - 1); k[n, g] = (q + D * w[q])[None, :]
            elif m == 2:
                k[n, g] = -1; k[n, g, :, T - 1] = T - 1 + D * w[T - 1]
            elif m == 3:
                q = np.array([0, 1, T - 1, T, D - 1])[rng.integers(0, 5, (16, D))]; k[n, g] = q + D * (w[q] + rng.integers(0, 3, (16, D)))
            elif m == 4:
                w = (CM - RO) * rng.integers(0, 2, D); c[n, g] = w; q = p[n, g]
                k[n, g] = q + D * np.maximum(w[q] + np.where(rng.random((16, D)) < 0.75, 0, rng.integers(-1, 2, (16, D))), 0)
            elif m == 5: k[n, g] = np.where((rng.random(D) < 0.5)[None, :], -1, k[n, g])
            elif m == 6:
                q = col ^ 1; k[n, g] = q + D * (w[q] + (r16 >= 13))
            else: z[n, g] = rng.integers(0, 16, (1, T)) + np.zeros((16, 1), np.int64)
    return pack(k, x, c, z)
def setup_inputs_crowd(rng):
    c, p, x, z = parts(rng); k = np.where(rng.random(p.shape) < 0.04, -1, p + D * grow(rng, c, p)); r16 = np.arange(16)
    for n in range(N):
        kinds = rng.permutation(8)
        for g in range(8):
            m = int(kinds[g]); w = c[n, g]
            if m > 5: continue
            h = T + rng.permutation(D - T)[:L + 7]; dd = h[L - 1:L + 3]; odd = int(rng.choice(np.array([0, T - 1])))
            k[n, g, :, :T] = h[0] + D * w[h[0]]
            for j in range(L - 2): k[n, g, :, h[j]] = h[j + 1] + D * w[h[j + 1]]
            to = dd[r16 & 3] if m == 2 else np.full(16, h[0] if m == 5 else dd[0])
            k[n, g, :, h[L - 2]] = to + D * (w[to] + ((r16 & 3) if m == 3 else 0))
            if m == 1: k[n, g, :, odd] = -1
            if m == 4: k[n, g, :, odd] = odd + D * w[odd]
    return pack(k, x, c, z)
def setup_inputs_ends(rng):
    F = D >> 4; M = 4; top = D * (CM + 1) - 1; last = np.arange(16) * F + F - 1
    c = (CM - RO) * rng.integers(0, 2, (N, 8, D)); x = 15 * rng.integers(0, 2, (N, 8, 16, D)); z = 15 * rng.integers(0, 2, (N, 8, 16, T))
    m = rng.integers(0, 3, (N, 8, 16, F)); m[:, :, 6:, F - 1] = 1; m[:, :, 6::2, 0] = 0; m[:, :, 7::2, 0] = 1
    m = np.tile(m, (1, 1, 1, 16)); k = np.where((m == 1) | ((m == 2) & (rng.random(m.shape) < 0.5)), top, -1)
    ti = np.concatenate([np.array([T - 1, 0]), 1 + rng.permutation(T - 2)[:M * RO - 2]]).reshape(M, RO); z[:, :, :, ti.reshape(-1)] = 0
    for n in range(N):
        for g in range(8):
            quiet = (n == N - 1 and g == 7) or (n + g) % 3 == 0
            cand = T + rng.permutation(D - T); cand = cand[(cand & (F - 1)) != F - 1][:M * (RO * (L - 1) + 1)]
            dd = cand[:M].copy(); nodes = cand[M:].reshape(M, RO, L - 1)
            if not quiet: dd[0] = D - 1
            c[n, g, dd] = (CM - RO) * ((np.arange(M) + g) & 1); x[n, g, :, dd] = 0
            tb = np.ones(D, bool); tb[cand] = False; tb[dd] = False; tb[ti.reshape(-1)] = False; tb[D - 1] = False
            if quiet:
                tb[last] = False; x[n, g, :, last] = 15
            lv = np.flatnonzero(tb)
            for s in (0, 15):
                q = np.where(rng.random(D) < 0.05, lv[rng.integers(0, 4, D)], lv[rng.integers(0, len(lv), D)])
                live = q + D * (c[n, g][q] + (rng.random(D) < 0.1)); k[n, g, s] = np.where(rng.random(D) < 0.1, k[n, g, s], live)
            if quiet: k[n, g, 15, last] = top
            for j in range(M):
                for t in range(RO):
                    v = ti[j, t]
                    for a in nodes[j, t]:
                        k[n, g, 0, v] = a + D * c[n, g, a]; v = a
                    k[n, g, 0, v] = dd[j] + D * (c[n, g, dd[j]] + t)
    return pack(k, x, c, z)
def setup_inputs_spread(rng):
    pw = rng.choice(np.array([0.3, 1.0, 4.0]), (N, 8, 1)); c = np.minimum(((CM - RO + 1) * rng.random((N, 8, D)) ** pw).astype(np.int64), CM - RO)
    pw = rng.choice(np.array([0.6, 1.0, 1.7]), (N, 8, 1, 1)); p = np.minimum((D * rng.random((N, 8, 16, D)) ** pw).astype(np.int64), D - 1)
    x = np.minimum((16 * rng.random((N, 8, 16, D)) ** rng.choice(np.array([0.4, 1.0, 2.5]), (N, 8, 1, D))).astype(np.int64), 15)
    z = np.minimum((16 * rng.random((N, 8, 16, T)) ** rng.choice(np.array([0.4, 1.0, 2.5]), (N, 8, 1, T))).astype(np.int64), 15)
    return pack(np.where(rng.random(p.shape) < 0.03, -1, p + D * grow(rng, c, p)), x, c, z)
def check_inputs(d):
    bad = []
    for k, lo, hi in (("nkey", -1, D * (CM + 1) - 1), ("xreg", 0, 15), ("cnt", 0, CM - RO), ("zin", 0, 15)):
        a = np.asarray(d[k]).astype(np.float64)
        if not (np.min(a) >= lo and np.max(a) <= hi): bad.append("range of " + k)
        elif np.any(a != np.floor(a)): bad.append("whole numbers in " + k)
    return bad
def reference(nkey, xreg, cnt, zin):
    K = nkey.astype(np.int64).reshape(N, 8, 16, D); X = xreg.astype(np.float32).astype(np.int64).reshape(N, 8, 16, D)
    C = cnt.astype(np.int64); Z = zin.astype(np.float32).astype(np.int64).reshape(N, 8, 16, T)
    for t in range(RO):
        if t > 0: Z = np.roll(Z, (1, t), axis=(0, 1))
        for q in range(N):
            for h in range(8):
                k, x, c, z = K[q, h], X[q, h], C[q, h], Z[q, h]
                v = np.arange(T); ok = np.ones(T, bool); key = None
                for m in range(L):
                    s = z[L * t + m].copy(); back = key
                    key = k[s, v]; v = key & (D - 1)
                    ok = ok & (key >= 0) & ((key >> SH) == c[v])
                w = np.flatnonzero(ok); d = v[w]
                u, first = np.unique(d, return_index=True); win = w[first]
                left = z[:, win]
                z[:, w] = x[:, d]
                x[:, u] = left
                c[u] += 1
                k[s[win], u] = back[win]
                k[t, w] = d + D * c[d]
    return {"yz": Z.reshape(N, 128, T).astype(np.float32).astype(BF), "yk": np.add.reduce(K.reshape(N, 128, 16, D >> 4), axis=2).astype(np.float32),
            "yx": np.add.reduce(X.reshape(N, 128, 16, D >> 4), axis=2).astype(np.float32).astype(BF), "yc": C.astype(np.float32)}

@@ -1,0 +1,417 @@
+from concourse.mybir import AluOpType as A, ActivationFunctionType as F
+
+f32, bf, i32, u16 = "float32", "bfloat16", "int32", "uint16"
+SCRATCH = {
+    "K": ("sbuf", [128, 2560], f32), "H": ("sbuf", [128, 4096], bf), "M": ("sbuf", [128, 2560], f32),
+    "NUM": ("sbuf", [128, 2064], f32), "Mb": ("sbuf", [128, 2048], bf), "G": ("sbuf", [128, 2048], bf),
+    "zi1": ("sbuf", [128, 512], bf), "zi2": ("sbuf", [128, 512], bf), "zi3": ("sbuf", [128, 512], bf),
+    "zo0": ("sbuf", [128, 512], bf), "zo1": ("sbuf", [128, 512], bf), "zo2": ("sbuf", [128, 512], bf),
+    "zo3": ("sbuf", [128, 512], bf),
+    "m1": ("sbuf", [128, 512], f32), "m2": ("sbuf", [128, 512], f32), "nm2": ("sbuf", [128, 512], f32),
+    "Mk0": ("sbuf", [128, 512], f32), "Mk1": ("sbuf", [128, 512], f32), "Mk2": ("sbuf", [128, 512], f32),
+    "Aa": ("sbuf", [128, 512], f32), "Bb": ("sbuf", [128, 512], f32), "S": ("sbuf", [128, 512], f32),
+    "D": ("sbuf", [128, 768], f32), "E": ("sbuf", [128, 768], bf), "NM": ("sbuf", [128, 512], bf),
+    "C12": ("sbuf", [128, 1024], bf), "C3": ("sbuf", [128, 512], bf),
+    "tmp": ("sbuf", [128, 64], f32), "key": ("sbuf", [128, 96], i32), "vi": ("sbuf", [128, 96], i32),
+    "off": ("sbuf", [128, 96], u16), "q01": ("sbuf", [128, 64], f32), "q2": ("sbuf", [128, 32], f32),
+    "ne": ("sbuf", [128, 64], bf), "ay": ("sbuf", [128, 32], f32), "zf": ("sbuf", [128, 32], f32),
+    "zoff": ("sbuf", [128, 32], u16), "big": ("sbuf", [128, 32], f32), "Wd": ("sbuf", [128, 32], f32),
+    "offD": ("sbuf", [128, 48], u16), "sf": ("sbuf", [128, 32], f32), "soff": ("sbuf", [128, 32], u16),
+    "ip": ("sbuf", [128, 1], i32), "pm": ("sbuf", [128, 1], i32), "pf": ("sbuf", [128, 1], f32),
+    "pc": ("sbuf", [128, 1], f32), "g16": ("sbuf", [128, 1], f32), "h8": ("sbuf", [128, 1], f32),
+    "ix": ("sbuf", [128, 144], f32), "ib": ("sbuf", [128, 256], f32), "ih": ("sbuf", [128, 64], f32),
+    "iw": ("sbuf", [128, 128], f32), "own": ("sbuf", [128, 128], f32),
+    "RM": ("sbuf", [128, 16], f32), "LT": ("sbuf", [128, 16], f32), "WC": ("sbuf", [128, 32], f32),
+    "BB": ("sbuf", [128, 256], bf), "BBf": ("sbuf", [128, 128], f32), "II": ("sbuf", [128, 256], bf),
+    "idf": ("sbuf", [128, 128], f32), "idm": ("sbuf", [128, 128], f32), "IW": ("sbuf", [128, 256], bf),
+    "F1": ("sbuf", [128, 144], bf), "Ff": ("sbuf", [128, 136], f32), "FW": ("sbuf", [128, 864], bf),
+    "TR": ("sbuf", [128, 2048], bf), "Sel": ("sbuf", [128, 1536], bf), "Ssel": ("sbuf", [128, 128], bf),
+    "Con": ("sbuf", [128, 512], bf), "hm": ("sbuf", [128, 64], f32), "FL": ("sbuf", [128, 48], u16),
+    "eps": ("sbuf", [128, 32], bf), "ci": ("sbuf", [128, 128], i32), "cm": ("sbuf", [128, 384], f32),
+    "lo32": ("sbuf", [128, 128], f32),
+    "fo": ("sbuf", [128, 128], u16), "t3": ("sbuf", [128, 512], f32), "ok_": ("sbuf", [128, 128], f32),
+    "ox": ("sbuf", [128, 128], bf), "oc": ("sbuf", [128, 128], f32),
+    "pa": ("psum", [128, 512], f32), "pb": ("psum", [128, 512], f32), "pcc": ("psum", [128, 512], f32),
+    "pd": ("psum", [128, 512], f32), "pe": ("psum", [128, 512], f32), "pw": ("psum", [128, 512], f32),
+    "pg": ("psum", [128, 512], f32), "ph": ("psum", [128, 512], f32),
+}
+NDMA = 20
+SEMAPHORES = ["sv", "ss", "sp", "sg", "arr1", "arr2", "arr3", "snt"] + ["d%d" % k for k in range(NDMA)]
+BANKS = ("pa", "pb", "pcc", "pd", "pe", "pw", "pg", "ph")
+PIECES = ("FL", "TR", "Con", "offD")
+VISITS = 4
+
+
+def route(T, topo, r):
+    src, dst = T.cores[r], T.cores[(r + 1) % len(T.cores)]
+    if topo.may_write(src, dst):
+        return [src, dst]
+    cand = [c for c in topo.cores_of(src) if T.rank_of(c) is None and topo.may_write(c, dst)]
+    near = [c for c in cand if topo.die(c) == topo.die(src)]
+    return [src, (near or cand)[0], dst]
+
+
+def emit(g, T, ops):
+    q = {"v": g.vector, "s": g.scalar, "p": g.tensor, "g": g, "y": g.sync}
+    writer, readers, before, known = {}, {}, {}, {e: {} for e in q}
+    count = {e: 0 for e in q}
+    ndma = [0]
+    for o in ops:
+        e = o["e"]
+        deps = []
+        for r in o["r"]:
+            deps += writer.get(r, [])
+            if r in BANKS:
+                deps += [x for x in readers.get(r, []) if x["e"] != e]
+        for w in o["w"]:
+            if w in PIECES and not readers.get(w):
+                deps += before.get(w, [])
+                continue
+            old = writer.get(w, []) + readers.get(w, [])
+            before[w] = old
+            deps += [x for x in old if x["e"] != "p" or e != "p"]
+        waits = []
+        if o["kind"] != "x":
+            kn = known[e]
+            deps.sort(key=lambda x: -x["pos"])
+            for x in deps:
+                k, n = x["tok"]
+                if kn.get(k, 0) >= n:
+                    continue
+                waits.append(x)
+                x["need"] = True
+                for kk, nn in x["clock"].items():
+                    kn[kk] = max(kn.get(kk, 0), nn)
+        o["waits"] = waits
+        if o["kind"] == "c":
+            count[e] += 1
+            o["tok"] = (e, count[e])
+        elif o["kind"] == "d":
+            o["tok"] = ("d%d" % ndma[0], 1)
+            ndma[0] += 1
+        elif o["kind"] == "x":
+            o["tok"] = (o["sem"], 1)
+        else:
+            o["tok"] = ("none", 0)
+        o["clock"] = {} if o["kind"] == "x" else dict(known[e])
+        o["clock"][o["tok"][0]] = o["tok"][1]
+        for r in o["r"]:
+            readers.setdefault(r, []).append(o)
+        for w in o["w"]:
+            keep = writer.get(w, []) if w in PIECES and not readers.get(w) else []
+            writer[w] = keep + [o]
+            readers[w] = []
+    run = {e: 0 for e in q}
+    for o in ops:
+        if o["kind"] == "c" and o.get("need"):
+            run[o["e"]] += 1
+            o["val"] = (T.sem["s" + o["e"]], run[o["e"]])
+        elif o["kind"] == "d":
+            o["val"] = (T.sem[o["tok"][0]], 16)
+        elif o["kind"] == "x":
+            o["val"] = (T.sem[o["sem"]], o["n"])
+    for o in ops:
+        if o["kind"] == "x":
+            continue
+        for x in o["waits"]:
+            q[o["e"]].wait_ge(x["val"][0], x["val"][1])
+        ins = o["fn"]()
+        if o["kind"] == "d":
+            ins.then_inc(o["val"][0], 16)
+        elif o["kind"] == "c" and o.get("need"):
+            ins.then_inc(o["val"][0], 1)
+    for o in ops:
+        if o["kind"] == "d" and not o.get("need"):
+            q[o["e"]].wait_ge(o["val"][0], 16)
+
+
+def rank_program(g, core, T, topo):
+    n = len(T.cores)
+    rank = T.rank_of(core)
+    if rank is None:
+        for r in range(n):
+            way = route(T, topo, r)
+            if len(way) == 3 and way[1] == core:
+                rid, pid = topo.addr(way[2], core)
+                for t in range(1, VISITS):
+                    g.wait_ge(T.sem["arr%d" % t], len(topo.engines(way[0], core)))
+                    g.remote_dma(T["zi%d" % t][:], T["zi%d" % t][:], T.sem["arr%d" % t], T.sem.snt, pid, rid,
+                                 topo.mask(core, way[2]))
+                g.wait_ge(T.sem.snt, (VISITS - 1) * len(topo.engines(core, way[2])))
+        return
+    nxt = route(T, topo, rank)[1]
+    n_in = len(topo.engines(route(T, topo, (rank - 1) % n)[-2], core))
+    V, S, P = g.vector, g.scalar, g.tensor
+    ops = []
+
+    def add(e, fn, r, w, kind="c", **kw):
+        o = {"e": e, "fn": fn, "r": list(r), "w": list(w), "kind": kind, "pos": len(ops)}
+        o.update(kw)
+        ops.append(o)
+
+    def ts(out, in0, s1, s2, o0, o1, r, w):
+        if o1 is None:
+            add("v", lambda: V.tensor_scalar(out, in0, s1, None, o0), r, w)
+        else:
+            add("v", lambda: V.tensor_scalar(out, in0, s1, s2, o0, o1), r, w)
+
+    def tt(out, a, b, op, r, w):
+        add("v", lambda: V.tensor_tensor(out, a, b, op), r, w)
+
+    def cp(out, a, r, w):
+        add("v", lambda: V.tensor_copy(out, a), r, w)
+
+    def act(out, a, r, w, func=F.Identity, **kw):
+        add("s", lambda: S.activation(out, a, func, **kw), r, w)
+
+    def mm(out, l, rhs, st, sp, r, w):
+        add("p", lambda: P.matmul(out, l, rhs, st, sp), r, w)
+
+    def iota(out, pat, base, cm, w, flag=True):
+        if flag:
+            add("g", lambda: g.iota(out, pat, base, cm, allow_small_or_imprecise_dtypes=True), [], w)
+        else:
+            add("g", lambda: g.iota(out, pat, base, cm), [], w)
+
+    def dma(e, out, in_, r, w):
+        qq = g.sync if e == "y" else g.scalar
+        add(e, lambda: qq.dma_start(out, in_), r, w, kind="d")
+
+    def col(k):
+        return T.WC[:, k:k + 1]
+
+    def rm(k):
+        return T.RM[:, k:k + 1]
+
+    def fw(k, r):
+        return T.FW[:, 144 * k + 16 - r:144 * k + 144 - r]
+
+    KALL = ["Ka", "Kb", "Kc"]
+    dma("y", T.H[:, 2048:2560], T.zin[:], [], ["H0"])
+    dma("y", T.K[:, 0:512], T.nkey[:, 0:512], [], ["Ka"])
+    dma("s", T.ci[:], T.cnt[:], [], ["ci"])
+    dma("y", T.K[:, 512:1280], T.nkey[:, 512:1280], [], ["Kb"])
+    dma("y", T.K[:, 1280:2048], T.nkey[:, 1280:2048], [], ["Kc"])
+    dma("y", T.H[:, 0:2048], T.xreg[:], [], ["Hx"])
+    iota(T.ip[:], [[0, 1]], 0, 1, ["ip"], flag=False)
+    iota(T.ix[:], [[1, 144]], 0, 0, ["ix"])
+    iota(T.ib[:], [[0, 2], [16, 8], [0, 16]], 0, 0, ["ib"])
+    iota(T.ih[:], [[0, 32], [1, 2]], 0, 0, ["ih"])
+    iota(T.M[:, 0:2048], [[0, 2048]], 0, 0, ["M"])
+    iota(T.iw[:], [[16, 128]], 2048, 0, ["iw"])
+    iota(T.NUM[:], [[1, 2064]], 0, 0, ["NUM"])
+    ts(T.pm[:], T.ip[:], 15, None, A.bitwise_and, None, ["ip"], ["pm"])
+    cp(T.pf[:], T.ip[:], ["ip"], ["pf"])
+    cp(T.pc[:], T.pm[:], ["pm"], ["pc"])
+    tt(T.g16[:], T.pf[:], T.pc[:], A.subtract, ["pf", "pc"], ["g16"])
+    ts(T.RM[:], T.ix[:, 0:16], T.pc[:], None, A.is_equal, None, ["ix", "pc"], ["RM"])
+    ts(T.F1[:], T.ix[:], -16.0, T.g16[:], A.add, A.is_equal, ["ix", "g16"], ["F1"])
+    ts(T.h8[:], T.pc[:], 8.0, None, A.is_ge, None, ["pc"], ["h8"])
+    ts(T.BB[:], T.ib[:], T.g16[:], None, A.is_equal, None, ["ib", "g16"], ["BB"])
+    tt(T.Ff[:], T.F1[:, 8:144], T.F1[:, 0:136], A.add, ["F1"], ["Ff"])
+    for m in range(3):
+        ts(T.Sel[:, 128 * m:128 * m + 128], T.BB[:, 128:256], rm(m), None, A.mult, None, ["BB", "RM"], ["Sel%d" % m])
+    ts(T.hm[:], T.ih[:], T.h8[:], None, A.is_equal, None, ["ih", "h8"], ["hm"])
+    ts(T.idf[:], T.ix[:, 0:128], T.pf[:], None, A.is_equal, None, ["ix", "pf"], ["idf"])
+    ts(T.cm[:, 0:128], T.ci[:], 32.0, None, A.mult, None, ["ci"], ["cm0"])
+    ts(T.BBf[:], T.ib[:, 0:128], T.g16[:], None, A.is_equal, None, ["ib", "g16"], ["BBf"])
+    ts(T.LT[:], T.ix[:, 0:16], T.pc[:], 4096.0, A.is_gt, A.mult, ["ix", "pc"], ["LT"])
+    cp(T.FL[:, 0:32], T.ix[:, 0:32], ["ix"], ["FL"])
+    cp(T.FL[:, 32:48], T.ix[:, 0:32:2], ["ix"], ["FL"])
+    add("v", lambda: V.memset(T.eps[:], 2.0 ** -9), [], ["eps"])
+    act(T.lo32[:], T.ix[:, 0:128], ["ix"], ["lo32"], scale=32.0)
+    act(T.cm[:, 128:256], T.lo32[:], ["lo32"], ["cm1"], func=F.Silu)
+    act(col(9), T.pc[:], ["pc"], ["w9"], scale=32.0)
+    act(col(10), rm(1), ["RM"], ["w10"], scale=1.0 / 32)
+    act(col(11), rm(3), ["RM"], ["w11"], scale=1.0 / 32)
+    act(T.cm[:, 256:384], T.ix[:, 0:128], ["ix", "w9"], ["cm2"], scale=0.0, bias=col(9))
+    act(col(2), rm(0), ["RM"], ["w2"], scale=64.0)
+    act(col(0), rm(2), ["RM", "w10"], ["w0"], scale=4.0, bias=col(10))
+    act(col(12), rm(4), ["RM", "w11"], ["w12"], scale=4.0, bias=col(11))
+    act(col(13), rm(3), ["RM"], ["w13"], bias=rm(4))
+    act(T.FW[:, 288:432], T.F1[:], ["F1", "w2"], ["FW2"], scale=col(2))
+    act(col(1), rm(0), ["RM", "w0"], ["w1"], scale=256.0, bias=col(0))
+    act(col(4), rm(0), ["RM", "w12"], ["w4"], scale=64.0, bias=col(12))
+    act(col(5), rm(0), ["RM", "w13"], ["w5"], bias=col(13))
+    act(col(3), rm(0), ["RM"], ["w3"], scale=1.0 / 32)
+    act(col(6), rm(0), ["RM"], ["w6"], scale=32.0)
+    act(col(7), rm(1), ["RM"], ["w7"], scale=32.0)
+    act(col(8), rm(2), ["RM"], ["w8"], scale=32.0)
+    act(T.WC[:, 24:28], T.RM[:, 0:4], ["RM"], ["wn"], scale=-2048.0, bias=1.0)
+    act(T.FW[:, 144:288], T.F1[:], ["F1", "w1"], ["FW1"], scale=col(1))
+    act(T.WC[:, 16:20], T.ix[:, 0:4], ["ix", "w8"], ["wb"], scale=col(8))
+    act(T.WC[:, 20:24], T.ix[:, 16:32:4], ["ix", "w8"], ["wt"], scale=col(8))
+    act(T.idm[:], T.idf[:], ["idf"], ["idm"], scale=-4.0)
+    act(T.IW[:, 0:128], T.idf[:], ["idf"], ["IW0"], scale=-2.0 ** 22)
+    act(T.II[:, 0:128], T.idf[:], ["idf"], ["II0"])
+    for row, f in ((0, 0), (1, 1), (2, 2), (3, 1), (4, 2)):
+        dma("y", T.M[row:128:16, 0:2048], T.cm[:, 128 * f:128 * f + 128], ["cm%d" % f, "M"], ["Mr%d" % row])
+    MALL = ["M"] + ["Mr%d" % k for k in range(5)]
+
+    def late0():
+        act(T.Ssel[:], T.idf[:], ["idf", "w5"], ["Ssel"], scale=col(5))
+        for b in range(4):
+            act(T.Con[:, 128 * b:128 * b + 128], T.ix[:, 0:128], ["ix", "w7", "wb"], ["Con"], scale=col(7),
+                bias=col(16 + b))
+        act(T.FW[:, 720:864], T.F1[:], ["F1"], ["FW5"], scale=4096.0)
+        for r in range(1, 6):
+            tri(r)
+
+    def tri(r):
+        act(T.TR[:, 128 * r:128 * r + 128], T.F1[:, 16 - r:144 - r], ["F1", "LT"], ["TR"], scale=T.LT[:, r:r + 1])
+
+    def late1():
+        for r in range(6, 16):
+            tri(r)
+
+    def late2():
+        act(T.FW[:, 576:720], T.F1[:], ["F1", "w4"], ["FW4"], scale=col(4))
+        act(T.IW[:, 128:256], T.idf[:], ["idf"], ["IW1"], scale=2.0 ** 22)
+        act(T.II[:, 128:256], T.idf[:], ["idf"], ["II1"])
+
+    def sel(t):
+        for m in range(3):
+            k = 3 * t + m
+            act(T.Sel[:, 128 * k:128 * k + 128], T.BB[:, 128 - 16 * t:256 - 16 * t], ["BB", "RM"], ["Sel%d" % k],
+                scale=rm(k))
+
+    def wrap(m):
+        Mk = T["Mk%d" % m]
+        for r in range(8):
+            mm(T.pw[:, 0:64], T.Ff[:, 8 - r:136 - r], Mk[:, r:512:8], r == 0, r == 7, ["Ff", "Mk%d" % m], ["pw"])
+
+    def cut(m):
+        c = slice(32 * m, 32 * m + 32)
+        tt(T.tmp[:], T.pw[:, 0:64], T.hm[:], A.mult, ["pw", "hm"], ["tmp"])
+        tt(T.key[:, c], T.tmp[:, 0:64:2], T.tmp[:, 1:64:2], A.add, ["tmp"], ["key%d" % m])
+        ts(T.vi[:, c], T.key[:, c], 2047, None, A.bitwise_and, None, ["key%d" % m], ["vi%d" % m])
+        cp(T.off[:, c], T.vi[:, c], ["vi%d" % m], ["off%d" % m])
+
+    sent = 0
+    for t in range(VISITS):
+        hz = slice(2048 + 512 * t, 2560 + 512 * t)
+        HALL = ["Hx"] + ["H%d" % k for k in range(t + 1)]
+        if t == 0:
+            z, zr = T.H[:, hz], "H0"
+        else:
+            z, zr = T["zi%d" % t][:], "zi%d" % t
+            add("x", None, [], [zr], kind="x", sem="arr%d" % t, n=n_in)
+        for m, b in enumerate(("pa", "pb", "pcc")):
+            k = 3 * t + m
+            mm(T[b][:], T.Sel[:, 128 * k:128 * k + 128], z, True, True, ["Sel%d" % k, zr], [b])
+        if t > 0:
+            mm(T.pd[:], T.II[:, 128 - 16 * t:256 - 16 * t], z, True, True, ["II0", "II1", zr], ["pd"])
+            act(T.H[:, hz], T.pd[:], ["pd"], ["H%d" % t])
+        ts(T.pe[:], T.pa[:], T.pc[:], None, A.is_equal, None, ["pa", "pc"], ["pe"])
+        tt(T.Mk0[:], T.K[:, 0:512], T.pe[:], A.mult, ["Ka", "pe"], ["Mk0"])
+        wrap(0)
+        ts(T.m1[:], T.pb[:], T.pc[:], None, A.is_equal, None, ["pb", "pc"], ["m1"])
+        if t == 0:
+            ts(T.own[:], T.iw[:], T.pc[:], None, A.add, None, ["iw", "pc"], ["own"])
+        cut(0)
+        tt(T.Mk1[:], T.K[:, 0:2048].indirect(T.off[:, 0:32]), T.m1[:], A.mult, KALL + ["off0", "m1"], ["Mk1"])
+        if t == 0:
+            late0()
+        act(T.C12[:, 0:512], T.M[:, 0:2048].indirect(T.off[:, 0:32]), MALL + ["off0"], ["C1"])
+        if t == 0:
+            late1()
+        wrap(1)
+        mm(T.pa[:], T.BBf[:], T.Mk1[:], True, True, ["BBf", "Mk1"], ["pa"])
+        ts(T.m2[:], T.pcc[:], T.pc[:], None, A.is_equal, None, ["pcc", "pc"], ["m2"])
+        ts(T.nm2[:], T.pcc[:], T.pc[:], None, A.not_equal, None, ["pcc", "pc"], ["nm2"])
+        cut(1)
+        tt(T.Mk2[:], T.K[:, 0:2048].indirect(T.off[:, 32:64]), T.m2[:], A.mult, KALL + ["off1", "m2"], ["Mk2"])
+        act(T.C12[:, 512:1024], T.M[:, 0:2048].indirect(T.off[:, 32:64]), MALL + ["off1"], ["C2"])
+        if t == 0:
+            late2()
+        if t < VISITS - 1:
+            sel(t + 1)
+        else:
+            act(T.FW[:, 0:144], T.F1[:], ["F1", "w0"], ["FW0"], scale=col(0))
+            act(T.FW[:, 432:576], T.F1[:], ["F1", "w3"], ["FW3"], scale=col(3))
+        wrap(2)
+        for r in range(16):
+            mm(T.pg[:, 0:64], fw(2, r), T.C12[:, r:1024:16], r == 0, r == 15, ["FW2", "C1", "C2"], ["pg"])
+        tt(T.q01[:], T.key[:, 0:64], T.vi[:, 0:64], A.subtract, ["key0", "key1", "vi0", "vi1"], ["q01"])
+        tt(T.Aa[:], T.pa[:], T.m2[:], A.mult, ["pa", "m2"], ["Aa"])
+        cut(2)
+        act(T.C3[:], T.M[:, 0:2048].indirect(T.off[:, 64:96]), MALL + ["off2", "w6"], ["C3"], bias=col(6))
+        tt(T.q2[:], T.key[:, 64:96], T.vi[:, 64:96], A.subtract, ["key2", "vi2"], ["q2"])
+        tt(T.ne[:], T.pg[:, 0:64], T.q01[:], A.not_equal, ["pg", "q01"], ["ne"])
+        tt(T.Bb[:], T.K[:, 0:2048].indirect(T.off[:, 64:96]), T.nm2[:], A.mult, KALL + ["off2", "nm2"], ["Bb"])
+        y = T.pg[:, 64:96]
+        mm(y, T.idm[:], T.q2[:], True, False, ["idm", "q2"], ["pg"])
+        mm(y, T.IW[:, 0:128], T.eps[:], False, False, ["IW0", "eps"], ["pg"])
+        mm(y, T.IW[:, 0:128], T.ne[:, 0:32], False, False, ["IW0", "ne"], ["pg"])
+        mm(y, T.IW[:, 0:128], T.ne[:, 32:64], False, False, ["IW0", "ne"], ["pg"])
+        for r in range(16):
+            mm(y, fw(1, r), T.C3[:, r:512:16], False, r == 15, ["FW1", "C3"], ["pg"])
+        mm(T.pb[:], T.Ssel[:], T.C3[:], True, False, ["Ssel", "C3"], ["pb"])
+        mm(T.pb[:], T.II[:, 0:128], T.Con[:], False, True, ["II0", "Con"], ["pb"])
+        act(T.ay[:], y, ["pg"], ["ay"], func=F.Abs)
+        tt(T.zf[:], T.ay[:], T.own[:, 32 * t:32 * t + 32], A.min, ["ay", "own"], ["zf"])
+        ts(T.big[:], T.ay[:], 4095.5, 4096.0, A.is_ge, A.mult, ["ay"], ["big"])
+        cp(T.zoff[:], T.zf[:], ["zf"], ["zoff"])
+        tt(T.Wd[:], T.vi[:, 64:96], T.big[:], A.add, ["vi2", "big"], ["Wd"])
+        ts(T.offD[:, 0:32], T.Wd[:], 2048.0, None, A.min, None, ["Wd"], ["offD"])
+        ts(T.offD[:, 32:48], T.Wd[:, 1:32:2], 2048.0, None, A.min, None, ["Wd"], ["offD"])
+        zo = T["zo%d" % t]
+        cp(zo[:], T.H[:, 0:hz.stop].indirect(T.zoff[:]), HALL + ["zoff"], ["zo%d" % t])
+        if t < VISITS - 1:
+            rid, pid = topo.addr(nxt, core)
+            add("g", lambda a=T["zi%d" % (t + 1)][:], b=zo[:], s=T.sem["arr%d" % (t + 1)]:
+                g.remote_dma(a, b, s, T.sem.snt, pid, rid, topo.mask(core, nxt)), ["zo%d" % t], [], kind="r")
+            sent += len(topo.engines(core, nxt))
+        else:
+            dma("y", T.yz[:], zo[:], ["zo%d" % t], [])
+        act(T.D[:, 512:768], T.NUM[:].indirect(T.offD[:, 32:48]), ["NUM", "offD"], ["D1"])
+        act(T.D[:, 0:512], T.NUM[:].indirect(T.offD[:, 0:32]), ["NUM", "offD"], ["D0"])
+        act(T.S[:], T.pb[:], ["pb", "wt"], ["S"], bias=col(20 + t))
+        act(T.NM[:], T.D[:, 0:512], ["D0", "RM", "wn"], ["NM"], func=F.Relu, scale=rm(t), bias=col(24 + t))
+        tt(T.E[:, 512:768], T.Wd[:].indirect(T.FL[:, 32:48]), T.D[:, 512:768], A.is_equal, ["Wd", "FL", "D1"], ["E1"])
+        tt(T.E[:, 0:512], T.Wd[:].indirect(T.FL[:, 0:32]), T.D[:, 0:512], A.is_equal, ["Wd", "FL", "D0"], ["E0"])
+        mm(T.ph[:, 0:32], T.idf[:], T.Wd[:], True, False, ["idf", "Wd"], ["ph"])
+        for r in range(16):
+            mm(T.ph[:, 1:32:2], fw(5, r), T.E[:, 512 + r:768:16], False, False, ["FW5", "E1"], ["ph"])
+        for r in range(1, 16):
+            mm(T.ph[:, 0:32], T.TR[:, 128 * r:128 * r + 128], T.E[:, r:512:16], False, r == 15, ["TR", "E0"], ["ph"])
+        for b, w in (("pa", 1), ("pcc", 0)):
+            mm(T[b][:], fw(4, t), T.C3[:], True, False, ["FW4", "C3"], [b])
+            mm(T[b][:], T.IW[:, 128 * w:128 * w + 128], T.NM[:], False, True, ["IW%d" % w, "NM"], [b])
+        tt(T.sf[:], T.ph[:, 0:32], T.own[:, 0:32], A.min, ["ph", "own"], ["sf"])
+        cp(T.soff[:], T.sf[:], ["sf"], ["soff"])
+        for c in range(15, -1, -1):
+            u = slice(32 * c, 32 * c + 32)
+            o = T.soff[:, 2 * c:2 * c + 2]
+            tt(T.K[:].indirect(o), T.Aa[:, u], T.Bb[:, u], A.add, ["soff", "Aa", "Bb"], KALL)
+            act(T.M[:].indirect(o), T.S[:, u], ["soff", "S"], MALL, func=F.Silu)
+        tt(T.K[:, 0:512], T.K[:, 0:512], T.pa[:], A.min, ["Ka", "pa"], ["Ka"])
+        tt(T.K[:, 0:512], T.K[:, 0:512], T.pcc[:], A.max, ["Ka", "pcc"], ["Ka"])
+    for h in range(4):
+        u = slice(512 * h, 512 * h + 512)
+        act(T.Mb[:, u], T.M[:, u], MALL, ["Mb%d" % h])
+    for b in range(16):
+        mm(T.pd[:, 0:128], fw(0, b), T.Mb[:, 128 * b:128 * b + 128], b == 0, b == 15, ["FW0", "Mb%d" % (b // 4)], ["pd"])
+    for b in range(16):
+        mm(T.pb[:, 0:128], fw(3, b), T.Mb[:, 128 * b:128 * b + 128], b == 0, b == 15, ["FW3", "Mb%d" % (b // 4)], ["pb"])
+    tt(T.pe[:], T.K[:, 0:512], T.K[:, 512:1024], A.add, KALL, ["pe"])
+    cp(T.fo[:], T.pd[:, 0:128], ["pd"], ["fo"])
+    HALL = ["Hx", "H0", "H1", "H2", "H3"]
+    act(T.G[:, 0:1024], T.H[:].indirect(T.fo[:, 0:64]), HALL + ["fo"], ["G0"])
+    act(T.oc[:], T.pb[:, 0:128], ["pb"], ["oc"])
+    dma("s", T.yc[:], T.oc[:], ["oc"], [])
+    cp(T.G[:, 1024:2048], T.H[:].indirect(T.fo[:, 64:128]), HALL + ["fo"], ["G1"])
+    tt(T.pg[:], T.pe[:], T.K[:, 1024:1536], A.add, KALL + ["pe"], ["pg"])
+    tt(T.t3[:], T.pg[:], T.K[:, 1536:2048], A.add, KALL + ["pg"], ["t3"])
+    tt(T.pe[:, 0:128], T.t3[:, 0:128], T.t3[:, 128:256], A.add, ["t3"], ["pe"])
+    tt(T.pg[:, 0:128], T.pe[:, 0:128], T.t3[:, 256:384], A.add, ["t3", "pe"], ["pg"])
+    tt(T.ok_[:], T.pg[:, 0:128], T.t3[:, 384:512], A.add, ["t3", "pg"], ["ok_"])
+    dma("y", T.yk[:], T.ok_[:], ["ok_"], [])
+    for h, b in enumerate(("pw", "ph")):
+        for r in range(16):
+            mm(T[b][:, 0:64], T.II[:, 0:128], T.G[:, 1024 * h + r:1024 * h + 1024:16], r == 0, r == 15,
+               ["II0", "G%d" % h], [b])
+        act(T.ox[:, 64 * h:64 * h + 64], T[b][:, 0:64], [b], ["ox%d" % h])
+    dma("s", T.yx[:], T.ox[:], ["ox0", "ox1"], [])
+    emit(g, T, ops)
+    g.wait_ge(T.sem.snt, sent)

@@ -16,7 +16,7 @@ SCRATCH = {
     "off": ("sbuf", [128, 96], u16), "q01": ("sbuf", [128, 64], f32), "q2": ("sbuf", [128, 32], f32),
     "ne": ("sbuf", [128, 64], bf), "ay": ("sbuf", [128, 32], f32), "zf": ("sbuf", [128, 32], f32),
     "zoff": ("sbuf", [128, 32], u16), "big": ("sbuf", [128, 32], f32), "Wd": ("sbuf", [128, 32], f32),
-    "offD": ("sbuf", [128, 48], u16), "sf": ("sbuf", [128, 32], f32), "soff": ("sbuf", [128, 32], u16),
+    "offD": ("sbuf", [128, 16], u16), "sf": ("sbuf", [128, 32], f32), "soff": ("sbuf", [128, 32], u16),
     "ip": ("sbuf", [128, 1], i32), "pm": ("sbuf", [128, 1], i32), "pf": ("sbuf", [128, 1], f32),
     "pc": ("sbuf", [128, 1], f32), "g16": ("sbuf", [128, 1], f32), "h8": ("sbuf", [128, 1], f32),
     "ix": ("sbuf", [128, 144], f32), "ib": ("sbuf", [128, 256], f32), "ih": ("sbuf", [128, 64], f32),
@@ -27,8 +27,8 @@ SCRATCH = {
     "F1": ("sbuf", [128, 144], bf), "Ff": ("sbuf", [128, 136], f32), "FW": ("sbuf", [128, 864], bf),
     "TR": ("sbuf", [128, 2048], bf), "Sel": ("sbuf", [128, 1536], bf), "Ssel": ("sbuf", [128, 128], bf),
     "Con": ("sbuf", [128, 512], bf), "hm": ("sbuf", [128, 64], f32), "FL": ("sbuf", [128, 48], u16),
-    "eps": ("sbuf", [128, 32], bf), "ci": ("sbuf", [128, 128], i32), "cm": ("sbuf", [128, 384], f32),
-    "lo32": ("sbuf", [128, 128], f32),
+    "eps": ("sbuf", [128, 32], bf), "ci": ("sbuf", [128, 128], i32), "cm": ("sbuf", [128, 128], f32),
+    "WB": ("sbuf", [128, 16], f32), "NT": ("sbuf", [128, 8], f32), "offN": ("sbuf", [128, 32], u16),
     "fo": ("sbuf", [128, 128], u16), "t3": ("sbuf", [128, 512], f32), "ok_": ("sbuf", [128, 128], f32),
     "ox": ("sbuf", [128, 128], bf), "oc": ("sbuf", [128, 128], f32),
     "pa": ("psum", [128, 512], f32), "pb": ("psum", [128, 512], f32), "pcc": ("psum", [128, 512], f32),
@@ -38,7 +38,8 @@ SCRATCH = {
 NDMA = 20
 SEMAPHORES = ["sv", "ss", "sp", "sg", "arr1", "arr2", "arr3", "snt"] + ["d%d" % k for k in range(NDMA)]
 BANKS = ("pa", "pb", "pcc", "pd", "pe", "pw", "pg", "ph")
-PIECES = ("FL", "TR", "Con", "offD")
+PIECES = ("FL", "TR", "Con", "Mp", "NT", "pe", "m1")
+EARLY = {True: False, False: False}
 VISITS = 4
 
 
@@ -192,12 +193,10 @@ def rank_program(g, core, T, topo):
     dma("s", T.ci[:], T.cnt[:], [], ["ci"])
     dma("y", T.K[:, 512:1280], T.nkey[:, 512:1280], [], ["Kb"])
     dma("y", T.K[:, 1280:2048], T.nkey[:, 1280:2048], [], ["Kc"])
-    dma("y", T.H[:, 0:2048], T.xreg[:], [], ["Hx"])
     iota(T.ip[:], [[0, 1]], 0, 1, ["ip"], flag=False)
     iota(T.ix[:], [[1, 144]], 0, 0, ["ix"])
     iota(T.ib[:], [[0, 2], [16, 8], [0, 16]], 0, 0, ["ib"])
     iota(T.ih[:], [[0, 32], [1, 2]], 0, 0, ["ih"])
-    iota(T.M[:, 0:2048], [[0, 2048]], 0, 0, ["M"])
     iota(T.iw[:], [[16, 128]], 2048, 0, ["iw"])
     iota(T.NUM[:], [[1, 2064]], 0, 0, ["NUM"])
     ts(T.pm[:], T.ip[:], 15, None, A.bitwise_and, None, ["ip"], ["pm"])
@@ -206,7 +205,10 @@ def rank_program(g, core, T, topo):
     tt(T.g16[:], T.pf[:], T.pc[:], A.subtract, ["pf", "pc"], ["g16"])
     ts(T.RM[:], T.ix[:, 0:16], T.pc[:], None, A.is_equal, None, ["ix", "pc"], ["RM"])
     ts(T.F1[:], T.ix[:], -16.0, T.g16[:], A.add, A.is_equal, ["ix", "g16"], ["F1"])
+    tt(T.WC[:, 28:30], T.RM[:, 1:3], T.RM[:, 3:5], A.add, ["RM"], ["w28"])
     ts(T.h8[:], T.pc[:], 8.0, None, A.is_ge, None, ["pc"], ["h8"])
+    ts(col(14), col(28), 32.0, None, A.mult, None, ["w28"], ["w14"])
+    ts(T.WB[:], T.ix[:, 0:16], col(29), 32.0, A.mult, A.mult, ["ix", "w28"], ["WB"])
     ts(T.BB[:], T.ib[:], T.g16[:], None, A.is_equal, None, ["ib", "g16"], ["BB"])
     tt(T.Ff[:], T.F1[:, 8:144], T.F1[:, 0:136], A.add, ["F1"], ["Ff"])
     for m in range(3):
@@ -219,12 +221,13 @@ def rank_program(g, core, T, topo):
     cp(T.FL[:, 0:32], T.ix[:, 0:32], ["ix"], ["FL"])
     cp(T.FL[:, 32:48], T.ix[:, 0:32:2], ["ix"], ["FL"])
     add("v", lambda: V.memset(T.eps[:], 2.0 ** -9), [], ["eps"])
-    act(T.lo32[:], T.ix[:, 0:128], ["ix"], ["lo32"], scale=32.0)
-    act(T.cm[:, 128:256], T.lo32[:], ["lo32"], ["cm1"], func=F.Silu)
-    act(col(9), T.pc[:], ["pc"], ["w9"], scale=32.0)
+    for b in range(16):
+        act(T.M[:, 128 * b:128 * b + 128], T.ix[:, 0:128], ["ix", "w14", "WB"], ["Mp"], func=F.Silu, scale=col(14),
+            bias=T.WB[:, b:b + 1])
+    dma("y", T.M[0:128:16, 0:2048], T.cm[:], ["cm0", "Mp"], ["M"])
+    dma("y", T.H[:, 0:2048], T.xreg[:], [], ["Hx"])
     act(col(10), rm(1), ["RM"], ["w10"], scale=1.0 / 32)
     act(col(11), rm(3), ["RM"], ["w11"], scale=1.0 / 32)
-    act(T.cm[:, 256:384], T.ix[:, 0:128], ["ix", "w9"], ["cm2"], scale=0.0, bias=col(9))
     act(col(2), rm(0), ["RM"], ["w2"], scale=64.0)
     act(col(0), rm(2), ["RM", "w10"], ["w0"], scale=4.0, bias=col(10))
     act(col(12), rm(4), ["RM", "w11"], ["w12"], scale=4.0, bias=col(11))
@@ -237,16 +240,15 @@ def rank_program(g, core, T, topo):
     act(col(6), rm(0), ["RM"], ["w6"], scale=32.0)
     act(col(7), rm(1), ["RM"], ["w7"], scale=32.0)
     act(col(8), rm(2), ["RM"], ["w8"], scale=32.0)
-    act(T.WC[:, 24:28], T.RM[:, 0:4], ["RM"], ["wn"], scale=-2048.0, bias=1.0)
+    act(T.NT[:, 0:8:2], T.RM[:, 0:4], ["RM"], ["NT"], scale=-1.0, bias=1.0)
+    act(T.NT[:, 1:8:2], T.RM[:, 0:4], ["RM"], ["NT"], scale=0.0, bias=1.0)
     act(T.FW[:, 144:288], T.F1[:], ["F1", "w1"], ["FW1"], scale=col(1))
     act(T.WC[:, 16:20], T.ix[:, 0:4], ["ix", "w8"], ["wb"], scale=col(8))
     act(T.WC[:, 20:24], T.ix[:, 16:32:4], ["ix", "w8"], ["wt"], scale=col(8))
     act(T.idm[:], T.idf[:], ["idf"], ["idm"], scale=-4.0)
     act(T.IW[:, 0:128], T.idf[:], ["idf"], ["IW0"], scale=-2.0 ** 22)
     act(T.II[:, 0:128], T.idf[:], ["idf"], ["II0"])
-    for row, f in ((0, 0), (1, 1), (2, 2), (3, 1), (4, 2)):
-        dma("y", T.M[row:128:16, 0:2048], T.cm[:, 128 * f:128 * f + 128], ["cm%d" % f, "M"], ["Mr%d" % row])
-    MALL = ["M"] + ["Mr%d" % k for k in range(5)]
+    MALL = ["M"]
 
     def late0():
         act(T.Ssel[:], T.idf[:], ["idf", "w5"], ["Ssel"], scale=col(5))
@@ -287,12 +289,9 @@ def rank_program(g, core, T, topo):
         ts(T.vi[:, c], T.key[:, c], 2047, None, A.bitwise_and, None, ["key%d" % m], ["vi%d" % m])
         cp(T.off[:, c], T.vi[:, c], ["vi%d" % m], ["off%d" % m])
 
-    sent = 0
-    for t in range(VISITS):
-        hz = slice(2048 + 512 * t, 2560 + 512 * t)
-        HALL = ["Hx"] + ["H%d" % k for k in range(t + 1)]
+    def head(t):
         if t == 0:
-            z, zr = T.H[:, hz], "H0"
+            z, zr = T.H[:, 2048:2560], "H0"
         else:
             z, zr = T["zi%d" % t][:], "zi%d" % t
             add("x", None, [], [zr], kind="x", sem="arr%d" % t, n=n_in)
@@ -301,8 +300,21 @@ def rank_program(g, core, T, topo):
             mm(T[b][:], T.Sel[:, 128 * k:128 * k + 128], z, True, True, ["Sel%d" % k, zr], [b])
         if t > 0:
             mm(T.pd[:], T.II[:, 128 - 16 * t:256 - 16 * t], z, True, True, ["II0", "II1", zr], ["pd"])
+
+    def mask0(u):
+        ts(T.pe[:, u], T.pa[:, u], T.pc[:], None, A.is_equal, None, ["pa", "pc"], ["pe"])
+
+    sent = 0
+    early = EARLY[n_in == len(topo.engines(nxt, core))]
+    for t in range(VISITS):
+        hz = slice(2048 + 512 * t, 2560 + 512 * t)
+        HALL = ["Hx"] + ["H%d" % k for k in range(t + 1)]
+        if t == 0:
+            head(0)
+        else:
             act(T.H[:, hz], T.pd[:], ["pd"], ["H%d" % t])
-        ts(T.pe[:], T.pa[:], T.pc[:], None, A.is_equal, None, ["pa", "pc"], ["pe"])
+        if t == 0 or not early:
+            mask0(slice(0, 512))
         tt(T.Mk0[:], T.K[:, 0:512], T.pe[:], A.mult, ["Ka", "pe"], ["Mk0"])
         wrap(0)
         ts(T.m1[:], T.pb[:], T.pc[:], None, A.is_equal, None, ["pb", "pc"], ["m1"])
@@ -336,6 +348,8 @@ def rank_program(g, core, T, topo):
         tt(T.Aa[:], T.pa[:], T.m2[:], A.mult, ["pa", "m2"], ["Aa"])
         cut(2)
         act(T.C3[:], T.M[:, 0:2048].indirect(T.off[:, 64:96]), MALL + ["off2", "w6"], ["C3"], bias=col(6))
+        act(T.D[:, 0:512], T.NUM[:].indirect(T.off[:, 64:96]), ["NUM", "off2"], ["D0"])
+        cp(T.offD[:], T.vi[:, 65:96:2], ["vi2"], ["offD"])
         tt(T.q2[:], T.key[:, 64:96], T.vi[:, 64:96], A.subtract, ["key2", "vi2"], ["q2"])
         tt(T.ne[:], T.pg[:, 0:64], T.q01[:], A.not_equal, ["pg", "q01"], ["ne"])
         tt(T.Bb[:], T.K[:, 0:2048].indirect(T.off[:, 64:96]), T.nm2[:], A.mult, KALL + ["off2", "nm2"], ["Bb"])
@@ -353,10 +367,10 @@ def rank_program(g, core, T, topo):
         ts(T.big[:], T.ay[:], 4095.5, 4096.0, A.is_ge, A.mult, ["ay"], ["big"])
         cp(T.zoff[:], T.zf[:], ["zf"], ["zoff"])
         tt(T.Wd[:], T.vi[:, 64:96], T.big[:], A.add, ["vi2", "big"], ["Wd"])
-        ts(T.offD[:, 0:32], T.Wd[:], 2048.0, None, A.min, None, ["Wd"], ["offD"])
-        ts(T.offD[:, 32:48], T.Wd[:, 1:32:2], 2048.0, None, A.min, None, ["Wd"], ["offD"])
+        ts(T.offN[:], T.ay[:], 4095.5, 2.0 * t, A.is_ge, A.add, ["ay"], ["offN"])
+        act(T.D[:, 512:768], T.NUM[:].indirect(T.offD[:]), ["NUM", "offD"], ["D1"])
         zo = T["zo%d" % t]
-        cp(zo[:], T.H[:, 0:hz.stop].indirect(T.zoff[:]), HALL + ["zoff"], ["zo%d" % t])
+        act(zo[:], T.H[:, 0:hz.stop].indirect(T.zoff[:]), HALL + ["zoff"], ["zo%d" % t])
         if t < VISITS - 1:
             rid, pid = topo.addr(nxt, core)
             add("g", lambda a=T["zi%d" % (t + 1)][:], b=zo[:], s=T.sem["arr%d" % (t + 1)]:
@@ -364,29 +378,31 @@ def rank_program(g, core, T, topo):
             sent += len(topo.engines(core, nxt))
         else:
             dma("y", T.yz[:], zo[:], ["zo%d" % t], [])
-        act(T.D[:, 512:768], T.NUM[:].indirect(T.offD[:, 32:48]), ["NUM", "offD"], ["D1"])
-        act(T.D[:, 0:512], T.NUM[:].indirect(T.offD[:, 0:32]), ["NUM", "offD"], ["D0"])
         act(T.S[:], T.pb[:], ["pb", "wt"], ["S"], bias=col(20 + t))
-        act(T.NM[:], T.D[:, 0:512], ["D0", "RM", "wn"], ["NM"], func=F.Relu, scale=rm(t), bias=col(24 + t))
-        tt(T.E[:, 512:768], T.Wd[:].indirect(T.FL[:, 32:48]), T.D[:, 512:768], A.is_equal, ["Wd", "FL", "D1"], ["E1"])
+        act(T.NM[:], T.NT[:].indirect(T.offN[:]), ["NT", "offN"], ["NM"])
         tt(T.E[:, 0:512], T.Wd[:].indirect(T.FL[:, 0:32]), T.D[:, 0:512], A.is_equal, ["Wd", "FL", "D0"], ["E0"])
+        tt(T.E[:, 512:768], T.Wd[:].indirect(T.FL[:, 32:48]), T.D[:, 512:768], A.is_equal, ["Wd", "FL", "D1"], ["E1"])
         mm(T.ph[:, 0:32], T.idf[:], T.Wd[:], True, False, ["idf", "Wd"], ["ph"])
-        for r in range(16):
-            mm(T.ph[:, 1:32:2], fw(5, r), T.E[:, 512 + r:768:16], False, False, ["FW5", "E1"], ["ph"])
         for r in range(1, 16):
-            mm(T.ph[:, 0:32], T.TR[:, 128 * r:128 * r + 128], T.E[:, r:512:16], False, r == 15, ["TR", "E0"], ["ph"])
-        for b, w in (("pa", 1), ("pcc", 0)):
+            mm(T.ph[:, 0:32], T.TR[:, 128 * r:128 * r + 128], T.E[:, r:512:16], False, False, ["TR", "E0"], ["ph"])
+        for r in range(16):
+            mm(T.ph[:, 1:32:2], fw(5, r), T.E[:, 512 + r:768:16], False, r == 15, ["FW5", "E1"], ["ph"])
+        for b, w in (("pg", 1), ("pw", 0)):
             mm(T[b][:], fw(4, t), T.C3[:], True, False, ["FW4", "C3"], [b])
             mm(T[b][:], T.IW[:, 128 * w:128 * w + 128], T.NM[:], False, True, ["IW%d" % w, "NM"], [b])
         tt(T.sf[:], T.ph[:, 0:32], T.own[:, 0:32], A.min, ["ph", "own"], ["sf"])
         cp(T.soff[:], T.sf[:], ["sf"], ["soff"])
+        if t < VISITS - 1:
+            head(t + 1)
         for c in range(15, -1, -1):
             u = slice(32 * c, 32 * c + 32)
             o = T.soff[:, 2 * c:2 * c + 2]
             tt(T.K[:].indirect(o), T.Aa[:, u], T.Bb[:, u], A.add, ["soff", "Aa", "Bb"], KALL)
             act(T.M[:].indirect(o), T.S[:, u], ["soff", "S"], MALL, func=F.Silu)
-        tt(T.K[:, 0:512], T.K[:, 0:512], T.pa[:], A.min, ["Ka", "pa"], ["Ka"])
-        tt(T.K[:, 0:512], T.K[:, 0:512], T.pcc[:], A.max, ["Ka", "pcc"], ["Ka"])
+            if early and t < VISITS - 1 and c < 4:
+                mask0(slice(128 * c, 128 * c + 128))
+        tt(T.K[:, 0:512], T.K[:, 0:512], T.pg[:], A.min, ["Ka", "pg"], ["Ka"])
+        tt(T.K[:, 0:512], T.K[:, 0:512], T.pw[:], A.max, ["Ka", "pw"], ["Ka"])
     for h in range(4):
         u = slice(512 * h, 512 * h + 512)
         act(T.Mb[:, u], T.M[:, u], MALL, ["Mb%d" % h])

@@ -10,13 +10,13 @@ SCRATCH = {
     "m1": ("sbuf", [128, 512], f32), "m2": ("sbuf", [128, 512], f32), "nm2": ("sbuf", [128, 512], f32),
     "Mk0": ("sbuf", [128, 512], f32), "Mk1": ("sbuf", [128, 512], f32), "Mk2": ("sbuf", [128, 512], f32),
     "Aa": ("sbuf", [128, 512], f32), "Bb": ("sbuf", [128, 512], f32), "S": ("sbuf", [128, 512], f32),
-    "D": ("sbuf", [128, 768], f32), "E": ("sbuf", [128, 768], bf), "NM": ("sbuf", [128, 512], bf),
+    "D": ("sbuf", [128, 512], f32), "E": ("sbuf", [128, 1280], bf), "NM": ("sbuf", [128, 512], bf),
     "C12": ("sbuf", [128, 1024], bf), "C3": ("sbuf", [128, 512], bf),
     "tmp": ("sbuf", [128, 64], f32), "key": ("sbuf", [128, 96], i32), "vi": ("sbuf", [128, 96], i32),
     "off": ("sbuf", [128, 96], u16), "q01": ("sbuf", [128, 64], f32), "q2": ("sbuf", [128, 32], f32),
     "ne": ("sbuf", [128, 64], bf), "ay": ("sbuf", [128, 32], f32), "zf": ("sbuf", [128, 32], f32),
     "zoff": ("sbuf", [128, 32], u16), "big": ("sbuf", [128, 32], f32), "Wd": ("sbuf", [128, 32], f32),
-    "offD": ("sbuf", [128, 16], u16), "sf": ("sbuf", [128, 32], f32), "soff": ("sbuf", [128, 32], u16),
+    "offD": ("sbuf", [128, 32], u16), "sf": ("sbuf", [128, 32], f32), "soff": ("sbuf", [128, 32], u16),
     "ip": ("sbuf", [128, 1], i32), "pm": ("sbuf", [128, 1], i32), "pf": ("sbuf", [128, 1], f32),
     "pc": ("sbuf", [128, 1], f32), "g16": ("sbuf", [128, 1], f32), "h8": ("sbuf", [128, 1], f32),
     "ix": ("sbuf", [128, 144], f32), "ib": ("sbuf", [128, 256], f32), "ih": ("sbuf", [128, 64], f32),
@@ -26,7 +26,7 @@ SCRATCH = {
     "idf": ("sbuf", [128, 128], f32), "idm": ("sbuf", [128, 128], f32), "IW": ("sbuf", [128, 256], bf),
     "F1": ("sbuf", [128, 144], bf), "Ff": ("sbuf", [128, 136], f32), "FW": ("sbuf", [128, 864], bf),
     "TR": ("sbuf", [128, 2048], bf), "Sel": ("sbuf", [128, 1536], bf), "Ssel": ("sbuf", [128, 128], bf),
-    "Con": ("sbuf", [128, 512], bf), "hm": ("sbuf", [128, 64], f32), "FL": ("sbuf", [128, 48], u16),
+    "Con": ("sbuf", [128, 512], bf), "hm": ("sbuf", [128, 64], f32), "FL": ("sbuf", [128, 80], u16),
     "eps": ("sbuf", [128, 32], bf), "ci": ("sbuf", [128, 128], i32), "cm": ("sbuf", [128, 128], f32),
     "WB": ("sbuf", [128, 16], f32), "NT": ("sbuf", [128, 8], f32), "offN": ("sbuf", [128, 32], u16),
     "fo": ("sbuf", [128, 128], u16), "t3": ("sbuf", [128, 512], f32), "ok_": ("sbuf", [128, 128], f32),
@@ -38,8 +38,8 @@ SCRATCH = {
 NDMA = 20
 SEMAPHORES = ["sv", "ss", "sp", "sg", "arr1", "arr2", "arr3", "snt"] + ["d%d" % k for k in range(NDMA)]
 BANKS = ("pa", "pb", "pcc", "pd", "pe", "pw", "pg", "ph")
-PIECES = ("FL", "TR", "Con", "Mp", "NT", "pe", "m1")
-EARLY = {True: False, False: False}
+PIECES = ("FL", "TR", "Con", "Mp", "NT", "Mk0", "soff", "offD")
+ORD = (0, 1, 3, 2)
 VISITS = 4
 
 
@@ -187,9 +187,9 @@ def rank_program(g, core, T, topo):
     def fw(k, r):
         return T.FW[:, 144 * k + 16 - r:144 * k + 144 - r]
 
-    KALL = ["Ka", "Kb", "Kc"]
+    KALL = ["Ka0", "Ka1", "Kb", "Kc"]
     dma("y", T.H[:, 2048:2560], T.zin[:], [], ["H0"])
-    dma("y", T.K[:, 0:512], T.nkey[:, 0:512], [], ["Ka"])
+    dma("y", T.K[:, 0:512], T.nkey[:, 0:512], [], ["Ka0", "Ka1"])
     dma("s", T.ci[:], T.cnt[:], [], ["ci"])
     dma("y", T.K[:, 512:1280], T.nkey[:, 512:1280], [], ["Kb"])
     dma("y", T.K[:, 1280:2048], T.nkey[:, 1280:2048], [], ["Kc"])
@@ -218,8 +218,8 @@ def rank_program(g, core, T, topo):
     ts(T.cm[:, 0:128], T.ci[:], 32.0, None, A.mult, None, ["ci"], ["cm0"])
     ts(T.BBf[:], T.ib[:, 0:128], T.g16[:], None, A.is_equal, None, ["ib", "g16"], ["BBf"])
     ts(T.LT[:], T.ix[:, 0:16], T.pc[:], 4096.0, A.is_gt, A.mult, ["ix", "pc"], ["LT"])
-    cp(T.FL[:, 0:32], T.ix[:, 0:32], ["ix"], ["FL"])
-    cp(T.FL[:, 32:48], T.ix[:, 0:32:2], ["ix"], ["FL"])
+    for j, k in enumerate(ORD + (0, 2, 0, 0, 1, 1)):
+        cp(T.FL[:, 8 * j:8 * j + 8], T.ix[:, k:32:4], ["ix"], ["FL"])
     add("v", lambda: V.memset(T.eps[:], 2.0 ** -9), [], ["eps"])
     for b in range(16):
         act(T.M[:, 128 * b:128 * b + 128], T.ix[:, 0:128], ["ix", "w14", "WB"], ["Mp"], func=F.Silu, scale=col(14),
@@ -256,7 +256,7 @@ def rank_program(g, core, T, topo):
             act(T.Con[:, 128 * b:128 * b + 128], T.ix[:, 0:128], ["ix", "w7", "wb"], ["Con"], scale=col(7),
                 bias=col(16 + b))
         act(T.FW[:, 720:864], T.F1[:], ["F1"], ["FW5"], scale=4096.0)
-        for r in range(1, 6):
+        for r in range(0, 6):
             tri(r)
 
     def tri(r):
@@ -301,11 +301,8 @@ def rank_program(g, core, T, topo):
         if t > 0:
             mm(T.pd[:], T.II[:, 128 - 16 * t:256 - 16 * t], z, True, True, ["II0", "II1", zr], ["pd"])
 
-    def mask0(u):
-        ts(T.pe[:, u], T.pa[:, u], T.pc[:], None, A.is_equal, None, ["pa", "pc"], ["pe"])
-
     sent = 0
-    early = EARLY[n_in == len(topo.engines(nxt, core))]
+    HALF = (slice(0, 256), slice(256, 512))
     for t in range(VISITS):
         hz = slice(2048 + 512 * t, 2560 + 512 * t)
         HALL = ["Hx"] + ["H%d" % k for k in range(t + 1)]
@@ -313,9 +310,11 @@ def rank_program(g, core, T, topo):
             head(0)
         else:
             act(T.H[:, hz], T.pd[:], ["pd"], ["H%d" % t])
-        if t == 0 or not early:
-            mask0(slice(0, 512))
-        tt(T.Mk0[:], T.K[:, 0:512], T.pe[:], A.mult, ["Ka", "pe"], ["Mk0"])
+        for h, u in enumerate(HALF):
+            ts(T.pe[:, u], T.pa[:, u], T.pc[:], None, A.is_equal, None, ["pa", "pc"] + (["pe"] if h == 0 else []),
+               ["e%d" % h])
+        for h, u in enumerate(HALF):
+            tt(T.Mk0[:, u], T.K[:, u], T.pe[:, u], A.mult, ["Ka%d" % h, "e%d" % h, "pe"], ["Mk0"])
         wrap(0)
         ts(T.m1[:], T.pb[:], T.pc[:], None, A.is_equal, None, ["pb", "pc"], ["m1"])
         if t == 0:
@@ -348,8 +347,9 @@ def rank_program(g, core, T, topo):
         tt(T.Aa[:], T.pa[:], T.m2[:], A.mult, ["pa", "m2"], ["Aa"])
         cut(2)
         act(T.C3[:], T.M[:, 0:2048].indirect(T.off[:, 64:96]), MALL + ["off2", "w6"], ["C3"], bias=col(6))
-        act(T.D[:, 0:512], T.NUM[:].indirect(T.off[:, 64:96]), ["NUM", "off2"], ["D0"])
-        cp(T.offD[:], T.vi[:, 65:96:2], ["vi2"], ["offD"])
+        for j, k in enumerate(ORD):
+            cp(T.offD[:, 8 * j:8 * j + 8], T.vi[:, 64 + k:96:4], ["vi2"], ["offD"])
+        act(T.D[:], T.NUM[:].indirect(T.offD[:]), ["NUM", "offD"], ["D0"])
         tt(T.q2[:], T.key[:, 64:96], T.vi[:, 64:96], A.subtract, ["key2", "vi2"], ["q2"])
         tt(T.ne[:], T.pg[:, 0:64], T.q01[:], A.not_equal, ["pg", "q01"], ["ne"])
         tt(T.Bb[:], T.K[:, 0:2048].indirect(T.off[:, 64:96]), T.nm2[:], A.mult, KALL + ["off2", "nm2"], ["Bb"])
@@ -368,7 +368,6 @@ def rank_program(g, core, T, topo):
         cp(T.zoff[:], T.zf[:], ["zf"], ["zoff"])
         tt(T.Wd[:], T.vi[:, 64:96], T.big[:], A.add, ["vi2", "big"], ["Wd"])
         ts(T.offN[:], T.ay[:], 4095.5, 2.0 * t, A.is_ge, A.add, ["ay"], ["offN"])
-        act(T.D[:, 512:768], T.NUM[:].indirect(T.offD[:]), ["NUM", "offD"], ["D1"])
         zo = T["zo%d" % t]
         act(zo[:], T.H[:, 0:hz.stop].indirect(T.zoff[:]), HALL + ["zoff"], ["zo%d" % t])
         if t < VISITS - 1:
@@ -380,54 +379,73 @@ def rank_program(g, core, T, topo):
             dma("y", T.yz[:], zo[:], ["zo%d" % t], [])
         act(T.S[:], T.pb[:], ["pb", "wt"], ["S"], bias=col(20 + t))
         act(T.NM[:], T.NT[:].indirect(T.offN[:]), ["NT", "offN"], ["NM"])
+        for k, a in ((1, 8), (2, 16), (3, 16)):
+            tt(T.E[:, 256 + 256 * k:512 + 256 * k], T.Wd[:].indirect(T.FL[:, 16 + 16 * k:32 + 16 * k]),
+               T.D[:, 16 * a:16 * a + 256], A.is_equal, ["Wd", "FL", "D0"], ["E%d" % k])
         tt(T.E[:, 0:512], T.Wd[:].indirect(T.FL[:, 0:32]), T.D[:, 0:512], A.is_equal, ["Wd", "FL", "D0"], ["E0"])
-        tt(T.E[:, 512:768], T.Wd[:].indirect(T.FL[:, 32:48]), T.D[:, 512:768], A.is_equal, ["Wd", "FL", "D1"], ["E1"])
-        mm(T.ph[:, 0:32], T.idf[:], T.Wd[:], True, False, ["idf", "Wd"], ["ph"])
+        mm(T.ph[:, 0:32], T.TR[:, 0:128], T.eps[:], True, False, ["TR", "eps"], ["ph"])
+        for j, k in enumerate(ORD):
+            mm(T.ph[:, 8 * j:8 * j + 8], T.idf[:], T.Wd[:, k:32:4], False, False, ["idf", "Wd"], ["ph"])
+        for k, a in ((1, 8), (2, 16), (3, 16)):
+            for r in range(16):
+                mm(T.ph[:, a:a + 16], fw(5, r), T.E[:, 256 + 256 * k + r:512 + 256 * k:16], False, False,
+                   ["FW5", "E%d" % k], ["ph"])
         for r in range(1, 16):
-            mm(T.ph[:, 0:32], T.TR[:, 128 * r:128 * r + 128], T.E[:, r:512:16], False, False, ["TR", "E0"], ["ph"])
-        for r in range(16):
-            mm(T.ph[:, 1:32:2], fw(5, r), T.E[:, 512 + r:768:16], False, r == 15, ["FW5", "E1"], ["ph"])
+            mm(T.ph[:, 0:32], T.TR[:, 128 * r:128 * r + 128], T.E[:, r:512:16], False, r == 15, ["TR", "E0"], ["ph"])
         for b, w in (("pg", 1), ("pw", 0)):
             mm(T[b][:], fw(4, t), T.C3[:], True, False, ["FW4", "C3"], [b])
             mm(T[b][:], T.IW[:, 128 * w:128 * w + 128], T.NM[:], False, True, ["IW%d" % w, "NM"], [b])
-        tt(T.sf[:], T.ph[:, 0:32], T.own[:, 0:32], A.min, ["ph", "own"], ["sf"])
-        cp(T.soff[:], T.sf[:], ["sf"], ["soff"])
+        for j, k in enumerate(ORD):
+            ts(T.soff[:, k:32:4], T.ph[:, 8 * j:8 * j + 8], T.own[:, k:k + 1], None, A.min, None, ["ph", "own"],
+               ["soff"])
         if t < VISITS - 1:
             head(t + 1)
-        for c in range(15, -1, -1):
-            u = slice(32 * c, 32 * c + 32)
-            o = T.soff[:, 2 * c:2 * c + 2]
+        for c in range(7, -1, -1):
+            u = slice(64 * c, 64 * c + 64)
+            o = T.soff[:, 4 * c:4 * c + 4]
             tt(T.K[:].indirect(o), T.Aa[:, u], T.Bb[:, u], A.add, ["soff", "Aa", "Bb"], KALL)
             act(T.M[:].indirect(o), T.S[:, u], ["soff", "S"], MALL, func=F.Silu)
-            if early and t < VISITS - 1 and c < 4:
-                mask0(slice(128 * c, 128 * c + 128))
-        tt(T.K[:, 0:512], T.K[:, 0:512], T.pg[:], A.min, ["Ka", "pg"], ["Ka"])
-        tt(T.K[:, 0:512], T.K[:, 0:512], T.pw[:], A.max, ["Ka", "pw"], ["Ka"])
-    for h in range(4):
-        u = slice(512 * h, 512 * h + 512)
-        act(T.Mb[:, u], T.M[:, u], MALL, ["Mb%d" % h])
-    for b in range(16):
-        mm(T.pd[:, 0:128], fw(0, b), T.Mb[:, 128 * b:128 * b + 128], b == 0, b == 15, ["FW0", "Mb%d" % (b // 4)], ["pd"])
-    for b in range(16):
-        mm(T.pb[:, 0:128], fw(3, b), T.Mb[:, 128 * b:128 * b + 128], b == 0, b == 15, ["FW3", "Mb%d" % (b // 4)], ["pb"])
-    tt(T.pe[:], T.K[:, 0:512], T.K[:, 512:1024], A.add, KALL, ["pe"])
+        for b, op in (("pg", A.min), ("pw", A.max)):
+            for h, u in enumerate(HALF):
+                tt(T.K[:, u], T.K[:, u], T[b][:, u], op, ["Ka%d" % h, b], ["Ka%d" % h])
+            if t == VISITS - 1 and b == "pg":
+                cp(T.Mb[:, 1536:2048], T.M[:, 1536:2048], MALL, ["Mb3"])
+                for h in range(3):
+                    u = slice(512 * h, 512 * h + 512)
+                    act(T.Mb[:, u], T.M[:, u], MALL, ["Mb%d" % h])
+                for b2 in range(8, 12):
+                    mm(T.pa[:, 0:128], T.idf[:], T.K[:, 128 * b2:128 * b2 + 128], b2 == 8, False, ["idf", "Kb", "Kc"],
+                       ["pa"])
+                order = [0, 1, 2, 3, 12, 13, 14, 15, 4, 5, 6, 7, 8, 9, 10, 11]
+                for b2 in order:
+                    mm(T.pd[:, 0:128], fw(0, b2), T.Mb[:, 128 * b2:128 * b2 + 128], b2 == 0, b2 == 11,
+                       ["FW0", "Mb%d" % (b2 // 4)], ["pd"])
     cp(T.fo[:], T.pd[:, 0:128], ["pd"], ["fo"])
     HALL = ["Hx", "H0", "H1", "H2", "H3"]
-    act(T.G[:, 0:1024], T.H[:].indirect(T.fo[:, 0:64]), HALL + ["fo"], ["G0"])
-    act(T.oc[:], T.pb[:, 0:128], ["pb"], ["oc"])
-    dma("s", T.yc[:], T.oc[:], ["oc"], [])
-    cp(T.G[:, 1024:2048], T.H[:].indirect(T.fo[:, 64:128]), HALL + ["fo"], ["G1"])
-    tt(T.pg[:], T.pe[:], T.K[:, 1024:1536], A.add, KALL + ["pe"], ["pg"])
-    tt(T.t3[:], T.pg[:], T.K[:, 1536:2048], A.add, KALL + ["pg"], ["t3"])
-    tt(T.pe[:, 0:128], T.t3[:, 0:128], T.t3[:, 128:256], A.add, ["t3"], ["pe"])
-    tt(T.pg[:, 0:128], T.pe[:, 0:128], T.t3[:, 256:384], A.add, ["t3", "pe"], ["pg"])
-    tt(T.ok_[:], T.pg[:, 0:128], T.t3[:, 384:512], A.add, ["t3", "pg"], ["ok_"])
+    GS = ((0, 48, "s"), (48, 96, "s"), (96, 128, "v"))
+    for k, (a, b, e) in enumerate(GS):
+        (act if e == "s" else cp)(T.G[:, 16 * a:16 * b], T.H[:].indirect(T.fo[:, a:b]), HALL + ["fo"], ["G%d" % k])
+    for b in range(12, 16):
+        mm(T.pa[:, 0:128], T.idf[:], T.K[:, 128 * b:128 * b + 128], False, b == 15, ["idf", "Kb", "Kc"], ["pa"])
+    for b in range(16):
+        mm(T.pb[:, 0:128], fw(3, b), T.Mb[:, 128 * b:128 * b + 128], b == 0, b == 15, ["FW3", "Mb%d" % (b // 4)], ["pb"])
+    for h, u in enumerate(HALF):
+        tt(T.t3[:, u], T.K[:, u], T.K[:, 512 + u.start:512 + u.stop], A.add, KALL, ["t3%d" % h])
+    cp(T.oc[:], T.pb[:, 0:128], ["pb"], ["oc"])
+    dma("y", T.yc[:], T.oc[:], ["oc"], [])
+    tt(T.pe[:, 0:128], T.pa[:, 0:128], T.t3[:, 0:128], A.add, ["pa", "t30", "e0", "e1"], ["pe"])
+    tt(T.Aa[:, 0:128], T.t3[:, 256:384], T.t3[:, 384:512], A.add, ["t31"], ["Aa"])
+    tt(T.pg[:, 0:128], T.pe[:, 0:128], T.t3[:, 128:256], A.add, ["pe", "t30"], ["pg"])
+    tt(T.ok_[:], T.pg[:, 0:128], T.Aa[:, 0:128], A.add, ["pg", "Aa"], ["ok_"])
     dma("y", T.yk[:], T.ok_[:], ["ok_"], [])
-    for h, b in enumerate(("pw", "ph")):
+    for k, bank in ((0, "pcc"), (2, "ph"), (1, "pd")):
+        a, b, e = GS[k]
         for r in range(16):
-            mm(T[b][:, 0:64], T.II[:, 0:128], T.G[:, 1024 * h + r:1024 * h + 1024:16], r == 0, r == 15,
-               ["II0", "G%d" % h], [b])
-        act(T.ox[:, 64 * h:64 * h + 64], T[b][:, 0:64], [b], ["ox%d" % h])
-    dma("s", T.yx[:], T.ox[:], ["ox0", "ox1"], [])
+            mm(T[bank][:, 0:b - a], T.II[:, 0:128], T.G[:, 16 * a + r:16 * b:16], r == 0, r == 15,
+               ["II0", "G%d" % k], [bank])
+    for k, bank in ((0, "pcc"), (2, "ph"), (1, "pd")):
+        a, b, e = GS[k]
+        act(T.ox[:, a:b], T[bank][:, 0:b - a], [bank], ["ox%d" % k])
+    dma("s", T.yx[:], T.ox[:], ["ox0", "ox1", "ox2"], [])
     emit(g, T, ops)
     g.wait_ge(T.sem.snt, sent)

@@ -1,46 +1,60 @@
 from concourse.mybir import AluOpType as A, ActivationFunctionType as F
 
-f32, bf, i32, u16 = "float32", "bfloat16", "int32", "uint16"
+f32, bf, f16, i32, u16 = "float32", "bfloat16", "float16", "int32", "uint16"
 SCRATCH = {
+    "Kr": ("sbuf", [128, 2048], f32), "cf": ("sbuf", [128, 2048], f16),
     "K": ("sbuf", [128, 2560], f32), "H": ("sbuf", [128, 4096], bf), "M": ("sbuf", [128, 2560], f32),
-    "NUM": ("sbuf", [128, 2064], f32), "Mb": ("sbuf", [128, 2048], bf), "G": ("sbuf", [128, 2048], bf),
+    "Mb": ("sbuf", [128, 2048], bf), "G": ("sbuf", [128, 2048], bf),
     "zi1": ("sbuf", [128, 512], bf), "zi2": ("sbuf", [128, 512], bf), "zi3": ("sbuf", [128, 512], bf),
     "zo0": ("sbuf", [128, 512], bf), "zo1": ("sbuf", [128, 512], bf), "zo2": ("sbuf", [128, 512], bf),
     "zo3": ("sbuf", [128, 512], bf),
+    "xi0": ("sbuf", [128, 64], u16), "xi1": ("sbuf", [128, 64], u16), "xi2": ("sbuf", [128, 64], u16),
+    "xi3": ("sbuf", [128, 64], u16),
+    "xo1": ("sbuf", [128, 64], u16), "xo2": ("sbuf", [128, 64], u16), "xo3": ("sbuf", [128, 64], u16),
     "m1": ("sbuf", [128, 512], f32), "m2": ("sbuf", [128, 512], f32), "nm2": ("sbuf", [128, 512], f32),
-    "Mk0": ("sbuf", [128, 512], f32), "Mk1": ("sbuf", [128, 512], f32), "Mk2": ("sbuf", [128, 512], f32),
+    "Kh0": ("sbuf", [128, 512], f16), "Kh1": ("sbuf", [128, 512], f16), "Kh2": ("sbuf", [128, 512], f16),
+    "Kf0": ("sbuf", [128, 512], f32), "Kf1": ("sbuf", [128, 512], f32), "Kf2": ("sbuf", [128, 512], f32),
+    "C0": ("sbuf", [128, 512], bf), "C1": ("sbuf", [128, 512], bf), "C2": ("sbuf", [128, 512], bf),
     "Aa": ("sbuf", [128, 512], f32), "Bb": ("sbuf", [128, 512], f32), "S": ("sbuf", [128, 512], f32),
-    "D": ("sbuf", [128, 512], f32), "E": ("sbuf", [128, 1280], bf), "NM": ("sbuf", [128, 512], bf),
-    "C12": ("sbuf", [128, 1024], bf), "C3": ("sbuf", [128, 512], bf),
-    "tmp": ("sbuf", [128, 64], f32), "key": ("sbuf", [128, 96], i32), "vi": ("sbuf", [128, 96], i32),
-    "off": ("sbuf", [128, 96], u16), "q01": ("sbuf", [128, 64], f32), "q2": ("sbuf", [128, 32], f32),
-    "ne": ("sbuf", [128, 64], bf), "ay": ("sbuf", [128, 32], f32), "zf": ("sbuf", [128, 32], f32),
-    "zoff": ("sbuf", [128, 32], u16), "big": ("sbuf", [128, 32], f32), "Wd": ("sbuf", [128, 32], f32),
-    "offD": ("sbuf", [128, 32], u16), "sf": ("sbuf", [128, 32], f32), "soff": ("sbuf", [128, 32], u16),
+    "Wb": ("sbuf", [128, 512], f32), "E": ("sbuf", [128, 2048], bf), "NM": ("sbuf", [128, 512], bf),
+    "off": ("sbuf", [128, 96], u16), "Wd": ("sbuf", [128, 32], f32), "cw": ("sbuf", [128, 32], f32),
+    "zf": ("sbuf", [128, 32], f32), "zoff": ("sbuf", [128, 32], u16), "offN": ("sbuf", [128, 32], u16),
+    "sf": ("sbuf", [128, 32], f32), "soff": ("sbuf", [128, 32], u16), "FL": ("sbuf", [128, 32], u16),
     "ip": ("sbuf", [128, 1], i32), "pm": ("sbuf", [128, 1], i32), "pf": ("sbuf", [128, 1], f32),
-    "pc": ("sbuf", [128, 1], f32), "g16": ("sbuf", [128, 1], f32), "h8": ("sbuf", [128, 1], f32),
-    "ix": ("sbuf", [128, 144], f32), "ib": ("sbuf", [128, 256], f32), "ih": ("sbuf", [128, 64], f32),
-    "iw": ("sbuf", [128, 128], f32), "own": ("sbuf", [128, 128], f32),
-    "RM": ("sbuf", [128, 16], f32), "LT": ("sbuf", [128, 16], f32), "WC": ("sbuf", [128, 32], f32),
-    "BB": ("sbuf", [128, 256], bf), "BBf": ("sbuf", [128, 128], f32), "II": ("sbuf", [128, 256], bf),
-    "idf": ("sbuf", [128, 128], f32), "idm": ("sbuf", [128, 128], f32), "IW": ("sbuf", [128, 256], bf),
-    "F1": ("sbuf", [128, 144], bf), "Ff": ("sbuf", [128, 136], f32), "FW": ("sbuf", [128, 864], bf),
-    "TR": ("sbuf", [128, 2048], bf), "Sel": ("sbuf", [128, 1536], bf), "Ssel": ("sbuf", [128, 128], bf),
-    "Con": ("sbuf", [128, 512], bf), "hm": ("sbuf", [128, 64], f32), "FL": ("sbuf", [128, 80], u16),
-    "eps": ("sbuf", [128, 32], bf), "ci": ("sbuf", [128, 128], i32), "cm": ("sbuf", [128, 128], f32),
-    "WB": ("sbuf", [128, 16], f32), "NT": ("sbuf", [128, 8], f32), "offN": ("sbuf", [128, 32], u16),
-    "fo": ("sbuf", [128, 128], u16), "t3": ("sbuf", [128, 512], f32), "ok_": ("sbuf", [128, 128], f32),
+    "pc": ("sbuf", [128, 1], f32), "g16": ("sbuf", [128, 1], f32),
+    "ix": ("sbuf", [128, 256], f32), "ib": ("sbuf", [128, 128], f32), "ilo": ("sbuf", [128, 256], f32),
+    "ihi": ("sbuf", [128, 256], f32), "iw": ("sbuf", [128, 128], f32), "own": ("sbuf", [128, 128], f32),
+    "RM": ("sbuf", [128, 16], f32), "LT": ("sbuf", [128, 16], f32), "WC": ("sbuf", [128, 40], f32),
+    "T0": ("sbuf", [128, 256], bf), "T1": ("sbuf", [128, 256], bf), "F2": ("sbuf", [128, 256], bf),
+    "F1": ("sbuf", [128, 144], bf), "nil": ("sbuf", [128, 128], f32),
+    "BB": ("sbuf", [128, 128], bf), "BF": ("sbuf", [128, 384], f32), "CW": ("sbuf", [128, 512], bf),
+    "idf": ("sbuf", [128, 128], f32), "ID": ("sbuf", [128, 896], bf), "XW": ("sbuf", [128, 1152], bf),
+    "FW": ("sbuf", [128, 576], bf), "TR": ("sbuf", [128, 2048], bf), "Ssel": ("sbuf", [128, 128], bf),
+    "Con": ("sbuf", [128, 512], bf), "one": ("sbuf", [128, 512], bf),
+    "ci": ("sbuf", [128, 128], i32), "cm": ("sbuf", [128, 128], f32),
+    "WB": ("sbuf", [128, 8], f32), "NT": ("sbuf", [128, 8], f32),
+    "fo": ("sbuf", [128, 128], u16), "ok_": ("sbuf", [128, 128], f32),
     "ox": ("sbuf", [128, 128], bf), "oc": ("sbuf", [128, 128], f32),
-    "pa": ("psum", [128, 512], f32), "pb": ("psum", [128, 512], f32), "pcc": ("psum", [128, 512], f32),
-    "pd": ("psum", [128, 512], f32), "pe": ("psum", [128, 512], f32), "pw": ("psum", [128, 512], f32),
-    "pg": ("psum", [128, 512], f32), "ph": ("psum", [128, 512], f32),
+    "pw": ("psum", [128, 512], f32), "pz": ("psum", [128, 512], f32), "pY": ("psum", [128, 512], f32),
+    "pk": ("psum", [128, 512], f32), "ph": ("psum", [128, 512], f32), "pb": ("psum", [128, 512], f32),
+    "pU": ("psum", [128, 512], f32), "pL": ("psum", [128, 512], f32),
 }
-NDMA = 20
-SEMAPHORES = ["sv", "ss", "sp", "sg", "arr1", "arr2", "arr3", "snt"] + ["d%d" % k for k in range(NDMA)]
-BANKS = ("pa", "pb", "pcc", "pd", "pe", "pw", "pg", "ph")
-PIECES = ("FL", "TR", "Con", "Mp", "NT", "Mk0", "soff", "offD")
-ORD = (0, 1, 3, 2)
+NDMA = 24
+SEMAPHORES = (["sv", "ss", "sp", "sg", "snt"] + ["ax%d" % t for t in (1, 2, 3)] + ["az%d" % t for t in (1, 2, 3)]
+              + ["d%d" % k for k in range(NDMA)])
+BANKS = ("pw", "pz", "pY", "pk", "ph", "pb", "pU", "pL")
 VISITS = 4
+NB = 4
+ROUND = 1.5 * 2.0 ** 23
+W0, W1 = 2.0 ** 35, 2.0 ** 25
+DIAG = {0: 1.0, 1: -2048.0, 2: 2048.0, 3: 2.0 ** -11, 4: 4096.0, 5: 2.0 ** 22, 6: -2.0 ** 22}
+COLS = {
+    "hcol": {1: 1 / 32, 2: 8.0},
+    "key": {0: 2.0 ** -16, 3: 1 / 32, 4: 8.0},
+    "last": {0: -2.0 ** -16, 5: 4096.0, 6: 2.0 ** -11},
+    "step": {0: 32.0, 5: 1.0, 6: 1.0},
+    "keep": {0: 1.0, 3: 1.0, 4: 1.0},
+}
 
 
 def route(T, topo, r):
@@ -54,7 +68,7 @@ def route(T, topo, r):
 
 def emit(g, T, ops):
     q = {"v": g.vector, "s": g.scalar, "p": g.tensor, "g": g, "y": g.sync}
-    writer, readers, before, known = {}, {}, {}, {e: {} for e in q}
+    writer, readers, known = {}, {}, {e: {} for e in q}
     count = {e: 0 for e in q}
     ndma = [0]
     for o in ops:
@@ -65,12 +79,7 @@ def emit(g, T, ops):
             if r in BANKS:
                 deps += [x for x in readers.get(r, []) if x["e"] != e]
         for w in o["w"]:
-            if w in PIECES and not readers.get(w):
-                deps += before.get(w, [])
-                continue
-            old = writer.get(w, []) + readers.get(w, [])
-            before[w] = old
-            deps += [x for x in old if x["e"] != "p" or e != "p"]
+            deps += [x for x in writer.get(w, []) + readers.get(w, []) if x["e"] != "p" or e != "p"]
         waits = []
         if o["kind"] != "x":
             kn = known[e]
@@ -99,8 +108,7 @@ def emit(g, T, ops):
         for r in o["r"]:
             readers.setdefault(r, []).append(o)
         for w in o["w"]:
-            keep = writer.get(w, []) if w in PIECES and not readers.get(w) else []
-            writer[w] = keep + [o]
+            writer[w] = [o]
             readers[w] = []
     run = {e: 0 for e in q}
     for o in ops:
@@ -135,10 +143,10 @@ def rank_program(g, core, T, topo):
             if len(way) == 3 and way[1] == core:
                 rid, pid = topo.addr(way[2], core)
                 for t in range(1, VISITS):
-                    g.wait_ge(T.sem["arr%d" % t], len(topo.engines(way[0], core)))
-                    g.remote_dma(T["zi%d" % t][:], T["zi%d" % t][:], T.sem["arr%d" % t], T.sem.snt, pid, rid,
-                                 topo.mask(core, way[2]))
-                g.wait_ge(T.sem.snt, (VISITS - 1) * len(topo.engines(core, way[2])))
+                    for buf, sem in (("xi%d" % t, "ax%d" % t), ("zi%d" % t, "az%d" % t)):
+                        g.wait_ge(T.sem[sem], len(topo.engines(way[0], core)))
+                        g.remote_dma(T[buf][:], T[buf][:], T.sem[sem], T.sem.snt, pid, rid, topo.mask(core, way[2]))
+                g.wait_ge(T.sem.snt, 2 * (VISITS - 1) * len(topo.engines(core, way[2])))
         return
     nxt = route(T, topo, rank)[1]
     n_in = len(topo.engines(route(T, topo, (rank - 1) % n)[-2], core))
@@ -165,6 +173,12 @@ def rank_program(g, core, T, topo):
     def act(out, a, r, w, func=F.Identity, **kw):
         add("s", lambda: S.activation(out, a, func, **kw), r, w)
 
+    def scaled(e, out, a, c, r, w):
+        if e == "v":
+            ts(out, a, c, None, A.mult, None, r, w)
+        else:
+            act(out, a, r, w, scale=c)
+
     def mm(out, l, rhs, st, sp, r, w):
         add("p", lambda: P.matmul(out, l, rhs, st, sp), r, w)
 
@@ -174,9 +188,16 @@ def rank_program(g, core, T, topo):
         else:
             add("g", lambda: g.iota(out, pat, base, cm), [], w)
 
+    def diag(out, c, w):
+        add("g", lambda: g.affine_select(out, T.nil[:], [[-1, 128]], A.not_equal, c, 0, 1), ["nil"], [w])
+
     def dma(e, out, in_, r, w):
         qq = g.sync if e == "y" else g.scalar
         add(e, lambda: qq.dma_start(out, in_), r, w, kind="d")
+
+    def send(dst, src, sem, r):
+        rid, pid = topo.addr(nxt, core)
+        add("g", lambda: g.remote_dma(dst, src, T.sem[sem], T.sem.snt, pid, rid, topo.mask(core, nxt)), r, [], kind="r")
 
     def col(k):
         return T.WC[:, k:k + 1]
@@ -184,267 +205,307 @@ def rank_program(g, core, T, topo):
     def rm(k):
         return T.RM[:, k:k + 1]
 
-    def fw(k, r):
-        return T.FW[:, 144 * k + 16 - r:144 * k + 144 - r]
+    def wcol(name):
+        return col(list(COLS).index(name))
 
-    KALL = ["Ka0", "Ka1", "Kb", "Kc"]
-    dma("y", T.H[:, 2048:2560], T.zin[:], [], ["H0"])
-    dma("y", T.K[:, 0:512], T.nkey[:, 0:512], [], ["Ka0", "Ka1"])
+    def weights(e, name):
+        for j, (row, c) in enumerate(COLS[name].items()):
+            if j == 0:
+                scaled(e, wcol(name), rm(row), c, ["RM"], [name])
+            elif e == "v":
+                ts(wcol(name), rm(row), c, wcol(name), A.mult, A.add, ["RM", name], [name])
+            else:
+                act(wcol(name), rm(row), ["RM", name], [name], scale=c, bias=wcol(name))
+
+    def blk(buf, k):
+        return buf[:, 128 * k:128 * k + 128]
+
+    def wide(buf, k):
+        return buf[:, 144 * k:144 * k + 144]
+
+    def band(buf, k, r):
+        return buf[:, 144 * k + 16 - r:144 * k + 144 - r]
+
+    def to_w(out, buf, k, u, lo, hi, st, sp, r, w):
+        for j in range(16):
+            mm(out, band(buf, k, j), u[:, lo + j:hi:16], st and j == 0, sp and j == 15, r, w)
+
+    def xw(t, e):
+        for k, c in ((2 * t, col(36 + t)), (2 * t + 1, rm(3 * t + 2))):
+            scaled(e, wide(T.XW, k), T.F2[:, 112 - 16 * t:256 - 16 * t], c, ["F2a", "F2b", "w36", "RM"], ["XW%d" % k])
+
+    def slots(t, z, lo, zr):
+        for k in range(2):
+            to_w(T.pz[:, 64 + 32 * k:96 + 32 * k], T.XW, 2 * t + k, z, lo, lo + 512, True, True,
+                 ["XW%d" % (2 * t + k), zr], ["pz"])
+
+    def convert(k):
+        a, b, bank = PARTS[k]
+        u, out = slice(a, b), T[bank][:, 0:b - a]
+        mm(out, T.idf[:], T.Kr[:, u], False, False, ["idf", "Kr%d" % k], [bank])
+        ts(T.cf[:, u], T.Kr[:, u], 2.0 ** -11, 1279.5 + 2.0 ** -12, A.mult, A.add, ["Kr%d" % k], ["cf%d" % k])
+        mm(out, blk(T.ID, 1), T.cf[:, u], False, False, ["ID1", "cf%d" % k], [bank])
+        mm(out, blk(T.ID, 3), T.cf[:, u], False, True, ["ID3", "cf%d" % k], [bank])
+        act(T.K[:, u], out, [bank], ["K0a", "K0b"] if k == 0 else ["K%d" % k], bias=-0.625)
+
+    def tri(e, rs):
+        for r in rs:
+            scaled(e, blk(T.TR, r), blk(T.ID, 0), T.LT[:, r:r + 1], ["ID0", "LT"], ["TR%d" % r])
+
+    def masks(t, m):
+        xi, xr = T["xi%d" % t], "xi%d" % t
+        if m == 1:
+            act(T.m1[:], T.T1[:].indirect(xi[:, 0:32]), ["T1", xr], ["m1"])
+        else:
+            act(T.m2[:], T.RM[:].indirect(xi[:, 32:64]), ["RM", xr], ["m2"])
+
+    PARTS = ((0, 512, "pk"), (512, 1024, "ph"), (1024, 1536, "pU"), (1536, 1792, "pL"), (1792, 2048, "pb"))
+    KC = ["K0a", "K0b", "K1", "K2", "K3", "K4"]
+    IX = ["ix0", "ix1"]
     dma("s", T.ci[:], T.cnt[:], [], ["ci"])
-    dma("y", T.K[:, 512:1280], T.nkey[:, 512:1280], [], ["Kb"])
-    dma("y", T.K[:, 1280:2048], T.nkey[:, 1280:2048], [], ["Kc"])
+    dma("y", T.H[:, 2048:2560], T.zin[:], [], ["H0"])
+    for k, (a, b, bank) in enumerate(PARTS):
+        dma("y", T.Kr[:, a:b], T.nkey[:, a:b], [], ["Kr%d" % k])
+    add("v", lambda: V.memset(T.nil[:], 0.0), [], ["nil"])
     iota(T.ip[:], [[0, 1]], 0, 1, ["ip"], flag=False)
-    iota(T.ix[:], [[1, 144]], 0, 0, ["ix"])
-    iota(T.ib[:], [[0, 2], [16, 8], [0, 16]], 0, 0, ["ib"])
-    iota(T.ih[:], [[0, 32], [1, 2]], 0, 0, ["ih"])
+    iota(T.ix[:, 0:16], [[1, 16]], 0, 0, ["ix0"])
+    iota(T.ix[:, 16:256], [[1, 240]], 16, 0, ["ix1"])
+    iota(T.ilo[:], [[0, 16], [1, 16]], 0, 0, ["ilo"])
+    iota(T.ib[:], [[16, 8], [0, 16]], 0, 0, ["ib"])
+    diag(blk(T.ID, 2), DIAG[2], "ID2")
+    iota(T.ihi[:], [[1, 16], [0, 16]], 0, 0, ["ihi"])
+    diag(T.idf[:], 1.0, "idf")
+    for k in (1, 3, 0):
+        diag(blk(T.ID, k), DIAG[k], "ID%d" % k)
     iota(T.iw[:], [[16, 128]], 2048, 0, ["iw"])
-    iota(T.NUM[:], [[1, 2064]], 0, 0, ["NUM"])
+    for k in (4, 5, 6):
+        diag(blk(T.ID, k), DIAG[k], "ID%d" % k)
     ts(T.pm[:], T.ip[:], 15, None, A.bitwise_and, None, ["ip"], ["pm"])
     cp(T.pf[:], T.ip[:], ["ip"], ["pf"])
     cp(T.pc[:], T.pm[:], ["pm"], ["pc"])
+    ts(T.RM[:], T.ix[:, 0:16], T.pc[:], None, A.is_equal, None, ["ix0", "pc"], ["RM"])
     tt(T.g16[:], T.pf[:], T.pc[:], A.subtract, ["pf", "pc"], ["g16"])
-    ts(T.RM[:], T.ix[:, 0:16], T.pc[:], None, A.is_equal, None, ["ix", "pc"], ["RM"])
-    ts(T.F1[:], T.ix[:], -16.0, T.g16[:], A.add, A.is_equal, ["ix", "g16"], ["F1"])
     tt(T.WC[:, 28:30], T.RM[:, 1:3], T.RM[:, 3:5], A.add, ["RM"], ["w28"])
-    ts(T.h8[:], T.pc[:], 8.0, None, A.is_ge, None, ["pc"], ["h8"])
+    ts(T.WC[:, 32:36], T.RM[:, 1:12:3], 16.0, None, A.mult, None, ["RM"], ["w32"])
     ts(col(14), col(28), 32.0, None, A.mult, None, ["w28"], ["w14"])
-    ts(T.WB[:], T.ix[:, 0:16], col(29), 32.0, A.mult, A.mult, ["ix", "w28"], ["WB"])
-    ts(T.BB[:], T.ib[:], T.g16[:], None, A.is_equal, None, ["ib", "g16"], ["BB"])
-    tt(T.Ff[:], T.F1[:, 8:144], T.F1[:, 0:136], A.add, ["F1"], ["Ff"])
-    for m in range(3):
-        ts(T.Sel[:, 128 * m:128 * m + 128], T.BB[:, 128:256], rm(m), None, A.mult, None, ["BB", "RM"], ["Sel%d" % m])
-    ts(T.hm[:], T.ih[:], T.h8[:], None, A.is_equal, None, ["ih", "h8"], ["hm"])
-    ts(T.idf[:], T.ix[:, 0:128], T.pf[:], None, A.is_equal, None, ["ix", "pf"], ["idf"])
-    ts(T.cm[:, 0:128], T.ci[:], 32.0, None, A.mult, None, ["ci"], ["cm0"])
-    ts(T.BBf[:], T.ib[:, 0:128], T.g16[:], None, A.is_equal, None, ["ib", "g16"], ["BBf"])
-    ts(T.LT[:], T.ix[:, 0:16], T.pc[:], 4096.0, A.is_gt, A.mult, ["ix", "pc"], ["LT"])
-    for j, k in enumerate(ORD + (0, 2, 0, 0, 1, 1)):
-        cp(T.FL[:, 8 * j:8 * j + 8], T.ix[:, k:32:4], ["ix"], ["FL"])
-    add("v", lambda: V.memset(T.eps[:], 2.0 ** -9), [], ["eps"])
-    for b in range(16):
-        act(T.M[:, 128 * b:128 * b + 128], T.ix[:, 0:128], ["ix", "w14", "WB"], ["Mp"], func=F.Silu, scale=col(14),
+    ts(T.WB[:], T.ix[:, 0:8], col(29), 32.0, A.mult, A.mult, ["ix0", "w28"], ["WB"])
+    tt(T.WC[:, 36:40], T.WC[:, 32:36], T.RM[:, 0:12:3], A.add, ["w32", "RM"], ["w36"])
+    for b in range(8):
+        act(T.M[:, 256 * b:256 * b + 256], T.ix[:], IX + ["w14", "WB"], ["Mp%d" % b], func=F.Silu, scale=col(14),
             bias=T.WB[:, b:b + 1])
-    dma("y", T.M[0:128:16, 0:2048], T.cm[:], ["cm0", "Mp"], ["M"])
-    dma("y", T.H[:, 0:2048], T.xreg[:], [], ["Hx"])
-    act(col(10), rm(1), ["RM"], ["w10"], scale=1.0 / 32)
-    act(col(11), rm(3), ["RM"], ["w11"], scale=1.0 / 32)
-    act(col(2), rm(0), ["RM"], ["w2"], scale=64.0)
-    act(col(0), rm(2), ["RM", "w10"], ["w0"], scale=4.0, bias=col(10))
-    act(col(12), rm(4), ["RM", "w11"], ["w12"], scale=4.0, bias=col(11))
-    act(col(13), rm(3), ["RM"], ["w13"], bias=rm(4))
-    act(T.FW[:, 288:432], T.F1[:], ["F1", "w2"], ["FW2"], scale=col(2))
-    act(col(1), rm(0), ["RM", "w0"], ["w1"], scale=256.0, bias=col(0))
-    act(col(4), rm(0), ["RM", "w12"], ["w4"], scale=64.0, bias=col(12))
-    act(col(5), rm(0), ["RM", "w13"], ["w5"], bias=col(13))
-    act(col(3), rm(0), ["RM"], ["w3"], scale=1.0 / 32)
-    act(col(6), rm(0), ["RM"], ["w6"], scale=32.0)
-    act(col(7), rm(1), ["RM"], ["w7"], scale=32.0)
-    act(col(8), rm(2), ["RM"], ["w8"], scale=32.0)
-    act(T.NT[:, 0:8:2], T.RM[:, 0:4], ["RM"], ["NT"], scale=-1.0, bias=1.0)
-    act(T.NT[:, 1:8:2], T.RM[:, 0:4], ["RM"], ["NT"], scale=0.0, bias=1.0)
-    act(T.FW[:, 144:288], T.F1[:], ["F1", "w1"], ["FW1"], scale=col(1))
-    act(T.WC[:, 16:20], T.ix[:, 0:4], ["ix", "w8"], ["wb"], scale=col(8))
-    act(T.WC[:, 20:24], T.ix[:, 16:32:4], ["ix", "w8"], ["wt"], scale=col(8))
-    act(T.idm[:], T.idf[:], ["idf"], ["idm"], scale=-4.0)
-    act(T.IW[:, 0:128], T.idf[:], ["idf"], ["IW0"], scale=-2.0 ** 22)
-    act(T.II[:, 0:128], T.idf[:], ["idf"], ["II0"])
-    MALL = ["M"]
+    add("v", lambda: V.memset(T.one[:], 1280.0), [], ["one"])
+    for h in range(2):
+        ts(blk(T.F2, h), T.ix[:, 0:128], T.g16[:], None, A.is_equal, None, IX + ["g16"], ["F2" + "ab"[h]])
+    weights("v", "key")
+    xw(0, "v")
+    cp(T.F1[:], T.F2[:, 112:256], ["F2a", "F2b"], ["F1"])
+    ts(T.T0[:], T.ilo[:], T.pc[:], None, A.is_equal, None, ["ilo", "pc"], ["T0"])
+    ts(T.cm[:], T.ci[:], 32.0, None, A.mult, None, ["ci"], ["cm0"])
+    dma("s", T.M[0:128:16, 0:2048], T.cm[:], ["cm0"] + ["Mp%d" % b for b in range(8)], ["M"])
+    slots(0, T.H, 2048, "H0")
+    for a, b, bank in PARTS:
+        mm(T[bank][:, 0:b - a], blk(T.ID, 2), T.one[:, 0:b - a], True, False, ["ID2", "one"], [bank])
+    ts(T.BB[:], T.ib[:], T.g16[:], None, A.is_equal, None, ["ib", "g16"], ["BB"])
+    for k, c in enumerate((W0, W1, 1.0)):
+        ts(blk(T.BF, k), T.ib[:], T.g16[:], c, A.is_equal, A.mult, ["ib", "g16"], ["BF%d" % k])
+    ts(T.T1[:], T.ihi[:], T.pc[:], None, A.is_equal, None, ["ihi", "pc"], ["T1"])
+    for k, c in enumerate((-W0, -W1)):
+        ts(blk(T.CW, k), T.BB[:], wcol("key"), c, A.mult, A.mult, ["BB", "key"], ["CW%d" % k])
+    cp(T.xi0[:], T.pz[:, 64:128], ["pz"], ["xi0"])
+    masks(0, 1)
+    convert(0)
+    masks(0, 2)
+    ts(T.LT[:], T.ix[:, 0:16], T.pc[:], None, A.is_lt, None, ["ix0", "pc"], ["LT"])
+    cp(T.FL[:], T.ix[:, 0:32], IX, ["FL"])
+    tt(T.LT[:], T.LT[:], T.RM[:], A.subtract, ["LT", "RM"], ["LT"])
+    scaled("v", blk(T.CW, 2), T.BB[:], wcol("key"), ["BB", "key"], ["CW2"])
+    ts(T.LT[:], T.LT[:], 4096.0, None, A.mult, None, ["LT"], ["LT"])
+    ts(T.own[:], T.iw[:], T.pc[:], None, A.add, None, ["iw", "pc"], ["own"])
+    scaled("v", wide(T.FW, 1), T.F1[:], -8192.0, ["F1"], ["FW1"])
+    convert(1)
+    for name in ("hcol", "last", "step", "keep"):
+        weights("s", name)
+    dma("y", T.H[:, 0:2048], T.xreg[:], ["Kr1"], ["Hx"])
 
-    def late0():
-        act(T.Ssel[:], T.idf[:], ["idf", "w5"], ["Ssel"], scale=col(5))
-        for b in range(4):
-            act(T.Con[:, 128 * b:128 * b + 128], T.ix[:, 0:128], ["ix", "w7", "wb"], ["Con"], scale=col(7),
-                bias=col(16 + b))
-        act(T.FW[:, 720:864], T.F1[:], ["F1"], ["FW5"], scale=4096.0)
-        for r in range(0, 6):
-            tri(r)
+    def setup_rest():
+        convert(4)
+        tri("v", range(12))
+        scaled("v", blk(T.CW, 3), T.BB[:], wcol("last"), ["BB", "last"], ["CW3"])
+        scaled("v", wide(T.FW, 0), T.F1[:], wcol("hcol"), ["F1", "hcol"], ["FW0"])
 
-    def tri(r):
-        act(T.TR[:, 128 * r:128 * r + 128], T.F1[:, 16 - r:144 - r], ["F1", "LT"], ["TR"], scale=T.LT[:, r:r + 1])
-
-    def late1():
-        for r in range(6, 16):
-            tri(r)
-
-    def late2():
-        act(T.FW[:, 576:720], T.F1[:], ["F1", "w4"], ["FW4"], scale=col(4))
-        act(T.IW[:, 128:256], T.idf[:], ["idf"], ["IW1"], scale=2.0 ** 22)
-        act(T.II[:, 128:256], T.idf[:], ["idf"], ["II1"])
-
-    def sel(t):
-        for m in range(3):
-            k = 3 * t + m
-            act(T.Sel[:, 128 * k:128 * k + 128], T.BB[:, 128 - 16 * t:256 - 16 * t], ["BB", "RM"], ["Sel%d" % k],
-                scale=rm(k))
-
-    def wrap(m):
-        Mk = T["Mk%d" % m]
-        for r in range(8):
-            mm(T.pw[:, 0:64], T.Ff[:, 8 - r:136 - r], Mk[:, r:512:8], r == 0, r == 7, ["Ff", "Mk%d" % m], ["pw"])
-
-    def cut(m):
-        c = slice(32 * m, 32 * m + 32)
-        tt(T.tmp[:], T.pw[:, 0:64], T.hm[:], A.mult, ["pw", "hm"], ["tmp"])
-        tt(T.key[:, c], T.tmp[:, 0:64:2], T.tmp[:, 1:64:2], A.add, ["tmp"], ["key%d" % m])
-        ts(T.vi[:, c], T.key[:, c], 2047, None, A.bitwise_and, None, ["key%d" % m], ["vi%d" % m])
-        cp(T.off[:, c], T.vi[:, c], ["vi%d" % m], ["off%d" % m])
-
-    def head(t):
-        if t == 0:
-            z, zr = T.H[:, 2048:2560], "H0"
-        else:
-            z, zr = T["zi%d" % t][:], "zi%d" % t
-            add("x", None, [], [zr], kind="x", sem="arr%d" % t, n=n_in)
-        for m, b in enumerate(("pa", "pb", "pcc")):
-            k = 3 * t + m
-            mm(T[b][:], T.Sel[:, 128 * k:128 * k + 128], z, True, True, ["Sel%d" % k, zr], [b])
-        if t > 0:
-            mm(T.pd[:], T.II[:, 128 - 16 * t:256 - 16 * t], z, True, True, ["II0", "II1", zr], ["pd"])
+    def setup_scalar(m):
+        if m == 0:
+            scaled("s", T.WC[:, 8:10], T.RM[:, 1:3], 32.0, ["RM"], ["w8"])
+            scaled("s", T.Ssel[:], blk(T.ID, 0), wcol("keep"), ["ID0", "keep"], ["Ssel"])
+            scaled("s", T.WC[:, 16:18], T.ix[:, 0:2], col(9), ["ix0", "w8"], ["wb"])
+            scaled("s", T.WC[:, 20:24], T.ix[:, 8:16:2], col(9), ["ix0", "w8"], ["wt"])
+        if m == 1:
+            tri("s", range(12, 16))
+        if m == 2:
+            for b in range(2):
+                act(T.Con[:, 256 * b:256 * b + 256], T.ix[:], IX + ["w8", "wb"], ["Con%d" % b], scale=col(8),
+                    bias=col(16 + b))
+        if m == 2:
+            act(T.NT[:, 0:8:2], T.RM[:, 0:4], ["RM"], ["NT0"], scale=-1.0, bias=1.0)
+            act(T.NT[:, 1:8:2], T.RM[:, 0:4], ["RM"], ["NT1"], scale=0.0, bias=1.0)
+            scaled("s", wide(T.FW, 2), T.F1[:], wcol("key"), ["F1", "key"], ["FW2"])
 
     sent = 0
     HALF = (slice(0, 256), slice(256, 512))
     for t in range(VISITS):
+        last = t == VISITS - 1
         hz = slice(2048 + 512 * t, 2560 + 512 * t)
-        HALL = ["Hx"] + ["H%d" % k for k in range(t + 1)]
-        if t == 0:
-            head(0)
-        else:
-            act(T.H[:, hz], T.pd[:], ["pd"], ["H%d" % t])
-        for h, u in enumerate(HALF):
-            ts(T.pe[:, u], T.pa[:, u], T.pc[:], None, A.is_equal, None, ["pa", "pc"] + (["pe"] if h == 0 else []),
-               ["e%d" % h])
-        for h, u in enumerate(HALF):
-            tt(T.Mk0[:, u], T.K[:, u], T.pe[:, u], A.mult, ["Ka%d" % h, "e%d" % h, "pe"], ["Mk0"])
-        wrap(0)
-        ts(T.m1[:], T.pb[:], T.pc[:], None, A.is_equal, None, ["pb", "pc"], ["m1"])
-        if t == 0:
-            ts(T.own[:], T.iw[:], T.pc[:], None, A.add, None, ["iw", "pc"], ["own"])
-        cut(0)
-        tt(T.Mk1[:], T.K[:, 0:2048].indirect(T.off[:, 0:32]), T.m1[:], A.mult, KALL + ["off0", "m1"], ["Mk1"])
-        if t == 0:
-            late0()
-        act(T.C12[:, 0:512], T.M[:, 0:2048].indirect(T.off[:, 0:32]), MALL + ["off0"], ["C1"])
-        if t == 0:
-            late1()
-        wrap(1)
-        mm(T.pa[:], T.BBf[:], T.Mk1[:], True, True, ["BBf", "Mk1"], ["pa"])
-        ts(T.m2[:], T.pcc[:], T.pc[:], None, A.is_equal, None, ["pcc", "pc"], ["m2"])
-        ts(T.nm2[:], T.pcc[:], T.pc[:], None, A.not_equal, None, ["pcc", "pc"], ["nm2"])
-        cut(1)
-        tt(T.Mk2[:], T.K[:, 0:2048].indirect(T.off[:, 32:64]), T.m2[:], A.mult, KALL + ["off1", "m2"], ["Mk2"])
-        act(T.C12[:, 512:1024], T.M[:, 0:2048].indirect(T.off[:, 32:64]), MALL + ["off1"], ["C2"])
-        if t == 0:
-            late2()
-        if t < VISITS - 1:
-            sel(t + 1)
-        else:
-            act(T.FW[:, 0:144], T.F1[:], ["F1", "w0"], ["FW0"], scale=col(0))
-            act(T.FW[:, 432:576], T.F1[:], ["F1", "w3"], ["FW3"], scale=col(3))
-        wrap(2)
-        for r in range(16):
-            mm(T.pg[:, 0:64], fw(2, r), T.C12[:, r:1024:16], r == 0, r == 15, ["FW2", "C1", "C2"], ["pg"])
-        tt(T.q01[:], T.key[:, 0:64], T.vi[:, 0:64], A.subtract, ["key0", "key1", "vi0", "vi1"], ["q01"])
-        tt(T.Aa[:], T.pa[:], T.m2[:], A.mult, ["pa", "m2"], ["Aa"])
-        cut(2)
-        act(T.C3[:], T.M[:, 0:2048].indirect(T.off[:, 64:96]), MALL + ["off2", "w6"], ["C3"], bias=col(6))
-        for j, k in enumerate(ORD):
-            cp(T.offD[:, 8 * j:8 * j + 8], T.vi[:, 64 + k:96:4], ["vi2"], ["offD"])
-        act(T.D[:], T.NUM[:].indirect(T.offD[:]), ["NUM", "offD"], ["D0"])
-        tt(T.q2[:], T.key[:, 64:96], T.vi[:, 64:96], A.subtract, ["key2", "vi2"], ["q2"])
-        tt(T.ne[:], T.pg[:, 0:64], T.q01[:], A.not_equal, ["pg", "q01"], ["ne"])
-        tt(T.Bb[:], T.K[:, 0:2048].indirect(T.off[:, 64:96]), T.nm2[:], A.mult, KALL + ["off2", "nm2"], ["Bb"])
-        y = T.pg[:, 64:96]
-        mm(y, T.idm[:], T.q2[:], True, False, ["idm", "q2"], ["pg"])
-        mm(y, T.IW[:, 0:128], T.eps[:], False, False, ["IW0", "eps"], ["pg"])
-        mm(y, T.IW[:, 0:128], T.ne[:, 0:32], False, False, ["IW0", "ne"], ["pg"])
-        mm(y, T.IW[:, 0:128], T.ne[:, 32:64], False, False, ["IW0", "ne"], ["pg"])
-        for r in range(16):
-            mm(y, fw(1, r), T.C3[:, r:512:16], False, r == 15, ["FW1", "C3"], ["pg"])
-        mm(T.pb[:], T.Ssel[:], T.C3[:], True, False, ["Ssel", "C3"], ["pb"])
-        mm(T.pb[:], T.II[:, 0:128], T.Con[:], False, True, ["II0", "Con"], ["pb"])
-        act(T.ay[:], y, ["pg"], ["ay"], func=F.Abs)
-        tt(T.zf[:], T.ay[:], T.own[:, 32 * t:32 * t + 32], A.min, ["ay", "own"], ["zf"])
-        ts(T.big[:], T.ay[:], 4095.5, 4096.0, A.is_ge, A.mult, ["ay"], ["big"])
-        cp(T.zoff[:], T.zf[:], ["zf"], ["zoff"])
-        tt(T.Wd[:], T.vi[:, 64:96], T.big[:], A.add, ["vi2", "big"], ["Wd"])
-        ts(T.offN[:], T.ay[:], 4095.5, 2.0 * t, A.is_ge, A.add, ["ay"], ["offN"])
-        zo = T["zo%d" % t]
-        act(zo[:], T.H[:, 0:hz.stop].indirect(T.zoff[:]), HALL + ["zoff"], ["zo%d" % t])
-        if t < VISITS - 1:
-            rid, pid = topo.addr(nxt, core)
-            add("g", lambda a=T["zi%d" % (t + 1)][:], b=zo[:], s=T.sem["arr%d" % (t + 1)]:
-                g.remote_dma(a, b, s, T.sem.snt, pid, rid, topo.mask(core, nxt)), ["zo%d" % t], [], kind="r")
-            sent += len(topo.engines(core, nxt))
-        else:
-            dma("y", T.yz[:], zo[:], ["zo%d" % t], [])
-        act(T.S[:], T.pb[:], ["pb", "wt"], ["S"], bias=col(20 + t))
-        act(T.NM[:], T.NT[:].indirect(T.offN[:]), ["NT", "offN"], ["NM"])
-        for k, a in ((1, 8), (2, 16), (3, 16)):
-            tt(T.E[:, 256 + 256 * k:512 + 256 * k], T.Wd[:].indirect(T.FL[:, 16 + 16 * k:32 + 16 * k]),
-               T.D[:, 16 * a:16 * a + 256], A.is_equal, ["Wd", "FL", "D0"], ["E%d" % k])
-        tt(T.E[:, 0:512], T.Wd[:].indirect(T.FL[:, 0:32]), T.D[:, 0:512], A.is_equal, ["Wd", "FL", "D0"], ["E0"])
-        mm(T.ph[:, 0:32], T.TR[:, 0:128], T.eps[:], True, False, ["TR", "eps"], ["ph"])
-        for j, k in enumerate(ORD):
-            mm(T.ph[:, 8 * j:8 * j + 8], T.idf[:], T.Wd[:, k:32:4], False, False, ["idf", "Wd"], ["ph"])
-        for k, a in ((1, 8), (2, 16), (3, 16)):
+        HALL = ["Hx", "H0"] + ["H%d%s" % (k, h) for k in range(1, t + 1) for h in "ab"]
+        xi, xr = T["xi%d" % t], "xi%d" % t
+        y = T.pU[:, 0:32]
+        if t > 0:
+            add("x", None, [], [xr], kind="x", sem="ax%d" % t, n=n_in)
+            add("x", None, [], ["zi%d" % t], kind="x", sem="az%d" % t, n=n_in)
+            zi = T["zi%d" % t]
+            dma("y", T.H[16 * t:128, hz], zi[0:128 - 16 * t, :], ["zi%d" % t], ["H%da" % t])
+            dma("y", T.H[0:16 * t, hz], zi[128 - 16 * t:128, :], ["zi%d" % t], ["H%db" % t])
+            masks(t, 1)
+            masks(t, 2)
+        for m in range(3):
+            if m == 0:
+                src, mask, rd = T.T0[:].indirect(xi[:, 0:32]), T.K[:, 0:512], ["T0", xr, "K0a", "K0b"]
+            else:
+                src = T.K[:, 0:2048].indirect(T.off[:, 32 * m - 32:32 * m])
+                mask, rd = T["m%d" % m][:], KC + ["off%d" % (m - 1), "m%d" % m]
+            Kh, Kf, C = T["Kh%d" % m], T["Kf%d" % m], T["C%d" % m]
+            tt(Kh[:], src, mask, A.mult, rd, ["Kh%d" % m])
+            if t == 0 and m == 0:
+                convert(2)
+            tt(Kf[:], src, mask, A.mult, rd, ["Kf%d" % m])
+            if t == 0 and m == 0:
+                convert(3)
+            pw = T.pw[:, 32 * m:32 * m + 32]
+            to_w(pw, T.F1, 0, Kh, 0, 512, True, True, ["F1", "Kh%d" % m], ["pw"])
+            o = T.off[:, 32 * m:32 * m + 32]
+            cp(o, pw, ["pw"], ["off%d" % m])
+            if t == 0 and m == 0:
+                setup_rest()
+            if m == 1:
+                mm(y, T.idf[:], T.own[:, 32 * t:32 * t + 32], True, False, ["idf", "own"], ["pU"])
+            if m > 0:
+                mm(T.pY[:], blk(T.CW, m - 1), T["C%d" % (m - 1)][:], False, False, ["CW%d" % (m - 1), "C%d" % (m - 1)],
+                   ["pY"])
+            if m == 2:
+                mm(T.pk[:], blk(T.CW, 2), T.C1[:], True, True, ["CW2", "C1"], ["pk"])
+            mm(T.pY[:], blk(T.BF, m), Kf[:], m == 0, False, ["BF%d" % m, "Kf%d" % m], ["pY"])
+            if m < 2:
+                act(C[:], T.M[:, 0:2048].indirect(o), ["M", "off%d" % m], ["C%d" % m])
+            else:
+                act(C[:], T.M[:, 0:2048].indirect(o), ["M", "off2", "step"], ["C2"], bias=wcol("step"))
+            if m == 0:
+                act(T.nm2[:], T.m2[:], ["m2"], ["nm2"], scale=-1.0, bias=1.0)
+            if m == 1 and not last:
+                xw(t + 1, "s")
+            if m == 1 and last:
+                scaled("s", col(10), rm(0), 1.0 / 32, ["RM"], ["w10"])
+                scaled("s", wide(T.FW, 3), T.F1[:], col(10), ["F1", "w10"], ["FW3"])
+            if t == 0:
+                setup_scalar(m)
+        ts(T.Wd[:], T.pw[:, 64:96], ROUND, ROUND - 4096.0, A.add, A.subtract, ["pw"], ["Wd"])
+        cp(T.Wb[:], T.Wd[:].indirect(T.FL[:]), ["Wd", "FL"], ["Wb"])
+        mm(T.pY[:], blk(T.CW, 3), T.C2[:], False, True, ["CW3", "C2"], ["pY"])
+        to_w(T.pz[:, 0:32], T.FW, 0, T.C2, 0, 512, True, True, ["FW0", "C2"], ["pz"])
+        mm(T.ph[:, 0:32], T.idf[:], T.Wd[:], True, False, ["idf", "Wd"], ["ph"])
+        tt(T.Aa[:], T.pk[:], T.m2[:], A.mult, ["pk", "m2"], ["Aa"])
+        act(T.cw[:], T.pz[:, 0:32], ["pz"], ["cw"])
+
+        def compare(k):
+            w = 512 - 16 * k
+            tt(T.E[:, 512 * k:512 * k + w], T.pY[:, 0:w], T.Wb[:, 16 * k:512], A.is_equal, ["pY", "Wb"], ["E%d" % k])
+
+        def count(k):
             for r in range(16):
-                mm(T.ph[:, a:a + 16], fw(5, r), T.E[:, 256 + 256 * k + r:512 + 256 * k:16], False, False,
-                   ["FW5", "E%d" % k], ["ph"])
-        for r in range(1, 16):
-            mm(T.ph[:, 0:32], T.TR[:, 128 * r:128 * r + 128], T.E[:, r:512:16], False, r == 15, ["TR", "E0"], ["ph"])
-        for b, w in (("pg", 1), ("pw", 0)):
-            mm(T[b][:], fw(4, t), T.C3[:], True, False, ["FW4", "C3"], [b])
-            mm(T[b][:], T.IW[:, 128 * w:128 * w + 128], T.NM[:], False, True, ["IW%d" % w, "NM"], [b])
-        for j, k in enumerate(ORD):
-            ts(T.soff[:, k:32:4], T.ph[:, 8 * j:8 * j + 8], T.own[:, k:k + 1], None, A.min, None, ["ph", "own"],
-               ["soff"])
-        if t < VISITS - 1:
-            head(t + 1)
-        for c in range(7, -1, -1):
-            u = slice(64 * c, 64 * c + 64)
-            o = T.soff[:, 4 * c:4 * c + 4]
-            tt(T.K[:].indirect(o), T.Aa[:, u], T.Bb[:, u], A.add, ["soff", "Aa", "Bb"], KALL)
-            act(T.M[:].indirect(o), T.S[:, u], ["soff", "S"], MALL, func=F.Silu)
-        for b, op in (("pg", A.min), ("pw", A.max)):
-            for h, u in enumerate(HALF):
-                tt(T.K[:, u], T.K[:, u], T[b][:, u], op, ["Ka%d" % h, b], ["Ka%d" % h])
-            if t == VISITS - 1 and b == "pg":
-                cp(T.Mb[:, 1536:2048], T.M[:, 1536:2048], MALL, ["Mb3"])
-                for h in range(3):
-                    u = slice(512 * h, 512 * h + 512)
-                    act(T.Mb[:, u], T.M[:, u], MALL, ["Mb%d" % h])
-                for b2 in range(8, 12):
-                    mm(T.pa[:, 0:128], T.idf[:], T.K[:, 128 * b2:128 * b2 + 128], b2 == 8, False, ["idf", "Kb", "Kc"],
-                       ["pa"])
-                order = [0, 1, 2, 3, 12, 13, 14, 15, 4, 5, 6, 7, 8, 9, 10, 11]
-                for b2 in order:
-                    mm(T.pd[:, 0:128], fw(0, b2), T.Mb[:, 128 * b2:128 * b2 + 128], b2 == 0, b2 == 11,
-                       ["FW0", "Mb%d" % (b2 // 4)], ["pd"])
-    cp(T.fo[:], T.pd[:, 0:128], ["pd"], ["fo"])
-    HALL = ["Hx", "H0", "H1", "H2", "H3"]
-    GS = ((0, 48, "s"), (48, 96, "s"), (96, 128, "v"))
-    for k, (a, b, e) in enumerate(GS):
+                mm(T.ph[:, k:32], blk(T.TR, r) if k == 0 else blk(T.ID, 4), T.E[:, 512 * k + r:512 * k + 512 - 16 * k:16],
+                   False, k == NB - 1 and r == 15, ["TR%d" % r, "ID4", "E%d" % k], ["ph"])
+
+        compare(0)
+        to_w(y, T.FW, 1, T.E, 0, 512, False, True, ["FW1", "E0"], ["pU"])
+        count(0)
+        compare(1)
+        count(1)
+        tt(T.zf[:], y, T.cw[:], A.max, ["pU", "cw"], ["zf"])
+        ts(T.offN[:], y, 0.0, 2.0 * t, A.is_ge, A.add, ["pU"], ["offN"])
+        cp(T.zoff[:], T.zf[:], ["zf"], ["zoff"])
+        zo, zr = T["zo%d" % t], "zo%d" % t
+        act(zo[:], T.H[:, 0:hz.stop].indirect(T.zoff[:]), HALL + ["zoff"], [zr])
+        act(T.NM[:], T.NT[:].indirect(T.offN[:]), ["NT0", "NT1", "offN"], ["NM"])
+        if last:
+            dma("y", T.yz[:], zo[:], [zr], [])
+        for k in range(2, NB):
+            compare(k)
+            count(k)
+        if not last:
+            slots(t + 1, zo, 0, zr)
+        mm(T.pb[:], T.Ssel[:], T.C2[:], True, False, ["Ssel", "C2"], ["pb"])
+        mm(T.pb[:], blk(T.ID, 0), T.Con[:], False, True, ["ID0", "Con0", "Con1"], ["pb"])
+        act(T.S[:], T.pb[:], ["pb", "wt"], ["S"], bias=col(20 + t))
+        tt(T.Bb[:], T.K[:, 0:2048].indirect(T.off[:, 64:96]), T.nm2[:], A.mult, KC + ["off2", "nm2"], ["Bb"])
+        tt(T.sf[:], T.ph[:, 0:32], T.own[:, 0:32], A.min, ["ph", "own"], ["sf"])
+        cp(T.soff[:], T.sf[:], ["sf"], ["soff"])
+        for b, w in (("pU", 5), ("pL", 6)):
+            mm(T[b][:], band(T.FW, 2, t), T.C2[:], True, False, ["FW2", "C2"], [b])
+            mm(T[b][:], blk(T.ID, w), T.NM[:], False, True, ["ID%d" % w, "NM"], [b])
+        nb = 32 // NB
+        for c in range(nb - 1, -1, -1):
+            u = slice(16 * NB * c, 16 * NB * (c + 1))
+            o = T.soff[:, NB * c:NB * (c + 1)]
+            tt(T.K[:].indirect(o), T.Aa[:, u], T.Bb[:, u], A.add, ["soff", "Aa", "Bb"], KC)
+            act(T.M[:].indirect(o), T.S[:, u], ["soff", "S"], ["M"], func=F.Silu)
+            if c == nb - 1 - 8 // NB + 1 and not last:
+                xo = T["xo%d" % (t + 1)]
+                cp(xo[:], T.pz[:, 64:128], ["pz"], ["xo"])
+                send(T["xi%d" % (t + 1)][:], xo[:], "ax%d" % (t + 1), ["xo"])
+                send(T["zi%d" % (t + 1)][:], zo[:], "az%d" % (t + 1), [zr])
+                sent += 2 * len(topo.engines(core, nxt))
+        if last:
+            mm(T.pk[:], T.idf[:], T.K[:, 512:1024], True, False, ["idf", "K1"], ["pk"])
+            for h in (0, 1):
+                act(T.Mb[:, 512 * h:512 * h + 512], T.M[:, 512 * h:512 * h + 512], ["M"], ["Mb%d" % h])
+        for b, op in (("pU", A.min), ("pL", A.max)):
+            for h, u in zip("ab", HALF):
+                tt(T.K[:, u], T.K[:, u], T[b][:, u], op, ["K0" + h, b], ["K0" + h])
+            if last:
+                h = 2 if b == "pU" else 3
+                cp(T.Mb[:, 512 * h:512 * h + 512], T.M[:, 512 * h:512 * h + 512], ["M"], ["Mb%d" % h])
+    order = [0, 1, 2, 3, 8, 9, 10, 11, 4, 5, 6, 7, 12, 13, 14, 15]
+    for b in order:
+        mm(T.pz[:, 0:128], band(T.FW, 0, b), blk(T.Mb, b), b == 0, b == 15, ["FW0", "Mb%d" % (b // 4)], ["pz"])
+    cp(T.fo[:], T.pz[:, 0:128], ["pz"], ["fo"])
+    mm(T.pk[:], T.idf[:], T.K[:, 1536:2048], False, True, ["idf", "K3", "K4"], ["pk"])
+    tt(T.Aa[:], T.K[:, 0:512], T.K[:, 1024:1536], A.add, KC, ["Aa"])
+    HALL = ["Hx", "H0"] + ["H%d%s" % (k, h) for k in range(1, 4) for h in "ab"]
+    GS = ((0, 48, "s", "pU"), (48, 96, "s", "ph"), (96, 128, "s", "pL"))
+    for k, (a, b, e, bank) in enumerate(GS):
         (act if e == "s" else cp)(T.G[:, 16 * a:16 * b], T.H[:].indirect(T.fo[:, a:b]), HALL + ["fo"], ["G%d" % k])
-    for b in range(12, 16):
-        mm(T.pa[:, 0:128], T.idf[:], T.K[:, 128 * b:128 * b + 128], False, b == 15, ["idf", "Kb", "Kc"], ["pa"])
     for b in range(16):
-        mm(T.pb[:, 0:128], fw(3, b), T.Mb[:, 128 * b:128 * b + 128], b == 0, b == 15, ["FW3", "Mb%d" % (b // 4)], ["pb"])
-    for h, u in enumerate(HALF):
-        tt(T.t3[:, u], T.K[:, u], T.K[:, 512 + u.start:512 + u.stop], A.add, KALL, ["t3%d" % h])
+        mm(T.pb[:, 0:128], band(T.FW, 3, b), blk(T.Mb, b), b == 0, b == 15, ["FW3", "Mb%d" % (b // 4)], ["pb"])
+
+    def gsum(k):
+        a, b, e, bank = GS[k]
+        for r in range(16):
+            mm(T[bank][:, 0:b - a], blk(T.ID, 0), T.G[:, 16 * a + r:16 * b:16], r == 0, r == 15,
+               ["ID0", "G%d" % k], [bank])
+
+    tt(T.pY[:], T.pk[:], T.Aa[:], A.add, ["pk", "Aa"], ["pY"])
+    ts(T.Bb[:], T.pY[:], ROUND, ROUND, A.add, A.subtract, ["pY"], ["Bb"])
+    tt(T.Kh0[:], T.pY[:], T.Bb[:], A.subtract, ["pY", "Bb"], ["Kh0"])
     cp(T.oc[:], T.pb[:, 0:128], ["pb"], ["oc"])
     dma("y", T.yc[:], T.oc[:], ["oc"], [])
-    tt(T.pe[:, 0:128], T.pa[:, 0:128], T.t3[:, 0:128], A.add, ["pa", "t30", "e0", "e1"], ["pe"])
-    tt(T.Aa[:, 0:128], T.t3[:, 256:384], T.t3[:, 384:512], A.add, ["t31"], ["Aa"])
-    tt(T.pg[:, 0:128], T.pe[:, 0:128], T.t3[:, 128:256], A.add, ["pe", "t30"], ["pg"])
-    tt(T.ok_[:], T.pg[:, 0:128], T.Aa[:, 0:128], A.add, ["pg", "Aa"], ["ok_"])
+    gsum(0)
+    for b in range(4):
+        mm(T.pw[:, 0:128], T.idf[:], blk(T.Bb, b), b == 0, False, ["idf", "Bb"], ["pw"])
+    gsum(1)
+    for b in range(4):
+        mm(T.pw[:, 0:128], blk(T.ID, 5), blk(T.Kh0, b), False, b == 3, ["ID5", "Kh0"], ["pw"])
+    cp(T.ok_[:], T.pw[:, 0:128], ["pw"], ["ok_"])
     dma("y", T.yk[:], T.ok_[:], ["ok_"], [])
-    for k, bank in ((0, "pcc"), (2, "ph"), (1, "pd")):
-        a, b, e = GS[k]
-        for r in range(16):
-            mm(T[bank][:, 0:b - a], T.II[:, 0:128], T.G[:, 16 * a + r:16 * b:16], r == 0, r == 15,
-               ["II0", "G%d" % k], [bank])
-    for k, bank in ((0, "pcc"), (2, "ph"), (1, "pd")):
-        a, b, e = GS[k]
+    gsum(2)
+    for k, (a, b, e, bank) in enumerate(GS):
         act(T.ox[:, a:b], T[bank][:, 0:b - a], [bank], ["ox%d" % k])
     dma("s", T.yx[:], T.ox[:], ["ox0", "ox1", "ox2"], [])
     emit(g, T, ops)

@@ -17,30 +17,30 @@ SCRATCH = {
     "C0": ("sbuf", [128, 512], bf), "C1": ("sbuf", [128, 512], bf), "C2": ("sbuf", [128, 512], bf),
     "Aa": ("sbuf", [128, 512], f32), "Bb": ("sbuf", [128, 512], f32), "S": ("sbuf", [128, 512], f32),
     "Wb": ("sbuf", [128, 512], f32), "E": ("sbuf", [128, 2048], bf), "NM": ("sbuf", [128, 512], bf),
-    "off": ("sbuf", [128, 96], u16), "Wd": ("sbuf", [128, 32], f32), "cw": ("sbuf", [128, 32], f32),
+    "Wb3": ("sbuf", [128, 8, 64], f32), "sm": ("sbuf", [128, 64], f32), "own2": ("sbuf", [128, 64], f32),
+    "off": ("sbuf", [128, 96], u16), "Wd": ("sbuf", [128, 64], f32), "cw": ("sbuf", [128, 32], f32),
     "zf": ("sbuf", [128, 32], f32), "zoff": ("sbuf", [128, 32], u16), "offN": ("sbuf", [128, 32], u16),
     "sf": ("sbuf", [128, 32], f32), "soff": ("sbuf", [128, 32], u16), "FL": ("sbuf", [128, 32], u16),
     "ip": ("sbuf", [128, 1], i32), "pm": ("sbuf", [128, 1], i32), "pf": ("sbuf", [128, 1], f32),
     "pc": ("sbuf", [128, 1], f32), "g16": ("sbuf", [128, 1], f32),
-    "ix": ("sbuf", [128, 256], f32), "ib": ("sbuf", [128, 128], f32), "ilo": ("sbuf", [128, 256], f32),
-    "ihi": ("sbuf", [128, 256], f32), "iw": ("sbuf", [128, 128], f32), "own": ("sbuf", [128, 128], f32),
+    "ix": ("sbuf", [128, 256], f32), "ib": ("sbuf", [128, 128], bf), "ilo": ("sbuf", [128, 256], bf),
+    "ihi": ("sbuf", [128, 256], bf), "iw": ("sbuf", [128, 128], f32), "own": ("sbuf", [128, 128], f32),
     "RM": ("sbuf", [128, 16], f32), "LT": ("sbuf", [128, 16], f32), "WC": ("sbuf", [128, 40], f32),
     "T0": ("sbuf", [128, 256], bf), "T1": ("sbuf", [128, 256], bf), "F2": ("sbuf", [128, 256], bf),
-    "F1": ("sbuf", [128, 144], bf), "nil": ("sbuf", [128, 128], f32),
+    "F1": ("sbuf", [128, 144], bf), "nil": ("sbuf", [128, 128], f32), "iw2": ("sbuf", [128, 64], f32),
     "BB": ("sbuf", [128, 128], bf), "BF": ("sbuf", [128, 384], f32), "CW": ("sbuf", [128, 512], bf),
     "idf": ("sbuf", [128, 128], f32), "ID": ("sbuf", [128, 896], bf), "XW": ("sbuf", [128, 1152], bf),
-    "FW": ("sbuf", [128, 576], bf), "TR": ("sbuf", [128, 2048], bf), "Ssel": ("sbuf", [128, 128], bf),
+    "FW": ("sbuf", [128, 432], bf), "TR": ("sbuf", [128, 2048], bf), "Ssel": ("sbuf", [128, 128], bf),
     "Con": ("sbuf", [128, 512], bf), "one": ("sbuf", [128, 512], bf),
     "ci": ("sbuf", [128, 128], i32), "cm": ("sbuf", [128, 128], f32),
     "WB": ("sbuf", [128, 8], f32), "NT": ("sbuf", [128, 8], f32),
-    "fo": ("sbuf", [128, 128], u16), "ok_": ("sbuf", [128, 128], f32),
-    "ox": ("sbuf", [128, 128], bf), "oc": ("sbuf", [128, 128], f32),
-    "pw": ("psum", [128, 512], f32), "pz": ("psum", [128, 512], f32), "pY": ("psum", [128, 512], f32),
-    "pk": ("psum", [128, 512], f32), "ph": ("psum", [128, 512], f32), "pb": ("psum", [128, 512], f32),
+    "fo": ("sbuf", [128, 128], u16), "ok_": ("sbuf", [128, 128], f32), "ox": ("sbuf", [128, 128], bf),
+    "pw": ("psum", [128, 512], f32), "pz": ("psum", [128, 512], f32), "pY": ("psum", [128, 8, 64], f32),
+    "pk": ("psum", [128, 512], f32), "ph": ("psum", [128, 64, 4, 2], f32), "pb": ("psum", [128, 512], f32),
     "pU": ("psum", [128, 512], f32), "pL": ("psum", [128, 512], f32),
 }
 NDMA = 24
-SEMAPHORES = (["sv", "ss", "sp", "sg", "snt"] + ["ax%d" % t for t in (1, 2, 3)] + ["az%d" % t for t in (1, 2, 3)]
+SEMAPHORES = (["sv", "ss", "sp", "sg", "snt"] + ["a%s%d" % (k, t) for k in "xsz" for t in (1, 2, 3)]
               + ["d%d" % k for k in range(NDMA)])
 BANKS = ("pw", "pz", "pY", "pk", "ph", "pb", "pU", "pL")
 VISITS = 4
@@ -143,10 +143,13 @@ def rank_program(g, core, T, topo):
             if len(way) == 3 and way[1] == core:
                 rid, pid = topo.addr(way[2], core)
                 for t in range(1, VISITS):
-                    for buf, sem in (("xi%d" % t, "ax%d" % t), ("zi%d" % t, "az%d" % t)):
-                        g.wait_ge(T.sem[sem], len(topo.engines(way[0], core)))
-                        g.remote_dma(T[buf][:], T[buf][:], T.sem[sem], T.sem.snt, pid, rid, topo.mask(core, way[2]))
-                g.wait_ge(T.sem.snt, 2 * (VISITS - 1) * len(topo.engines(core, way[2])))
+                    xi, zi = T["xi%d" % t], T["zi%d" % t]
+                    msgs = {"x": xi[:, 0:32], "s": xi[:, 32:64], "z": zi[:]}
+                    for k in "xsz":
+                        sem = T.sem["a%s%d" % (k, t)]
+                        g.wait_ge(sem, len(topo.engines(way[0], core)))
+                        g.remote_dma(msgs[k], msgs[k], sem, T.sem.snt, pid, rid, topo.mask(core, way[2]))
+                g.wait_ge(T.sem.snt, 3 * (VISITS - 1) * len(topo.engines(core, way[2])))
         return
     nxt = route(T, topo, rank)[1]
     n_in = len(topo.engines(route(T, topo, (rank - 1) % n)[-2], core))
@@ -173,11 +176,14 @@ def rank_program(g, core, T, topo):
     def act(out, a, r, w, func=F.Identity, **kw):
         add("s", lambda: S.activation(out, a, func, **kw), r, w)
 
-    def scaled(e, out, a, c, r, w):
+    def scaled(out, a, c, r, w, e="v"):
         if e == "v":
             ts(out, a, c, None, A.mult, None, r, w)
         else:
             act(out, a, r, w, scale=c)
+
+    def diag(out, c, w):
+        add("g", lambda: g.affine_select(out, T.nil[:], [[-1, 128]], A.not_equal, c, 0, 1), ["nil"], [w])
 
     def mm(out, l, rhs, st, sp, r, w):
         add("p", lambda: P.matmul(out, l, rhs, st, sp), r, w)
@@ -187,9 +193,6 @@ def rank_program(g, core, T, topo):
             add("g", lambda: g.iota(out, pat, base, cm, allow_small_or_imprecise_dtypes=True), [], w)
         else:
             add("g", lambda: g.iota(out, pat, base, cm), [], w)
-
-    def diag(out, c, w):
-        add("g", lambda: g.affine_select(out, T.nil[:], [[-1, 128]], A.not_equal, c, 0, 1), ["nil"], [w])
 
     def dma(e, out, in_, r, w):
         qq = g.sync if e == "y" else g.scalar
@@ -208,14 +211,15 @@ def rank_program(g, core, T, topo):
     def wcol(name):
         return col(list(COLS).index(name))
 
-    def weights(e, name):
-        for j, (row, c) in enumerate(COLS[name].items()):
-            if j == 0:
-                scaled(e, wcol(name), rm(row), c, ["RM"], [name])
-            elif e == "v":
-                ts(wcol(name), rm(row), c, wcol(name), A.mult, A.add, ["RM", name], [name])
-            else:
-                act(wcol(name), rm(row), ["RM", name], [name], scale=c, bias=wcol(name))
+    def weights(j, e):
+        for name, terms in COLS.items():
+            for row, c in list(terms.items())[j:j + 1]:
+                if j == 0:
+                    scaled(wcol(name), rm(row), c, ["RM"], [name], e)
+                elif e == "v":
+                    ts(wcol(name), rm(row), c, wcol(name), A.mult, A.add, ["RM", name], [name])
+                else:
+                    act(wcol(name), rm(row), ["RM", name], [name], scale=c, bias=wcol(name))
 
     def blk(buf, k):
         return buf[:, 128 * k:128 * k + 128]
@@ -230,34 +234,29 @@ def rank_program(g, core, T, topo):
         for j in range(16):
             mm(out, band(buf, k, j), u[:, lo + j:hi:16], st and j == 0, sp and j == 15, r, w)
 
-    def xw(t, e):
-        for k, c in ((2 * t, col(36 + t)), (2 * t + 1, rm(3 * t + 2))):
-            scaled(e, wide(T.XW, k), T.F2[:, 112 - 16 * t:256 - 16 * t], c, ["F2a", "F2b", "w36", "RM"], ["XW%d" % k])
+    def xw(t, h):
+        scaled(wide(T.XW, 2 * t + h), T.F2[:, 112 - 16 * t:256 - 16 * t], rm(3 * t + 2) if h else col(36 + t),
+               ["F2a", "F2b", "w36", "RM"], ["XW%d" % (2 * t + h)], "s" if t else "v")
 
     def slots(t, z, lo, zr):
-        for k in range(2):
-            to_w(T.pz[:, 64 + 32 * k:96 + 32 * k], T.XW, 2 * t + k, z, lo, lo + 512, True, True,
-                 ["XW%d" % (2 * t + k), zr], ["pz"])
+        for k, bank in enumerate(("pz", "pw")):
+            to_w(T[bank][:, 96:128], T.XW, 2 * t + k, z, lo, lo + 512, True, True, ["XW%d" % (2 * t + k), zr], [bank])
 
     def convert(k):
         a, b, bank = PARTS[k]
-        u, out = slice(a, b), T[bank][:, 0:b - a]
+        u, out = slice(a, b), T[bank][:] if b - a == 512 else T[bank][:, 0:b - a]
         mm(out, T.idf[:], T.Kr[:, u], False, False, ["idf", "Kr%d" % k], [bank])
         ts(T.cf[:, u], T.Kr[:, u], 2.0 ** -11, 1279.5 + 2.0 ** -12, A.mult, A.add, ["Kr%d" % k], ["cf%d" % k])
         mm(out, blk(T.ID, 1), T.cf[:, u], False, False, ["ID1", "cf%d" % k], [bank])
         mm(out, blk(T.ID, 3), T.cf[:, u], False, True, ["ID3", "cf%d" % k], [bank])
         act(T.K[:, u], out, [bank], ["K0a", "K0b"] if k == 0 else ["K%d" % k], bias=-0.625)
 
-    def tri(e, rs):
-        for r in rs:
-            scaled(e, blk(T.TR, r), blk(T.ID, 0), T.LT[:, r:r + 1], ["ID0", "LT"], ["TR%d" % r])
-
     def masks(t, m):
         xi, xr = T["xi%d" % t], "xi%d" % t
         if m == 1:
             act(T.m1[:], T.T1[:].indirect(xi[:, 0:32]), ["T1", xr], ["m1"])
         else:
-            act(T.m2[:], T.RM[:].indirect(xi[:, 32:64]), ["RM", xr], ["m2"])
+            act(T.m2[:], T.RM[:].indirect(xi[:, 32:64]), ["RM", "s" + xr], ["m2"])
 
     PARTS = ((0, 512, "pk"), (512, 1024, "ph"), (1024, 1536, "pU"), (1536, 1792, "pL"), (1792, 2048, "pb"))
     KC = ["K0a", "K0b", "K1", "K2", "K3", "K4"]
@@ -266,92 +265,114 @@ def rank_program(g, core, T, topo):
     dma("y", T.H[:, 2048:2560], T.zin[:], [], ["H0"])
     for k, (a, b, bank) in enumerate(PARTS):
         dma("y", T.Kr[:, a:b], T.nkey[:, a:b], [], ["Kr%d" % k])
-    add("v", lambda: V.memset(T.nil[:], 0.0), [], ["nil"])
     iota(T.ip[:], [[0, 1]], 0, 1, ["ip"], flag=False)
     iota(T.ix[:, 0:16], [[1, 16]], 0, 0, ["ix0"])
     iota(T.ix[:, 16:256], [[1, 240]], 16, 0, ["ix1"])
-    iota(T.ilo[:], [[0, 16], [1, 16]], 0, 0, ["ilo"])
-    iota(T.ib[:], [[16, 8], [0, 16]], 0, 0, ["ib"])
+    add("v", lambda: V.memset(T.nil[:], 0.0), [], ["nil"])
     diag(blk(T.ID, 2), DIAG[2], "ID2")
-    iota(T.ihi[:], [[1, 16], [0, 16]], 0, 0, ["ihi"])
     diag(T.idf[:], 1.0, "idf")
-    for k in (1, 3, 0):
+    iota(T.ilo[:], [[0, 16], [1, 16]], 0, 0, ["ilo"])
+    for k in (1, 3):
         diag(blk(T.ID, k), DIAG[k], "ID%d" % k)
+    iota(T.ib[:], [[16, 8], [0, 16]], 0, 0, ["ib"])
+    iota(T.ihi[:], [[1, 16], [0, 16]], 0, 0, ["ihi"])
+    diag(blk(T.ID, 0), DIAG[0], "ID0")
     iota(T.iw[:], [[16, 128]], 2048, 0, ["iw"])
-    for k in (4, 5, 6):
+    iota(T.iw2[:], [[16, 32], [0, 2]], 2048, 0, ["iw2"])
+    diag(blk(T.ID, 4), DIAG[4], "ID4")
+    NG = 12
+    trg, TRG = T.TR[:, 0:128 * NG], ["TR%d" % r for r in range(NG)]
+    iota(trg, [[-8192, NG], [0, 8], [8192, 16]], -4096, 0, TRG)
+    add("g", lambda: g.affine_select(trg, trg, [[-1, NG], [0, 8], [1, 16]], A.is_ge, 0.0, 0, 0), TRG, TRG)
+    add("g", lambda: g.affine_select(trg, trg, [[0, NG], [-1, 128]], A.is_equal, 0.0, 0, 1), TRG, TRG)
+    for k in (5, 6):
         diag(blk(T.ID, k), DIAG[k], "ID%d" % k)
     ts(T.pm[:], T.ip[:], 15, None, A.bitwise_and, None, ["ip"], ["pm"])
     cp(T.pf[:], T.ip[:], ["ip"], ["pf"])
     cp(T.pc[:], T.pm[:], ["pm"], ["pc"])
+    add("v", lambda: V.memset(T.Wd[:], 0.0), [], ["Wd"])
     ts(T.RM[:], T.ix[:, 0:16], T.pc[:], None, A.is_equal, None, ["ix0", "pc"], ["RM"])
     tt(T.g16[:], T.pf[:], T.pc[:], A.subtract, ["pf", "pc"], ["g16"])
     tt(T.WC[:, 28:30], T.RM[:, 1:3], T.RM[:, 3:5], A.add, ["RM"], ["w28"])
-    ts(T.WC[:, 32:36], T.RM[:, 1:12:3], 16.0, None, A.mult, None, ["RM"], ["w32"])
-    ts(col(14), col(28), 32.0, None, A.mult, None, ["w28"], ["w14"])
+    scaled(T.WC[:, 32:36], T.RM[:, 1:12:3], 16.0, ["RM"], ["w32"])
+    add("v", lambda: V.memset(T.one[:], 1280.0), [], ["one"])
+    scaled(col(14), col(28), 32.0, ["w28"], ["w14"])
     ts(T.WB[:], T.ix[:, 0:8], col(29), 32.0, A.mult, A.mult, ["ix0", "w28"], ["WB"])
     tt(T.WC[:, 36:40], T.WC[:, 32:36], T.RM[:, 0:12:3], A.add, ["w32", "RM"], ["w36"])
-    for b in range(8):
-        act(T.M[:, 256 * b:256 * b + 256], T.ix[:], IX + ["w14", "WB"], ["Mp%d" % b], func=F.Silu, scale=col(14),
-            bias=T.WB[:, b:b + 1])
-    add("v", lambda: V.memset(T.one[:], 1280.0), [], ["one"])
+    weights(0, "s")
+    weights(1, "s")
+    for a, b, bank in PARTS:
+        mm(T[bank][:] if b - a == 512 else T[bank][:, 0:b - a], blk(T.ID, 2), T.one[:, 0:b - a], True, False,
+           ["ID2", "one"], [bank])
     for h in range(2):
         ts(blk(T.F2, h), T.ix[:, 0:128], T.g16[:], None, A.is_equal, None, IX + ["g16"], ["F2" + "ab"[h]])
-    weights("v", "key")
-    xw(0, "v")
+    for b in range(2):
+        ts(T.M[:, 256 * b:256 * b + 256], T.ix[:], col(14), T.WB[:, b:b + 1], A.mult, A.add, IX + ["w14", "WB"],
+           ["Mp%d" % b])
+    for b in (1, 2, 3):
+        act(T.M[:, 512 * b:512 * b + 512], T.M[:, 0:512], ["Mp0", "Mp1", "WB"], ["Mp%d" % (b + 1)], func=F.Silu,
+            bias=T.WB[:, 2 * b:2 * b + 1])
+    xw(0, 0)
+    xw(0, 1)
+    slots(0, T.H, 2048, "H0")
+    scaled(T.cm[:], T.ci[:], 32.0, ["ci"], ["cm0"])
+    dma("y", T.M[0:128:16, 0:2048], T.cm[:], ["cm0"] + ["Mp%d" % b for b in range(5)], ["M"])
     cp(T.F1[:], T.F2[:, 112:256], ["F2a", "F2b"], ["F1"])
     ts(T.T0[:], T.ilo[:], T.pc[:], None, A.is_equal, None, ["ilo", "pc"], ["T0"])
-    ts(T.cm[:], T.ci[:], 32.0, None, A.mult, None, ["ci"], ["cm0"])
-    dma("s", T.M[0:128:16, 0:2048], T.cm[:], ["cm0"] + ["Mp%d" % b for b in range(8)], ["M"])
-    slots(0, T.H, 2048, "H0")
-    for a, b, bank in PARTS:
-        mm(T[bank][:, 0:b - a], blk(T.ID, 2), T.one[:, 0:b - a], True, False, ["ID2", "one"], [bank])
+    ts(T.LT[:], T.ix[:, 0:16], T.pc[:], None, A.is_lt, None, ["ix0", "pc"], ["LT"])
+    weights(2, "v")
+    tt(T.LT[:], T.LT[:], T.RM[:], A.subtract, ["LT", "RM"], ["LT"])
+    convert(0)
+    cp(T.xi0[:, 0:32], T.pz[:, 96:128], ["pz"], ["xi0"])
+    cp(T.xi0[:, 32:64], T.pw[:, 96:128], ["pw"], ["sxi0"])
     ts(T.BB[:], T.ib[:], T.g16[:], None, A.is_equal, None, ["ib", "g16"], ["BB"])
     for k, c in enumerate((W0, W1, 1.0)):
         ts(blk(T.BF, k), T.ib[:], T.g16[:], c, A.is_equal, A.mult, ["ib", "g16"], ["BF%d" % k])
     ts(T.T1[:], T.ihi[:], T.pc[:], None, A.is_equal, None, ["ihi", "pc"], ["T1"])
-    for k, c in enumerate((-W0, -W1)):
-        ts(blk(T.CW, k), T.BB[:], wcol("key"), c, A.mult, A.mult, ["BB", "key"], ["CW%d" % k])
-    cp(T.xi0[:], T.pz[:, 64:128], ["pz"], ["xi0"])
-    masks(0, 1)
-    convert(0)
-    masks(0, 2)
-    ts(T.LT[:], T.ix[:, 0:16], T.pc[:], None, A.is_lt, None, ["ix0", "pc"], ["LT"])
-    cp(T.FL[:], T.ix[:, 0:32], IX, ["FL"])
-    tt(T.LT[:], T.LT[:], T.RM[:], A.subtract, ["LT", "RM"], ["LT"])
-    scaled("v", blk(T.CW, 2), T.BB[:], wcol("key"), ["BB", "key"], ["CW2"])
-    ts(T.LT[:], T.LT[:], 4096.0, None, A.mult, None, ["LT"], ["LT"])
-    ts(T.own[:], T.iw[:], T.pc[:], None, A.add, None, ["iw", "pc"], ["own"])
-    scaled("v", wide(T.FW, 1), T.F1[:], -8192.0, ["F1"], ["FW1"])
     convert(1)
-    for name in ("hcol", "last", "step", "keep"):
-        weights("s", name)
-    dma("y", T.H[:, 0:2048], T.xreg[:], ["Kr1"], ["Hx"])
+    masks(0, 1)
+    dma("y", T.H[:, 0:2048], T.xreg[:], ["Kr2"], ["Hx"])
+    for k, c in enumerate((-W0, -W1, 1.0)):
+        ts(blk(T.CW, k), T.BB[:], wcol("key"), c, A.mult, A.mult, ["BB", "key"], ["CW%d" % k])
+    cp(T.FL[:], T.ix[:, 0:64:2], IX, ["FL"])
+    scaled(T.WC[:, 8:10], T.RM[:, 1:3], 32.0, ["RM"], ["w8"])
+    scaled(blk(T.CW, 3), T.BB[:], wcol("last"), ["BB", "last"], ["CW3"])
+    convert(2)
+
+    def tri(e, rs):
+        for r in rs:
+            scaled(blk(T.TR, r), blk(T.ID, 4), T.LT[:, r:r + 1], ["ID4", "LT"], ["TR%d" % r], e)
 
     def setup_rest():
-        convert(4)
-        tri("v", range(12))
-        scaled("v", blk(T.CW, 3), T.BB[:], wcol("last"), ["BB", "last"], ["CW3"])
-        scaled("v", wide(T.FW, 0), T.F1[:], wcol("hcol"), ["F1", "hcol"], ["FW0"])
+        ts(T.own[:], T.iw[:], T.pc[:], None, A.add, None, ["iw", "pc"], ["own"])
+        for k, c in enumerate((wcol("hcol"), -8192.0)):
+            scaled(wide(T.FW, k), T.F1[:], c, ["F1", "hcol"], ["FW%d" % k])
+        scaled(T.WC[:, 16:18], T.ix[:, 0:2], col(9), ["ix0", "w8"], ["wb"])
 
     def setup_scalar(m):
-        if m == 0:
-            scaled("s", T.WC[:, 8:10], T.RM[:, 1:3], 32.0, ["RM"], ["w8"])
-            scaled("s", T.Ssel[:], blk(T.ID, 0), wcol("keep"), ["ID0", "keep"], ["Ssel"])
-            scaled("s", T.WC[:, 16:18], T.ix[:, 0:2], col(9), ["ix0", "w8"], ["wb"])
-            scaled("s", T.WC[:, 20:24], T.ix[:, 8:16:2], col(9), ["ix0", "w8"], ["wt"])
         if m == 1:
-            tri("s", range(12, 16))
+            tri("s", range(NG, NG + 2))
         if m == 2:
-            for b in range(2):
-                act(T.Con[:, 256 * b:256 * b + 256], T.ix[:], IX + ["w8", "wb"], ["Con%d" % b], scale=col(8),
-                    bias=col(16 + b))
-        if m == 2:
-            act(T.NT[:, 0:8:2], T.RM[:, 0:4], ["RM"], ["NT0"], scale=-1.0, bias=1.0)
-            act(T.NT[:, 1:8:2], T.RM[:, 0:4], ["RM"], ["NT1"], scale=0.0, bias=1.0)
-            scaled("s", wide(T.FW, 2), T.F1[:], wcol("key"), ["F1", "key"], ["FW2"])
+            tri("s", range(NG + 2, 16))
+        if m == 3:
+            for h in range(2):
+                act(T.Con[:, 256 * h:256 * h + 256], T.ix[:], IX + ["w8", "wb"], ["Con%d" % h], scale=col(8),
+                    bias=col(16 + h))
+
+    def setup_pause():
+        for h in range(2):
+            ts(T.NT[:, h:8:2], T.RM[:, 0:4], h - 1.0, 1.0, A.mult, A.add, ["RM"], ["NT%d" % h])
+        ts(T.own2[:], T.iw2[:], T.pc[:], None, A.add, None, ["iw2", "pc"], ["own2"])
+        scaled(T.Ssel[:], blk(T.ID, 0), wcol("keep"), ["ID0", "keep"], ["Ssel"])
+        scaled(T.WC[:, 20:24], T.ix[:, 8:16:2], col(9), ["ix0", "w8"], ["wt"])
+        scaled(wide(T.FW, 2), T.F1[:], wcol("key"), ["F1", "key"], ["FW2"])
+
+    setup_pause()
 
     sent = 0
     HALF = (slice(0, 256), slice(256, 512))
+    nb = 32 // NB
+    AA = ["Aa%d" % c for c in range(nb)]
     for t in range(VISITS):
         last = t == VISITS - 1
         hz = slice(2048 + 512 * t, 2560 + 512 * t)
@@ -360,6 +381,7 @@ def rank_program(g, core, T, topo):
         y = T.pU[:, 0:32]
         if t > 0:
             add("x", None, [], [xr], kind="x", sem="ax%d" % t, n=n_in)
+            add("x", None, [], ["s" + xr], kind="x", sem="as%d" % t, n=n_in)
             add("x", None, [], ["zi%d" % t], kind="x", sem="az%d" % t, n=n_in)
             zi = T["zi%d" % t]
             dma("y", T.H[16 * t:128, hz], zi[0:128 - 16 * t, :], ["zi%d" % t], ["H%da" % t])
@@ -375,16 +397,16 @@ def rank_program(g, core, T, topo):
             Kh, Kf, C = T["Kh%d" % m], T["Kf%d" % m], T["C%d" % m]
             tt(Kh[:], src, mask, A.mult, rd, ["Kh%d" % m])
             if t == 0 and m == 0:
-                convert(2)
-            tt(Kf[:], src, mask, A.mult, rd, ["Kf%d" % m])
-            if t == 0 and m == 0:
                 convert(3)
+                convert(4)
+                masks(0, 2)
+            tt(Kf[:], src, mask, A.mult, rd, ["Kf%d" % m])
             pw = T.pw[:, 32 * m:32 * m + 32]
             to_w(pw, T.F1, 0, Kh, 0, 512, True, True, ["F1", "Kh%d" % m], ["pw"])
             o = T.off[:, 32 * m:32 * m + 32]
-            cp(o, pw, ["pw"], ["off%d" % m])
             if t == 0 and m == 0:
                 setup_rest()
+            cp(o, pw, ["pw"], ["off%d" % m])
             if m == 1:
                 mm(y, T.idf[:], T.own[:, 32 * t:32 * t + 32], True, False, ["idf", "own"], ["pU"])
             if m > 0:
@@ -399,114 +421,149 @@ def rank_program(g, core, T, topo):
                 act(C[:], T.M[:, 0:2048].indirect(o), ["M", "off2", "step"], ["C2"], bias=wcol("step"))
             if m == 0:
                 act(T.nm2[:], T.m2[:], ["m2"], ["nm2"], scale=-1.0, bias=1.0)
-            if m == 1 and not last:
-                xw(t + 1, "s")
-            if m == 1 and last:
-                scaled("s", col(10), rm(0), 1.0 / 32, ["RM"], ["w10"])
-                scaled("s", wide(T.FW, 3), T.F1[:], col(10), ["F1", "w10"], ["FW3"])
-            if t == 0:
-                setup_scalar(m)
-        ts(T.Wd[:], T.pw[:, 64:96], ROUND, ROUND - 4096.0, A.add, A.subtract, ["pw"], ["Wd"])
+            if m == 1 and t == 0:
+                setup_scalar(1)
+            if m < 2 and 0 < t < VISITS - 1:
+                xw(t + 1, m)
+
+        def old_keys(h):
+            u = HALF[h]
+            tt(T.Bb[:, u], T.K[:, 0:2048].indirect(T.off[:, 64 + 16 * h:80 + 16 * h]), T.nm2[:, u], A.mult,
+               KC + ["off2", "nm2"], ["Bb%d" % h])
+
+        ts(T.Wd[:, 0:64:2], T.pw[:, 64:96], ROUND, ROUND - 4096.0, A.add, A.subtract, ["pw"], ["Wd"])
         cp(T.Wb[:], T.Wd[:].indirect(T.FL[:]), ["Wd", "FL"], ["Wb"])
+        act(T.Wb3[:], T.Wb[:], ["Wb"], ["Wb3"])
+        old_keys(1)
         mm(T.pY[:], blk(T.CW, 3), T.C2[:], False, True, ["CW3", "C2"], ["pY"])
         to_w(T.pz[:, 0:32], T.FW, 0, T.C2, 0, 512, True, True, ["FW0", "C2"], ["pz"])
-        mm(T.ph[:, 0:32], T.idf[:], T.Wd[:], True, False, ["idf", "Wd"], ["ph"])
-        tt(T.Aa[:], T.pk[:], T.m2[:], A.mult, ["pk", "m2"], ["Aa"])
-        act(T.cw[:], T.pz[:, 0:32], ["pz"], ["cw"])
+        mm(T.ph[:, 0:8], T.idf[:], T.Wd[:], True, False, ["idf", "Wd"], ["ph"])
 
         def compare(k):
-            w = 512 - 16 * k
-            tt(T.E[:, 512 * k:512 * k + w], T.pY[:, 0:w], T.Wb[:, 16 * k:512], A.is_equal, ["pY", "Wb"], ["E%d" % k])
+            tt(T.E[:, 512 * k:512 * k + 512 - 128 * k], T.pY[:, :, 0:64 - 16 * k],
+               T.Wb[:] if k == 0 else T.Wb3[:, :, 16 * k:64], A.is_equal, ["pY", "Wb3" if k else "Wb"], ["E%d" % k])
 
         def count(k):
-            for r in range(16):
-                mm(T.ph[:, k:32], blk(T.TR, r) if k == 0 else blk(T.ID, 4), T.E[:, 512 * k + r:512 * k + 512 - 16 * k:16],
-                   False, k == NB - 1 and r == 15, ["TR%d" % r, "ID4", "E%d" % k], ["ph"])
+            for r in range(16 if k == 0 else 8):
+                if k == 0:
+                    mm(T.ph[:, 0:8, :, 0], blk(T.TR, r), T.E[:, r:512:16], False, False, ["TR%d" % r, "E0"], ["ph"])
+                else:
+                    mm(T.ph[:, 0:8, k:4, :], blk(T.ID, 4), T.E[:, 512 * k + r:512 * k + 512 - 128 * k:8], False,
+                       k == NB - 1 and r == 7, ["ID4", "E%d" % k], ["ph"])
 
+        def new_keys(c, end=None):
+            end = end or c + 1
+            u = slice(16 * NB * c, 16 * NB * end)
+            tt(T.Aa[:, u], T.pk[:, u], T.m2[:, u], A.mult, ["pk", "m2"], AA[c:end])
+
+        def new_state():
+            mm(T.pb[:], T.Ssel[:], T.C2[:], False, True, ["Ssel", "C2"], ["pb"])
+            act(T.S[:], T.pb[:], ["pb", "wt"], ["S"], bias=col(20 + t))
+
+        if t == 0:
+            setup_scalar(2)
+        act(T.cw[:], T.pz[:, 0:32], ["pz"], ["cw"])
+        if t:
+            new_state()
         compare(0)
         to_w(y, T.FW, 1, T.E, 0, 512, False, True, ["FW1", "E0"], ["pU"])
-        count(0)
-        compare(1)
-        count(1)
-        tt(T.zf[:], y, T.cw[:], A.max, ["pU", "cw"], ["zf"])
-        ts(T.offN[:], y, 0.0, 2.0 * t, A.is_ge, A.add, ["pU"], ["offN"])
-        cp(T.zoff[:], T.zf[:], ["zf"], ["zoff"])
+        if last:
+            act(col(11), rm(0), ["RM"], ["w11"], scale=-31.0 / 32, bias=1.0)
+        if t == 0:
+            xw(1, 0)
+            xw(1, 1)
+        for k in range(NB):
+            if k:
+                compare(k)
+            count(k)
+            if k == 2:
+                tt(T.zf[:], y, T.cw[:], A.max, ["pU", "cw"], ["zf"])
+                ts(T.offN[:], y, 0.0, 2.0 * t, A.is_ge, A.add, ["pU"], ["offN"])
+                cp(T.zoff[:], T.zf[:], ["zf"], ["zoff"])
+        old_keys(0)
+        new_keys(5, nb)
         zo, zr = T["zo%d" % t], "zo%d" % t
         act(zo[:], T.H[:, 0:hz.stop].indirect(T.zoff[:]), HALL + ["zoff"], [zr])
-        act(T.NM[:], T.NT[:].indirect(T.offN[:]), ["NT0", "NT1", "offN"], ["NM"])
         if last:
             dma("y", T.yz[:], zo[:], [zr], [])
-        for k in range(2, NB):
-            compare(k)
-            count(k)
-        if not last:
+        else:
             slots(t + 1, zo, 0, zr)
-        mm(T.pb[:], T.Ssel[:], T.C2[:], True, False, ["Ssel", "C2"], ["pb"])
-        mm(T.pb[:], blk(T.ID, 0), T.Con[:], False, True, ["ID0", "Con0", "Con1"], ["pb"])
-        act(T.S[:], T.pb[:], ["pb", "wt"], ["S"], bias=col(20 + t))
-        tt(T.Bb[:], T.K[:, 0:2048].indirect(T.off[:, 64:96]), T.nm2[:], A.mult, KC + ["off2", "nm2"], ["Bb"])
-        tt(T.sf[:], T.ph[:, 0:32], T.own[:, 0:32], A.min, ["ph", "own"], ["sf"])
+        if t == 0:
+            send(T.zi1[:], zo[:], "az1", [zr])
+            setup_scalar(3)
+            mm(T.pb[:], blk(T.ID, 0), T.Con[:], True, False, ["ID0", "Con0", "Con1"], ["pb"])
+        act(T.NM[:], T.NT[:].indirect(T.offN[:]), ["NT0", "NT1", "offN"], ["NM"])
+        if t == 0:
+            new_state()
+        tt(T.sm[:], T.ph[:, 0:8], T.own2[:], A.min, ["ph", "own2"], ["sm"])
+        new_keys(4)
+        tt(T.sf[:], T.sm[:, 0:64:2], T.sm[:, 1:64:2], A.max, ["sm"], ["sf"])
+        new_keys(3)
         cp(T.soff[:], T.sf[:], ["sf"], ["soff"])
+        new_keys(2)
+        if not last:
+            mm(T.pb[:], blk(T.ID, 0), T.Con[:], True, False, ["ID0", "Con0", "Con1"], ["pb"])
         for b, w in (("pU", 5), ("pL", 6)):
             mm(T[b][:], band(T.FW, 2, t), T.C2[:], True, False, ["FW2", "C2"], [b])
             mm(T[b][:], blk(T.ID, w), T.NM[:], False, True, ["ID%d" % w, "NM"], [b])
-        nb = 32 // NB
+        todo = [0, 1]
         for c in range(nb - 1, -1, -1):
             u = slice(16 * NB * c, 16 * NB * (c + 1))
             o = T.soff[:, NB * c:NB * (c + 1)]
-            tt(T.K[:].indirect(o), T.Aa[:, u], T.Bb[:, u], A.add, ["soff", "Aa", "Bb"], KC)
+            tt(T.K[:].indirect(o), T.Aa[:, u], T.Bb[:, u], A.add, ["soff", AA[c], "Bb0", "Bb1"], KC)
             act(T.M[:].indirect(o), T.S[:, u], ["soff", "S"], ["M"], func=F.Silu)
-            if c == nb - 1 - 8 // NB + 1 and not last:
-                xo = T["xo%d" % (t + 1)]
-                cp(xo[:], T.pz[:, 64:128], ["pz"], ["xo"])
-                send(T["xi%d" % (t + 1)][:], xo[:], "ax%d" % (t + 1), ["xo"])
-                send(T["zi%d" % (t + 1)][:], zo[:], "az%d" % (t + 1), [zr])
-                sent += 2 * len(topo.engines(core, nxt))
+            if c == nb - 1 and not last:
+                xo, xn = T["xo%d" % (t + 1)], T["xi%d" % (t + 1)]
+                cp(xo[:, 0:32], T.pz[:, 96:128], ["pz"], ["xo"])
+                send(xn[:, 0:32], xo[:, 0:32], "ax%d" % (t + 1), ["xo"])
+            elif c == nb - 3 and not last:
+                cp(xo[:, 32:64], T.pw[:, 96:128], ["pw"], ["so"])
+                send(xn[:, 32:64], xo[:, 32:64], "as%d" % (t + 1), ["so"])
+                if t:
+                    send(T["zi%d" % (t + 1)][:], zo[:], "az%d" % (t + 1), [zr])
+                sent += 3 * len(topo.engines(core, nxt))
+            elif todo:
+                new_keys(todo.pop())
         if last:
             mm(T.pk[:], T.idf[:], T.K[:, 512:1024], True, False, ["idf", "K1"], ["pk"])
-            for h in (0, 1):
-                act(T.Mb[:, 512 * h:512 * h + 512], T.M[:, 512 * h:512 * h + 512], ["M"], ["Mb%d" % h])
+            act(T.Mb[:, 1024:2048], T.M[:, 1024:2048], ["M", "w11"], ["Mb2", "Mb3"], scale=col(11))
+            for h in range(2):
+                u = slice(512 * h, 512 * h + 512)
+                scaled(T.Mb[:, u], T.M[:, u], col(11), ["M", "w11"], ["Mb%d" % h])
         for b, op in (("pU", A.min), ("pL", A.max)):
             for h, u in zip("ab", HALF):
                 tt(T.K[:, u], T.K[:, u], T[b][:, u], op, ["K0" + h, b], ["K0" + h])
-            if last:
-                h = 2 if b == "pU" else 3
-                cp(T.Mb[:, 512 * h:512 * h + 512], T.M[:, 512 * h:512 * h + 512], ["M"], ["Mb%d" % h])
-    order = [0, 1, 2, 3, 8, 9, 10, 11, 4, 5, 6, 7, 12, 13, 14, 15]
-    for b in order:
-        mm(T.pz[:, 0:128], band(T.FW, 0, b), blk(T.Mb, b), b == 0, b == 15, ["FW0", "Mb%d" % (b // 4)], ["pz"])
-    cp(T.fo[:], T.pz[:, 0:128], ["pz"], ["fo"])
-    mm(T.pk[:], T.idf[:], T.K[:, 1536:2048], False, True, ["idf", "K3", "K4"], ["pk"])
-    tt(T.Aa[:], T.K[:, 0:512], T.K[:, 1024:1536], A.add, KC, ["Aa"])
-    HALL = ["Hx", "H0"] + ["H%d%s" % (k, h) for k in range(1, 4) for h in "ab"]
-    GS = ((0, 48, "s", "pU"), (48, 96, "s", "ph"), (96, 128, "s", "pL"))
-    for k, (a, b, e, bank) in enumerate(GS):
-        (act if e == "s" else cp)(T.G[:, 16 * a:16 * b], T.H[:].indirect(T.fo[:, a:b]), HALL + ["fo"], ["G%d" % k])
+    add("g", lambda: g.dma_start(T.yc[:], T.Mb[0:128:16, :]), ["Mb%d" % h for h in range(4)], [], kind="d")
     for b in range(16):
-        mm(T.pb[:, 0:128], band(T.FW, 3, b), blk(T.Mb, b), b == 0, b == 15, ["FW3", "Mb%d" % (b // 4)], ["pb"])
+        mm(T.pz[:, 0:128], band(T.FW, 0, b), blk(T.Mb, b), b == 0, b == 15, ["FW0", "Mb%d" % (b // 4)], ["pz"])
+    mm(T.pk[:], T.idf[:], T.K[:, 1024:1536], False, False, ["idf", "K2"], ["pk"])
+    mm(T.pk[:], T.idf[:], T.K[:, 1536:2048], False, True, ["idf", "K3", "K4"], ["pk"])
+    cp(T.fo[:], T.pz[:, 0:128], ["pz"], ["fo"])
+    HALL = ["Hx", "H0"] + ["H%d%s" % (k, h) for k in range(1, 4) for h in "ab"]
 
-    def gsum(k):
-        a, b, e, bank = GS[k]
-        for r in range(16):
-            mm(T[bank][:, 0:b - a], blk(T.ID, 0), T.G[:, 16 * a + r:16 * b:16], r == 0, r == 15,
-               ["ID0", "G%d" % k], [bank])
+    def regs(e, a, b):
+        (act if e == "s" else cp)(T.G[:, 16 * a:16 * b], T.H[:].indirect(T.fo[:, a:b]), HALL + ["fo"], ["G%d" % a])
 
-    tt(T.pY[:], T.pk[:], T.Aa[:], A.add, ["pk", "Aa"], ["pY"])
-    ts(T.Bb[:], T.pY[:], ROUND, ROUND, A.add, A.subtract, ["pY"], ["Bb"])
-    tt(T.Kh0[:], T.pY[:], T.Bb[:], A.subtract, ["pY", "Bb"], ["Kh0"])
-    cp(T.oc[:], T.pb[:, 0:128], ["pb"], ["oc"])
-    dma("y", T.yc[:], T.oc[:], ["oc"], [])
-    gsum(0)
+    def gsum(a, b, bank, r):
+        for j in range(16):
+            mm(T[bank][:, 0:b - a], blk(T.ID, 0), T.G[:, 16 * a + j:16 * b:16], j == 0, j == 15, ["ID0"] + r, [bank])
+
+    regs("s", 0, 72)
+    regs("v", 72, 128)
+    gsum(0, 128, "pU", ["G0", "G72"])
+    act(T.ox[:], T.pU[:, 0:128], ["pU"], ["ox"])
+    dma("s", T.yx[:], T.ox[:], ["ox"], [])
+    for h, u in enumerate(HALF):
+        tt(T.pL[:, u], T.pk[:, u], T.K[:, u], A.add, ["pk", "K0" + "ab"[h]] + ["pL"] * h, ["pL"] * (1 - h) + ["s%d" % h])
+    for h, u in enumerate(HALF):
+        ts(T.Bb[:, u], T.pL[:, u], ROUND, ROUND, A.add, A.subtract, ["s%d" % h], ["Bb%d" % h])
+    for h, u in enumerate(HALF):
+        tt(T.Kh0[:, u], T.pL[:, u], T.Bb[:, u], A.subtract, ["s%d" % h, "Bb%d" % h], ["Kh0"] * (1 - h) + ["f%d" % h])
     for b in range(4):
-        mm(T.pw[:, 0:128], T.idf[:], blk(T.Bb, b), b == 0, False, ["idf", "Bb"], ["pw"])
-    gsum(1)
+        mm(T.pw[:, 0:128], T.idf[:], blk(T.Bb, b), b == 0, False, ["idf", "Bb%d" % (b // 2)], ["pw"])
     for b in range(4):
-        mm(T.pw[:, 0:128], blk(T.ID, 5), blk(T.Kh0, b), False, b == 3, ["ID5", "Kh0"], ["pw"])
+        mm(T.pw[:, 0:128], blk(T.ID, 5), blk(T.Kh0, b), False, b == 3, ["ID5", "f%d" % (b // 2)], ["pw"])
     cp(T.ok_[:], T.pw[:, 0:128], ["pw"], ["ok_"])
     dma("y", T.yk[:], T.ok_[:], ["ok_"], [])
-    gsum(2)
-    for k, (a, b, e, bank) in enumerate(GS):
-        act(T.ox[:, a:b], T[bank][:, 0:b - a], [bank], ["ox%d" % k])
-    dma("s", T.yx[:], T.ox[:], ["ox0", "ox1", "ox2"], [])
     emit(g, T, ops)
     g.wait_ge(T.sem.snt, sent)

from concourse.mybir import AluOpType as A, ActivationFunctionType as F

f32, bf, f16, i32, u16 = "float32", "bfloat16", "float16", "int32", "uint16"
SCRATCH = {
    "Kr": ("sbuf", [128, 2048], f32), "cf": ("sbuf", [128, 2048], f16),
    "K": ("sbuf", [128, 2560], f32), "H": ("sbuf", [128, 4096], bf), "M": ("sbuf", [128, 2560], f32),
    "Mb": ("sbuf", [128, 2048], bf), "G": ("sbuf", [128, 2048], bf),
    "zi1": ("sbuf", [128, 512], bf), "zi2": ("sbuf", [128, 512], bf), "zi3": ("sbuf", [128, 512], bf),
    "zo0": ("sbuf", [128, 512], bf), "zo1": ("sbuf", [128, 512], bf), "zo2": ("sbuf", [128, 512], bf),
    "zo3": ("sbuf", [128, 512], bf),
    "xi0": ("sbuf", [128, 64], u16), "xi1": ("sbuf", [128, 64], u16), "xi2": ("sbuf", [128, 64], u16),
    "xi3": ("sbuf", [128, 64], u16),
    "xo1": ("sbuf", [128, 64], u16), "xo2": ("sbuf", [128, 64], u16), "xo3": ("sbuf", [128, 64], u16),
    "m1": ("sbuf", [128, 512], f32), "m2": ("sbuf", [128, 512], f32), "nm2": ("sbuf", [128, 512], f32),
    "Kh0": ("sbuf", [128, 512], f16), "Kh1": ("sbuf", [128, 512], f16), "Kh2": ("sbuf", [128, 512], f16),
    "Kf0": ("sbuf", [128, 512], f32), "Kf1": ("sbuf", [128, 512], f32), "Kf2": ("sbuf", [128, 512], f32),
    "C0": ("sbuf", [128, 512], bf), "C1": ("sbuf", [128, 512], bf), "C2": ("sbuf", [128, 512], bf),
    "Aa": ("sbuf", [128, 512], f32), "Bb": ("sbuf", [128, 512], f32), "S": ("sbuf", [128, 512], f32),
    "Wb": ("sbuf", [128, 512], f32), "E": ("sbuf", [128, 2048], bf), "NM": ("sbuf", [128, 512], bf),
    "Wb3": ("sbuf", [128, 8, 64], f32), "sm": ("sbuf", [128, 64], f32), "own2": ("sbuf", [128, 64], f32),
    "off": ("sbuf", [128, 96], u16), "Wd": ("sbuf", [128, 64], f32), "cw": ("sbuf", [128, 32], f32),
    "zf": ("sbuf", [128, 32], f32), "zoff": ("sbuf", [128, 32], u16), "offN": ("sbuf", [128, 32], u16),
    "sf": ("sbuf", [128, 32], f32), "soff": ("sbuf", [128, 32], u16), "FL": ("sbuf", [128, 32], u16),
    "ip": ("sbuf", [128, 1], i32), "pm": ("sbuf", [128, 1], i32), "pf": ("sbuf", [128, 1], f32),
    "pc": ("sbuf", [128, 1], f32), "g16": ("sbuf", [128, 1], f32),
    "ix": ("sbuf", [128, 256], f32), "ib": ("sbuf", [128, 128], bf), "ilo": ("sbuf", [128, 256], bf),
    "ihi": ("sbuf", [128, 256], bf), "iw": ("sbuf", [128, 128], f32), "own": ("sbuf", [128, 128], f32),
    "RM": ("sbuf", [128, 16], f32), "LT": ("sbuf", [128, 16], f32), "WC": ("sbuf", [128, 40], f32),
    "T0": ("sbuf", [128, 256], bf), "T1": ("sbuf", [128, 256], bf), "F2": ("sbuf", [128, 256], bf),
    "F1": ("sbuf", [128, 144], bf), "nil": ("sbuf", [128, 128], f32), "iw2": ("sbuf", [128, 64], f32),
    "BB": ("sbuf", [128, 128], bf), "BF": ("sbuf", [128, 384], f32), "CW": ("sbuf", [128, 512], bf),
    "idf": ("sbuf", [128, 128], f32), "ID": ("sbuf", [128, 896], bf), "XW": ("sbuf", [128, 1152], bf),
    "FW": ("sbuf", [128, 432], bf), "TR": ("sbuf", [128, 2048], bf), "Ssel": ("sbuf", [128, 128], bf),
    "Con": ("sbuf", [128, 512], bf), "one": ("sbuf", [128, 512], bf),
    "ci": ("sbuf", [128, 128], i32), "cm": ("sbuf", [128, 128], f32),
    "WB": ("sbuf", [128, 8], f32), "NT": ("sbuf", [128, 8], f32),
    "fo": ("sbuf", [128, 128], u16), "ok_": ("sbuf", [128, 128], f32), "ox": ("sbuf", [128, 128], bf),
    "pw": ("psum", [128, 512], f32), "pz": ("psum", [128, 512], f32), "pY": ("psum", [128, 8, 64], f32),
    "pk": ("psum", [128, 512], f32), "ph": ("psum", [128, 64, 4, 2], f32), "pb": ("psum", [128, 512], f32),
    "pU": ("psum", [128, 512], f32), "pL": ("psum", [128, 512], f32),
}
NDMA = 24
SEMAPHORES = (["sv", "ss", "sp", "sg", "snt"] + ["a%s%d" % (k, t) for k in "xsz" for t in (1, 2, 3)]
              + ["d%d" % k for k in range(NDMA)])
BANKS = ("pw", "pz", "pY", "pk", "ph", "pb", "pU", "pL")
VISITS = 4
NB = 4
ROUND = 1.5 * 2.0 ** 23
W0, W1 = 2.0 ** 35, 2.0 ** 25
DIAG = {0: 1.0, 1: -2048.0, 2: 2048.0, 3: 2.0 ** -11, 4: 4096.0, 5: 2.0 ** 22, 6: -2.0 ** 22}
COLS = {
    "hcol": {1: 1 / 32, 2: 8.0},
    "key": {0: 2.0 ** -16, 3: 1 / 32, 4: 8.0},
    "last": {0: -2.0 ** -16, 5: 4096.0, 6: 2.0 ** -11},
    "step": {0: 32.0, 5: 1.0, 6: 1.0},
    "keep": {0: 1.0, 3: 1.0, 4: 1.0},
}


def route(T, topo, r):
    src, dst = T.cores[r], T.cores[(r + 1) % len(T.cores)]
    if topo.may_write(src, dst):
        return [src, dst]
    cand = [c for c in topo.cores_of(src) if T.rank_of(c) is None and topo.may_write(c, dst)]
    near = [c for c in cand if topo.die(c) == topo.die(src)]
    return [src, (near or cand)[0], dst]


def emit(g, T, ops):
    q = {"v": g.vector, "s": g.scalar, "p": g.tensor, "g": g, "y": g.sync}
    writer, readers, known = {}, {}, {e: {} for e in q}
    count = {e: 0 for e in q}
    ndma = [0]
    for o in ops:
        e = o["e"]
        deps = []
        for r in o["r"]:
            deps += writer.get(r, [])
            if r in BANKS:
                deps += [x for x in readers.get(r, []) if x["e"] != e]
        for w in o["w"]:
            deps += [x for x in writer.get(w, []) + readers.get(w, []) if x["e"] != "p" or e != "p"]
        waits = []
        if o["kind"] != "x":
            kn = known[e]
            deps.sort(key=lambda x: -x["pos"])
            for x in deps:
                k, n = x["tok"]
                if kn.get(k, 0) >= n:
                    continue
                waits.append(x)
                x["need"] = True
                for kk, nn in x["clock"].items():
                    kn[kk] = max(kn.get(kk, 0), nn)
        o["waits"] = waits
        if o["kind"] == "c":
            count[e] += 1
            o["tok"] = (e, count[e])
        elif o["kind"] == "d":
            o["tok"] = ("d%d" % ndma[0], 1)
            ndma[0] += 1
        elif o["kind"] == "x":
            o["tok"] = (o["sem"], 1)
        else:
            o["tok"] = ("none", 0)
        o["clock"] = {} if o["kind"] == "x" else dict(known[e])
        o["clock"][o["tok"][0]] = o["tok"][1]
        for r in o["r"]:
            readers.setdefault(r, []).append(o)
        for w in o["w"]:
            writer[w] = [o]
            readers[w] = []
    run = {e: 0 for e in q}
    for o in ops:
        if o["kind"] == "c" and o.get("need"):
            run[o["e"]] += 1
            o["val"] = (T.sem["s" + o["e"]], run[o["e"]])
        elif o["kind"] == "d":
            o["val"] = (T.sem[o["tok"][0]], 16)
        elif o["kind"] == "x":
            o["val"] = (T.sem[o["sem"]], o["n"])
    for o in ops:
        if o["kind"] == "x":
            continue
        for x in o["waits"]:
            q[o["e"]].wait_ge(x["val"][0], x["val"][1])
        ins = o["fn"]()
        if o["kind"] == "d":
            ins.then_inc(o["val"][0], 16)
        elif o["kind"] == "c" and o.get("need"):
            ins.then_inc(o["val"][0], 1)
    for o in ops:
        if o["kind"] == "d" and not o.get("need"):
            q[o["e"]].wait_ge(o["val"][0], 16)


def rank_program(g, core, T, topo):
    n = len(T.cores)
    rank = T.rank_of(core)
    if rank is None:
        for r in range(n):
            way = route(T, topo, r)
            if len(way) == 3 and way[1] == core:
                rid, pid = topo.addr(way[2], core)
                for t in range(1, VISITS):
                    xi, zi = T["xi%d" % t], T["zi%d" % t]
                    msgs = {"x": xi[:, 0:32], "s": xi[:, 32:64], "z": zi[:]}
                    for k in "xsz":
                        sem = T.sem["a%s%d" % (k, t)]
                        g.wait_ge(sem, len(topo.engines(way[0], core)))
                        g.remote_dma(msgs[k], msgs[k], sem, T.sem.snt, pid, rid, topo.mask(core, way[2]))
                g.wait_ge(T.sem.snt, 3 * (VISITS - 1) * len(topo.engines(core, way[2])))
        return
    nxt = route(T, topo, rank)[1]
    n_in = len(topo.engines(route(T, topo, (rank - 1) % n)[-2], core))
    V, S, P = g.vector, g.scalar, g.tensor
    ops = []

    def add(e, fn, r, w, kind="c", **kw):
        o = {"e": e, "fn": fn, "r": list(r), "w": list(w), "kind": kind, "pos": len(ops)}
        o.update(kw)
        ops.append(o)

    def ts(out, in0, s1, s2, o0, o1, r, w):
        if o1 is None:
            add("v", lambda: V.tensor_scalar(out, in0, s1, None, o0), r, w)
        else:
            add("v", lambda: V.tensor_scalar(out, in0, s1, s2, o0, o1), r, w)

    def tt(out, a, b, op, r, w):
        add("v", lambda: V.tensor_tensor(out, a, b, op), r, w)

    def cp(out, a, r, w):
        add("v", lambda: V.tensor_copy(out, a), r, w)

    def act(out, a, r, w, func=F.Identity, **kw):
        add("s", lambda: S.activation(out, a, func, **kw), r, w)

    def scaled(out, a, c, r, w, e="v"):
        if e == "v":
            ts(out, a, c, None, A.mult, None, r, w)
        else:
            act(out, a, r, w, scale=c)

    def diag(out, c, w):
        add("g", lambda: g.affine_select(out, T.nil[:], [[-1, 128]], A.not_equal, c, 0, 1), ["nil"], [w])

    def mm(out, l, rhs, st, sp, r, w):
        add("p", lambda: P.matmul(out, l, rhs, st, sp), r, w)

    def iota(out, pat, base, cm, w, flag=True):
        if flag:
            add("g", lambda: g.iota(out, pat, base, cm, allow_small_or_imprecise_dtypes=True), [], w)
        else:
            add("g", lambda: g.iota(out, pat, base, cm), [], w)

    def dma(e, out, in_, r, w):
        qq = g.sync if e == "y" else g.scalar
        add(e, lambda: qq.dma_start(out, in_), r, w, kind="d")

    def send(dst, src, sem, r):
        rid, pid = topo.addr(nxt, core)
        add("g", lambda: g.remote_dma(dst, src, T.sem[sem], T.sem.snt, pid, rid, topo.mask(core, nxt)), r, [], kind="r")

    def col(k):
        return T.WC[:, k:k + 1]

    def rm(k):
        return T.RM[:, k:k + 1]

    def wcol(name):
        return col(list(COLS).index(name))

    def weights(j, e):
        for name, terms in COLS.items():
            for row, c in list(terms.items())[j:j + 1]:
                if j == 0:
                    scaled(wcol(name), rm(row), c, ["RM"], [name], e)
                elif e == "v":
                    ts(wcol(name), rm(row), c, wcol(name), A.mult, A.add, ["RM", name], [name])
                else:
                    act(wcol(name), rm(row), ["RM", name], [name], scale=c, bias=wcol(name))

    def blk(buf, k):
        return buf[:, 128 * k:128 * k + 128]

    def wide(buf, k):
        return buf[:, 144 * k:144 * k + 144]

    def band(buf, k, r):
        return buf[:, 144 * k + 16 - r:144 * k + 144 - r]

    def to_w(out, buf, k, u, lo, hi, st, sp, r, w):
        for j in range(16):
            mm(out, band(buf, k, j), u[:, lo + j:hi:16], st and j == 0, sp and j == 15, r, w)

    def xw(t, h):
        scaled(wide(T.XW, 2 * t + h), T.F2[:, 112 - 16 * t:256 - 16 * t], rm(3 * t + 2) if h else col(36 + t),
               ["F2a", "F2b", "w36", "RM"], ["XW%d" % (2 * t + h)], "s" if t else "v")

    def slots(t, z, lo, zr):
        for k, bank in enumerate(("pz", "pw")):
            to_w(T[bank][:, 96:128], T.XW, 2 * t + k, z, lo, lo + 512, True, True, ["XW%d" % (2 * t + k), zr], [bank])

    def convert(k):
        a, b, bank = PARTS[k]
        u, out = slice(a, b), T[bank][:] if b - a == 512 else T[bank][:, 0:b - a]
        mm(out, T.idf[:], T.Kr[:, u], False, False, ["idf", "Kr%d" % k], [bank])
        ts(T.cf[:, u], T.Kr[:, u], 2.0 ** -11, 1279.5 + 2.0 ** -12, A.mult, A.add, ["Kr%d" % k], ["cf%d" % k])
        mm(out, blk(T.ID, 1), T.cf[:, u], False, False, ["ID1", "cf%d" % k], [bank])
        mm(out, blk(T.ID, 3), T.cf[:, u], False, True, ["ID3", "cf%d" % k], [bank])
        act(T.K[:, u], out, [bank], ["K0a", "K0b"] if k == 0 else ["K%d" % k], bias=-0.625)

    def masks(t, m):
        xi, xr = T["xi%d" % t], "xi%d" % t
        if m == 1:
            act(T.m1[:], T.T1[:].indirect(xi[:, 0:32]), ["T1", xr], ["m1"])
        else:
            act(T.m2[:], T.RM[:].indirect(xi[:, 32:64]), ["RM", "s" + xr], ["m2"])

    PARTS = ((0, 512, "pk"), (512, 1024, "ph"), (1024, 1536, "pU"), (1536, 1792, "pL"), (1792, 2048, "pb"))
    KC = ["K0a", "K0b", "K1", "K2", "K3", "K4"]
    IX = ["ix0", "ix1"]
    dma("s", T.ci[:], T.cnt[:], [], ["ci"])
    dma("y", T.H[:, 2048:2560], T.zin[:], [], ["H0"])
    for k, (a, b, bank) in enumerate(PARTS):
        dma("y", T.Kr[:, a:b], T.nkey[:, a:b], [], ["Kr%d" % k])
    iota(T.ip[:], [[0, 1]], 0, 1, ["ip"], flag=False)
    iota(T.ix[:, 0:16], [[1, 16]], 0, 0, ["ix0"])
    iota(T.ix[:, 16:256], [[1, 240]], 16, 0, ["ix1"])
    add("v", lambda: V.memset(T.nil[:], 0.0), [], ["nil"])
    diag(blk(T.ID, 2), DIAG[2], "ID2")
    diag(T.idf[:], 1.0, "idf")
    iota(T.ilo[:], [[0, 16], [1, 16]], 0, 0, ["ilo"])
    for k in (1, 3):
        diag(blk(T.ID, k), DIAG[k], "ID%d" % k)
    iota(T.ib[:], [[16, 8], [0, 16]], 0, 0, ["ib"])
    iota(T.ihi[:], [[1, 16], [0, 16]], 0, 0, ["ihi"])
    diag(blk(T.ID, 0), DIAG[0], "ID0")
    iota(T.iw[:], [[16, 128]], 2048, 0, ["iw"])
    iota(T.iw2[:], [[16, 32], [0, 2]], 2048, 0, ["iw2"])
    diag(blk(T.ID, 4), DIAG[4], "ID4")
    NG = 12
    trg, TRG = T.TR[:, 0:128 * NG], ["TR%d" % r for r in range(NG)]
    iota(trg, [[-8192, NG], [0, 8], [8192, 16]], -4096, 0, TRG)
    add("g", lambda: g.affine_select(trg, trg, [[-1, NG], [0, 8], [1, 16]], A.is_ge, 0.0, 0, 0), TRG, TRG)
    add("g", lambda: g.affine_select(trg, trg, [[0, NG], [-1, 128]], A.is_equal, 0.0, 0, 1), TRG, TRG)
    for k in (5, 6):
        diag(blk(T.ID, k), DIAG[k], "ID%d" % k)
    ts(T.pm[:], T.ip[:], 15, None, A.bitwise_and, None, ["ip"], ["pm"])
    cp(T.pf[:], T.ip[:], ["ip"], ["pf"])
    cp(T.pc[:], T.pm[:], ["pm"], ["pc"])
    add("v", lambda: V.memset(T.Wd[:], 0.0), [], ["Wd"])
    ts(T.RM[:], T.ix[:, 0:16], T.pc[:], None, A.is_equal, None, ["ix0", "pc"], ["RM"])
    tt(T.g16[:], T.pf[:], T.pc[:], A.subtract, ["pf", "pc"], ["g16"])
    tt(T.WC[:, 28:30], T.RM[:, 1:3], T.RM[:, 3:5], A.add, ["RM"], ["w28"])
    scaled(T.WC[:, 32:36], T.RM[:, 1:12:3], 16.0, ["RM"], ["w32"])
    add("v", lambda: V.memset(T.one[:], 1280.0), [], ["one"])
    scaled(col(14), col(28), 32.0, ["w28"], ["w14"])
    ts(T.WB[:], T.ix[:, 0:8], col(29), 32.0, A.mult, A.mult, ["ix0", "w28"], ["WB"])
    tt(T.WC[:, 36:40], T.WC[:, 32:36], T.RM[:, 0:12:3], A.add, ["w32", "RM"], ["w36"])
    weights(0, "s")
    weights(1, "s")
    for a, b, bank in PARTS:
        mm(T[bank][:] if b - a == 512 else T[bank][:, 0:b - a], blk(T.ID, 2), T.one[:, 0:b - a], True, False,
           ["ID2", "one"], [bank])
    for h in range(2):
        ts(blk(T.F2, h), T.ix[:, 0:128], T.g16[:], None, A.is_equal, None, IX + ["g16"], ["F2" + "ab"[h]])
    for b in range(2):
        ts(T.M[:, 256 * b:256 * b + 256], T.ix[:], col(14), T.WB[:, b:b + 1], A.mult, A.add, IX + ["w14", "WB"],
           ["Mp%d" % b])
    for b in (1, 2, 3):
        act(T.M[:, 512 * b:512 * b + 512], T.M[:, 0:512], ["Mp0", "Mp1", "WB"], ["Mp%d" % (b + 1)], func=F.Silu,
            bias=T.WB[:, 2 * b:2 * b + 1])
    xw(0, 0)
    xw(0, 1)
    slots(0, T.H, 2048, "H0")
    scaled(T.cm[:], T.ci[:], 32.0, ["ci"], ["cm0"])
    dma("y", T.M[0:128:16, 0:2048], T.cm[:], ["cm0"] + ["Mp%d" % b for b in range(5)], ["M"])
    cp(T.F1[:], T.F2[:, 112:256], ["F2a", "F2b"], ["F1"])
    ts(T.T0[:], T.ilo[:], T.pc[:], None, A.is_equal, None, ["ilo", "pc"], ["T0"])
    ts(T.LT[:], T.ix[:, 0:16], T.pc[:], None, A.is_lt, None, ["ix0", "pc"], ["LT"])
    weights(2, "v")
    tt(T.LT[:], T.LT[:], T.RM[:], A.subtract, ["LT", "RM"], ["LT"])
    convert(0)
    cp(T.xi0[:, 0:32], T.pz[:, 96:128], ["pz"], ["xi0"])
    cp(T.xi0[:, 32:64], T.pw[:, 96:128], ["pw"], ["sxi0"])
    ts(T.BB[:], T.ib[:], T.g16[:], None, A.is_equal, None, ["ib", "g16"], ["BB"])
    for k, c in enumerate((W0, W1, 1.0)):
        ts(blk(T.BF, k), T.ib[:], T.g16[:], c, A.is_equal, A.mult, ["ib", "g16"], ["BF%d" % k])
    ts(T.T1[:], T.ihi[:], T.pc[:], None, A.is_equal, None, ["ihi", "pc"], ["T1"])
    convert(1)
    masks(0, 1)
    dma("y", T.H[:, 0:2048], T.xreg[:], ["Kr2"], ["Hx"])
    for k, c in enumerate((-W0, -W1, 1.0)):
        ts(blk(T.CW, k), T.BB[:], wcol("key"), c, A.mult, A.mult, ["BB", "key"], ["CW%d" % k])
    cp(T.FL[:], T.ix[:, 0:64:2], IX, ["FL"])
    scaled(T.WC[:, 8:10], T.RM[:, 1:3], 32.0, ["RM"], ["w8"])
    scaled(blk(T.CW, 3), T.BB[:], wcol("last"), ["BB", "last"], ["CW3"])
    convert(2)

    def tri(e, rs):
        for r in rs:
            scaled(blk(T.TR, r), blk(T.ID, 4), T.LT[:, r:r + 1], ["ID4", "LT"], ["TR%d" % r], e)

    def setup_rest():
        ts(T.own[:], T.iw[:], T.pc[:], None, A.add, None, ["iw", "pc"], ["own"])
        for k, c in enumerate((wcol("hcol"), -8192.0)):
            scaled(wide(T.FW, k), T.F1[:], c, ["F1", "hcol"], ["FW%d" % k])
        scaled(T.WC[:, 16:18], T.ix[:, 0:2], col(9), ["ix0", "w8"], ["wb"])

    def setup_scalar(m):
        if m == 1:
            tri("s", range(NG, NG + 2))
        if m == 2:
            tri("s", range(NG + 2, 16))
        if m == 3:
            for h in range(2):
                act(T.Con[:, 256 * h:256 * h + 256], T.ix[:], IX + ["w8", "wb"], ["Con%d" % h], scale=col(8),
                    bias=col(16 + h))

    def setup_pause():
        for h in range(2):
            ts(T.NT[:, h:8:2], T.RM[:, 0:4], h - 1.0, 1.0, A.mult, A.add, ["RM"], ["NT%d" % h])
        ts(T.own2[:], T.iw2[:], T.pc[:], None, A.add, None, ["iw2", "pc"], ["own2"])
        scaled(T.Ssel[:], blk(T.ID, 0), wcol("keep"), ["ID0", "keep"], ["Ssel"])
        scaled(T.WC[:, 20:24], T.ix[:, 8:16:2], col(9), ["ix0", "w8"], ["wt"])
        scaled(wide(T.FW, 2), T.F1[:], wcol("key"), ["F1", "key"], ["FW2"])

    setup_pause()

    sent = 0
    HALF = (slice(0, 256), slice(256, 512))
    nb = 32 // NB
    AA = ["Aa%d" % c for c in range(nb)]
    for t in range(VISITS):
        last = t == VISITS - 1
        hz = slice(2048 + 512 * t, 2560 + 512 * t)
        HALL = ["Hx", "H0"] + ["H%d%s" % (k, h) for k in range(1, t + 1) for h in "ab"]
        xi, xr = T["xi%d" % t], "xi%d" % t
        y = T.pU[:, 0:32]
        if t > 0:
            add("x", None, [], [xr], kind="x", sem="ax%d" % t, n=n_in)
            add("x", None, [], ["s" + xr], kind="x", sem="as%d" % t, n=n_in)
            add("x", None, [], ["zi%d" % t], kind="x", sem="az%d" % t, n=n_in)
            zi = T["zi%d" % t]
            dma("y", T.H[16 * t:128, hz], zi[0:128 - 16 * t, :], ["zi%d" % t], ["H%da" % t])
            dma("y", T.H[0:16 * t, hz], zi[128 - 16 * t:128, :], ["zi%d" % t], ["H%db" % t])
            masks(t, 1)
            masks(t, 2)
        for m in range(3):
            if m == 0:
                src, mask, rd = T.T0[:].indirect(xi[:, 0:32]), T.K[:, 0:512], ["T0", xr, "K0a", "K0b"]
            else:
                src = T.K[:, 0:2048].indirect(T.off[:, 32 * m - 32:32 * m])
                mask, rd = T["m%d" % m][:], KC + ["off%d" % (m - 1), "m%d" % m]
            Kh, Kf, C = T["Kh%d" % m], T["Kf%d" % m], T["C%d" % m]
            tt(Kh[:], src, mask, A.mult, rd, ["Kh%d" % m])
            if t == 0 and m == 0:
                convert(3)
                convert(4)
                masks(0, 2)
            tt(Kf[:], src, mask, A.mult, rd, ["Kf%d" % m])
            pw = T.pw[:, 32 * m:32 * m + 32]
            to_w(pw, T.F1, 0, Kh, 0, 512, True, True, ["F1", "Kh%d" % m], ["pw"])
            o = T.off[:, 32 * m:32 * m + 32]
            if t == 0 and m == 0:
                setup_rest()
            cp(o, pw, ["pw"], ["off%d" % m])
            if m == 1:
                mm(y, T.idf[:], T.own[:, 32 * t:32 * t + 32], True, False, ["idf", "own"], ["pU"])
            if m > 0:
                mm(T.pY[:], blk(T.CW, m - 1), T["C%d" % (m - 1)][:], False, False, ["CW%d" % (m - 1), "C%d" % (m - 1)],
                   ["pY"])
            if m == 2:
                mm(T.pk[:], blk(T.CW, 2), T.C1[:], True, True, ["CW2", "C1"], ["pk"])
            mm(T.pY[:], blk(T.BF, m), Kf[:], m == 0, False, ["BF%d" % m, "Kf%d" % m], ["pY"])
            if m < 2:
                act(C[:], T.M[:, 0:2048].indirect(o), ["M", "off%d" % m], ["C%d" % m])
            else:
                act(C[:], T.M[:, 0:2048].indirect(o), ["M", "off2", "step"], ["C2"], bias=wcol("step"))
            if m == 0:
                act(T.nm2[:], T.m2[:], ["m2"], ["nm2"], scale=-1.0, bias=1.0)
            if m == 1 and t == 0:
                setup_scalar(1)
            if m < 2 and 0 < t < VISITS - 1:
                xw(t + 1, m)

        def old_keys(h):
            u = HALF[h]
            tt(T.Bb[:, u], T.K[:, 0:2048].indirect(T.off[:, 64 + 16 * h:80 + 16 * h]), T.nm2[:, u], A.mult,
               KC + ["off2", "nm2"], ["Bb%d" % h])

        ts(T.Wd[:, 0:64:2], T.pw[:, 64:96], ROUND, ROUND - 4096.0, A.add, A.subtract, ["pw"], ["Wd"])
        cp(T.Wb[:], T.Wd[:].indirect(T.FL[:]), ["Wd", "FL"], ["Wb"])
        act(T.Wb3[:], T.Wb[:], ["Wb"], ["Wb3"])
        old_keys(1)
        mm(T.pY[:], blk(T.CW, 3), T.C2[:], False, True, ["CW3", "C2"], ["pY"])
        to_w(T.pz[:, 0:32], T.FW, 0, T.C2, 0, 512, True, True, ["FW0", "C2"], ["pz"])
        mm(T.ph[:, 0:8], T.idf[:], T.Wd[:], True, False, ["idf", "Wd"], ["ph"])

        def compare(k):
            tt(T.E[:, 512 * k:512 * k + 512 - 128 * k], T.pY[:, :, 0:64 - 16 * k],
               T.Wb[:] if k == 0 else T.Wb3[:, :, 16 * k:64], A.is_equal, ["pY", "Wb3" if k else "Wb"], ["E%d" % k])

        def count(k):
            for r in range(16 if k == 0 else 8):
                if k == 0:
                    mm(T.ph[:, 0:8, :, 0], blk(T.TR, r), T.E[:, r:512:16], False, False, ["TR%d" % r, "E0"], ["ph"])
                else:
                    mm(T.ph[:, 0:8, k:4, :], blk(T.ID, 4), T.E[:, 512 * k + r:512 * k + 512 - 128 * k:8], False,
                       k == NB - 1 and r == 7, ["ID4", "E%d" % k], ["ph"])

        def new_keys(c, end=None):
            end = end or c + 1
            u = slice(16 * NB * c, 16 * NB * end)
            tt(T.Aa[:, u], T.pk[:, u], T.m2[:, u], A.mult, ["pk", "m2"], AA[c:end])

        def new_state():
            mm(T.pb[:], T.Ssel[:], T.C2[:], False, True, ["Ssel", "C2"], ["pb"])
            act(T.S[:], T.pb[:], ["pb", "wt"], ["S"], bias=col(20 + t))

        if t == 0:
            setup_scalar(2)
        act(T.cw[:], T.pz[:, 0:32], ["pz"], ["cw"])
        if t:
            new_state()
        compare(0)
        to_w(y, T.FW, 1, T.E, 0, 512, False, True, ["FW1", "E0"], ["pU"])
        if last:
            act(col(11), rm(0), ["RM"], ["w11"], scale=-31.0 / 32, bias=1.0)
        if t == 0:
            xw(1, 0)
            xw(1, 1)
        for k in range(NB):
            if k:
                compare(k)
            count(k)
            if k == 2:
                tt(T.zf[:], y, T.cw[:], A.max, ["pU", "cw"], ["zf"])
                ts(T.offN[:], y, 0.0, 2.0 * t, A.is_ge, A.add, ["pU"], ["offN"])
                cp(T.zoff[:], T.zf[:], ["zf"], ["zoff"])
        old_keys(0)
        new_keys(5, nb)
        zo, zr = T["zo%d" % t], "zo%d" % t
        act(zo[:], T.H[:, 0:hz.stop].indirect(T.zoff[:]), HALL + ["zoff"], [zr])
        if last:
            dma("y", T.yz[:], zo[:], [zr], [])
        else:
            slots(t + 1, zo, 0, zr)
        if t == 0:
            send(T.zi1[:], zo[:], "az1", [zr])
            setup_scalar(3)
            mm(T.pb[:], blk(T.ID, 0), T.Con[:], True, False, ["ID0", "Con0", "Con1"], ["pb"])
        act(T.NM[:], T.NT[:].indirect(T.offN[:]), ["NT0", "NT1", "offN"], ["NM"])
        if t == 0:
            new_state()
        tt(T.sm[:], T.ph[:, 0:8], T.own2[:], A.min, ["ph", "own2"], ["sm"])
        new_keys(4)
        tt(T.sf[:], T.sm[:, 0:64:2], T.sm[:, 1:64:2], A.max, ["sm"], ["sf"])
        new_keys(3)
        cp(T.soff[:], T.sf[:], ["sf"], ["soff"])
        new_keys(2)
        if not last:
            mm(T.pb[:], blk(T.ID, 0), T.Con[:], True, False, ["ID0", "Con0", "Con1"], ["pb"])
        for b, w in (("pU", 5), ("pL", 6)):
            mm(T[b][:], band(T.FW, 2, t), T.C2[:], True, False, ["FW2", "C2"], [b])
            mm(T[b][:], blk(T.ID, w), T.NM[:], False, True, ["ID%d" % w, "NM"], [b])
        todo = [0, 1]
        for c in range(nb - 1, -1, -1):
            u = slice(16 * NB * c, 16 * NB * (c + 1))
            o = T.soff[:, NB * c:NB * (c + 1)]
            tt(T.K[:].indirect(o), T.Aa[:, u], T.Bb[:, u], A.add, ["soff", AA[c], "Bb0", "Bb1"], KC)
            act(T.M[:].indirect(o), T.S[:, u], ["soff", "S"], ["M"], func=F.Silu)
            if c == nb - 1 and not last:
                xo, xn = T["xo%d" % (t + 1)], T["xi%d" % (t + 1)]
                cp(xo[:, 0:32], T.pz[:, 96:128], ["pz"], ["xo"])
                send(xn[:, 0:32], xo[:, 0:32], "ax%d" % (t + 1), ["xo"])
            elif c == nb - 3 and not last:
                cp(xo[:, 32:64], T.pw[:, 96:128], ["pw"], ["so"])
                send(xn[:, 32:64], xo[:, 32:64], "as%d" % (t + 1), ["so"])
                if t:
                    send(T["zi%d" % (t + 1)][:], zo[:], "az%d" % (t + 1), [zr])
                sent += 3 * len(topo.engines(core, nxt))
            elif todo:
                new_keys(todo.pop())
        if last:
            mm(T.pk[:], T.idf[:], T.K[:, 512:1024], True, False, ["idf", "K1"], ["pk"])
            act(T.Mb[:, 1024:2048], T.M[:, 1024:2048], ["M", "w11"], ["Mb2", "Mb3"], scale=col(11))
            for h in range(2):
                u = slice(512 * h, 512 * h + 512)
                scaled(T.Mb[:, u], T.M[:, u], col(11), ["M", "w11"], ["Mb%d" % h])
        for b, op in (("pU", A.min), ("pL", A.max)):
            for h, u in zip("ab", HALF):
                tt(T.K[:, u], T.K[:, u], T[b][:, u], op, ["K0" + h, b], ["K0" + h])
    add("g", lambda: g.dma_start(T.yc[:], T.Mb[0:128:16, :]), ["Mb%d" % h for h in range(4)], [], kind="d")
    for b in range(16):
        mm(T.pz[:, 0:128], band(T.FW, 0, b), blk(T.Mb, b), b == 0, b == 15, ["FW0", "Mb%d" % (b // 4)], ["pz"])
    mm(T.pk[:], T.idf[:], T.K[:, 1024:1536], False, False, ["idf", "K2"], ["pk"])
    mm(T.pk[:], T.idf[:], T.K[:, 1536:2048], False, True, ["idf", "K3", "K4"], ["pk"])
    cp(T.fo[:], T.pz[:, 0:128], ["pz"], ["fo"])
    HALL = ["Hx", "H0"] + ["H%d%s" % (k, h) for k in range(1, 4) for h in "ab"]

    def regs(e, a, b):
        (act if e == "s" else cp)(T.G[:, 16 * a:16 * b], T.H[:].indirect(T.fo[:, a:b]), HALL + ["fo"], ["G%d" % a])

    def gsum(a, b, bank, r):
        for j in range(16):
            mm(T[bank][:, 0:b - a], blk(T.ID, 0), T.G[:, 16 * a + j:16 * b:16], j == 0, j == 15, ["ID0"] + r, [bank])

    regs("s", 0, 72)
    regs("v", 72, 128)
    gsum(0, 128, "pU", ["G0", "G72"])
    act(T.ox[:], T.pU[:, 0:128], ["pU"], ["ox"])
    dma("s", T.yx[:], T.ox[:], ["ox"], [])
    for h, u in enumerate(HALF):
        tt(T.pL[:, u], T.pk[:, u], T.K[:, u], A.add, ["pk", "K0" + "ab"[h]] + ["pL"] * h, ["pL"] * (1 - h) + ["s%d" % h])
    for h, u in enumerate(HALF):
        ts(T.Bb[:, u], T.pL[:, u], ROUND, ROUND, A.add, A.subtract, ["s%d" % h], ["Bb%d" % h])
    for h, u in enumerate(HALF):
        tt(T.Kh0[:, u], T.pL[:, u], T.Bb[:, u], A.subtract, ["s%d" % h, "Bb%d" % h], ["Kh0"] * (1 - h) + ["f%d" % h])
    for b in range(4):
        mm(T.pw[:, 0:128], T.idf[:], blk(T.Bb, b), b == 0, False, ["idf", "Bb%d" % (b // 2)], ["pw"])
    for b in range(4):
        mm(T.pw[:, 0:128], blk(T.ID, 5), blk(T.Kh0, b), False, b == 3, ["ID5", "f%d" % (b // 2)], ["pw"])
    cp(T.ok_[:], T.pw[:, 0:128], ["pw"], ["ok_"])
    dma("y", T.yk[:], T.ok_[:], ["ok_"], [])
    emit(g, T, ops)
    g.wait_ge(T.sem.snt, sent)
